import numpy as np, ml_dtypes
CORES = [2,6,10,14,18,22,26,30]
N = 8
BF = ml_dtypes.bfloat16
B, S, D, SH = 1, 2048, 8192, 4
W, BC = N * B, 32
LAST = (2 * 255 * 255) >> SH
def middle(m):
    return 16 * (m % 16) + 8, 16 * (m // 16) + 8
def index(p, x, y):
    return ((x - int(p[0])) ** 2 + (y - int(p[1])) ** 2) >> SH
def loud(d, rng, cells):
    t = rng.integers(0, S, (N, 8)); sg = rng.choice(np.array([-15.0, 15.0]), 16); v = d["tr"].reshape(N, 8, 16, S); x, y = middle(np.array(cells))
    ld = sg - np.sign(sg) * rng.integers(0, 2, (N, 8, 16))
    for q in range(N):
        for g in range(8):
            d["tau"][q, g, index(d["pos"][q, g], x, y)] = t[q, g]; v[q, g, :, t[q, g]] = ld[q, g].astype(BF)
    return t, ld
def setup_inputs(rng):
    tr = rng.integers(-15, 16, (N, 128, S), dtype=np.int8).astype(np.float32).astype(BF)
    pos = rng.integers(0, 256, (N, 8, 2)).astype(np.int32)
    t = np.floor(np.sqrt(np.arange(D) / D) * (rng.random((N, 8, 1)) * 0.5 + 0.25) * S).astype(np.int64) + rng.integers(0, S // 4, (N, 8, D))
    return {"tr": tr, "pos": pos, "tau": t.astype(np.int32)}
def setup_inputs_ends(rng):
    d = setup_inputs(rng); c = np.array([[0, 0], [0, 255], [255, 0], [255, 255]])
    d["pos"] = np.stack([c[rng.permutation(8) % 4] for q in range(N)]).astype(np.int32)
    t = rng.integers(0, S, (N, 8, D)); t[:, :, 0] = 0; t[:, :, LAST] = S - 1; d["tau"] = t.astype(np.int32)
    e = rng.integers(0, 2, W); e[0] = 0; e[W - 1] = 1
    loud(d, rng, np.arange(W) * BC + e * (BC - 1)); return d
def setup_inputs_ties(rng):
    d = setup_inputs(rng); s = int(rng.integers(0, 3)); cells = []
    for k in range(W):
        z = (k + s) % 3; o = [0, BC - 1] if z == 0 else rng.choice(BC, 2, replace=False) if z == 1 else range(BC)
        cells += [k * BC + int(i) for i in o]
    loud(d, rng, cells); return d
def setup_inputs_close(rng):
    d = setup_inputs(rng); k = np.arange(W); lo = k * BC + rng.integers(0, BC // 2, W); hi = k * BC + BC // 2 + rng.integers(0, BC // 2, W); x, y = middle(lo)
    d["pos"][k % N, k // N, 0] = x; d["pos"][k % N, k // N, 1] = y
    t, ld = loud(d, rng, np.concatenate([lo, hi])); v = d["tr"].reshape(N, 8, 16, S); m = np.abs(np.sum(ld, axis=(0, 1)))
    for i in range(W):
        q, g = i % N, i // N; u = (int(t[q, g]) + int(rng.integers(1, S))) % S; h = ld[q, g].copy(); s = int(rng.integers(0, 16))
        if i % 2:
            z = [(m[a] - m[b], a, b) for a in range(16) for b in range(16) if m[a] > m[b] + 1 and abs(h[b]) < 15]
            if z:
                s, b = min(z)[1:]; h[b] = h[b] + np.sign(h[b])
        h[s] = h[s] - np.sign(h[s])
        d["tau"][q, g, 0] = u; v[q, g, :, u] = h.astype(BF)
    return d
def setup_inputs_steps(rng):
    d = setup_inputs(rng); d["pos"] = np.repeat(rng.integers(0, 256, (N, 1, 2)), 8, axis=1).astype(np.int32)
    d["tau"] = np.repeat(rng.integers(0, S, (N, 8, D // 64)), 64, axis=2).astype(np.int32); return d
def setup_inputs_spread(rng):
    d = setup_inputs(rng); a = rng.choice(np.array([0, 1, 4, 15], np.int8), (N, 8, 1, S))
    v = np.clip(rng.integers(-15, 16, (N, 8, 16, S), dtype=np.int8), -a, a)
    d["tr"] = v.reshape(N, 128, S).astype(np.float32).astype(BF)
    d["pos"] = np.floor(256 * rng.random((N, 8, 2)) ** 3).astype(np.int32); d["tau"] = np.floor(S * rng.random((N, 8, D)) ** 3).astype(np.int32); return d
def check_inputs(d):
    bad = []; v = np.asarray(d["tr"]).astype(np.float32)
    if not ((np.abs(v) <= 15) & (np.rint(v) == v)).all(): bad.append("samples")
    if not ((d["pos"] >= 0) & (d["pos"] <= 255)).all(): bad.append("places")
    if not ((d["tau"] >= 0) & (d["tau"] < S)).all(): bad.append("times")
    return bad
def focus(v, pos, tau, x, y):
    a = np.zeros((16, len(x)), np.int64)
    for q in range(N):
        for g in range(8): a += v[q, g][:, tau[q, g][index(pos[q, g], x, y)]]
    return a
def reference(tr, pos, tau):
    v = tr.astype(np.float32).astype(np.int32).reshape(N, 8, 16, S)
    x, y = middle(np.arange(256)); c = focus(v, pos, tau, x, y)
    e = np.sum(c * c, axis=0).reshape(W, BC)
    w = np.arange(W) * BC + np.argmax(e, axis=1)
    j = np.arange(256); x = (16 * (w % 16)[:, None] + j % 16).reshape(-1); y = (16 * (w // 16)[:, None] + j // 16).reshape(-1)
    fine = focus(v, pos, tau, x, y).reshape(16, N, B * 256).transpose(1, 0, 2)
    return {"y": np.ascontiguousarray(fine).astype(np.float32), "w": np.tile(w.reshape(1, 1, W), (N, 1, 1)).astype(np.float32)}

@@ -1,0 +1,426 @@
+from concourse.bass import DstId, RemoteDMATransfer
+from concourse.mybir import AluOpType, AxisListType, ActivationFunctionType
+
+ZC = 510
+ZL = 16 * ZC
+Z1, Z2, Z3 = 156, 246, 304
+ZG, ZV = 318, 414
+
+F32, B16, H16, I32, U16 = "float32", "bfloat16", "float16", "int32", "uint16"
+SCRATCH = {
+    "pin": ("sbuf", [128, 8, 64], I32), "pf": ("sbuf", [128, 4, 8, 16], H16),
+    "posi": ("sbuf", [8, 2], I32), "posb": ("sbuf", [8, 2], B16), "posf": ("sbuf", [8, 2], F32),
+    "feat": ("sbuf", [8, 128], B16), "gsel": ("sbuf", [8, 128], F32), "sel8": ("sbuf", [8, 128], B16),
+    "rrow": ("sbuf", [1, 128], B16), "trow": ("sbuf", [1, 128], B16), "cgt": ("sbuf", [16, 128], H16),
+    "kw": ("sbuf", [1, 8], F32), "wout": ("sbuf", [1, 8], F32), "yout": ("sbuf", [32, 128], F32),
+}
+for _nm, _w, _t in [
+        ("row", 512, I32), ("trs", 2048, B16), ("off", 512, U16), ("zed", ZL, B16), ("ints", 4, I32), ("cols", 4, F32),
+        ("cmid", 1, F32), ("cu", 144, F32), ("aj", 256, F32), ("bj", 256, F32), ("bsel", 8, H16), ("qs", 48, B16),
+        ("idh", 128, H16), ("idf", 128, F32), ("one", 128, F32), ("em0", 128, F32), ("em", 128, F32),
+        ("dfw", 32, F32), ("kcol", 128, B16), ("ccol", 1, F32), ("coef", 128, B16),
+        ("gee", 128, B16), ("kyi", 128, B16), ("kysq", 128, F32), ("lh4", 128, B16), ("lhw", 1, B16),
+        ("neg", 2, F32), ("yy", 256, F32), ("ss", 256, F32), ("rj", 256, F32), ("mask", 256, F32), ("wcol", 1, F32),
+        ("dxc", 1, F32), ("rx2", 1, F32), ("rxo", 1, F32), ("dyc", 16, F32), ("sl", 16, I32), ("ci", 16, I32),
+        ("cidx", 16, U16), ("yg", 256, H16), ("off2", 16, U16), ("cg", 256, B16), ("sendc", 32, H16),
+        ("landc", 256, H16), ("sq", 32, F32), ("mx", 1, F32), ("uu", 32, F32), ("ff", 32, F32), ("rhs", 128, B16),
+        ("lst", 128, U16), ("fg", 2048, B16), ("sendf", 256, H16), ("landf", 256, H16)]:
+    SCRATCH[_nm] = ("sbuf", [128, _w], _t)
+for _nm in ["pt", "po", "pc", "pe", "ps", "pf0", "pf1", "pm"]:
+    SCRATCH[_nm] = ("psum", [128, 512], F32)
+SEMAPHORES = ["s_pos", "s_row", "s_tau", "s_tr", "s_w", "s_y",
+              "i_p", "i_sel", "i_aj", "i_bj", "i_u", "i_k", "i_ky", "i_c", "i_rr", "i_kw", "i_e0", "i_em", "i_id",
+              "m_lw0", "m_lw1", "m_ft", "m_tr0", "m_tr1",
+              "v_int", "v_col", "v_cmid", "v_wcol", "v_sel", "v_bs", "v_qs", "v_idh", "v_km", "v_g", "v_posb",
+              "v_posf", "v_feat", "v_sl", "v_ci", "v_cidx", "v_ss0", "v_ss1", "v_pf0", "v_pf2",
+              "v_yg", "v_cgt", "v_off0", "v_off1", "v_off2", "v_cg", "v_sendc", "v_z", "v_mx", "v_u", "v_f", "v_rhs",
+              "v_l0", "v_l1", "v_e0", "v_e1", "v_w", "v_y",
+              "a_one", "a_d", "a_d1", "a_neg", "a_xx0", "a_xx1", "a_dc", "a_rx", "a_rxo", "a_t0", "a_t1", "a_m",
+              "a_ky", "a_lh4", "a_z", "a_sq",
+              "t_pos", "t_n", "t_o1", "t_off", "t_c", "t_lh4", "t_sum", "t_e", "t_s", "t_w",
+              "t_f0", "t_f1", "t_y", "l_t", "l_c", "l_f", "r_t"] + ["p%d" % _i for _i in range(8)] \
+    + ["r_c%d" % _i for _i in range(8)] + ["r_f%d" % _i for _i in range(8)]
+
+
+def rank_program(g, core, T, topo):
+    rank = T.rank_of(core)
+    if rank is None:
+        return
+    A, F = AluOpType, ActivationFunctionType
+    cores = list(T.cores)
+    n = len(cores)
+    half = n // 2
+    V, S, E, Y = g.vector, g.scalar, g.tensor, g.sync
+    Q = {"g": g, "v": V, "s": S, "t": E, "y": Y}
+    cnt, seen = {}, {}
+
+    def fin(ins, name, k=1):
+        ins.then_inc(T.sem[name], k)
+        cnt[name] = cnt.get(name, 0) + k
+
+    def need(q, *names):
+        for nm in names:
+            if seen.get((q, nm), 0) < cnt[nm]:
+                Q[q].wait_ge(T.sem[nm], cnt[nm])
+                seen[(q, nm)] = cnt[nm]
+
+    def order(r):
+        h = r // half
+        return [k for hh in (1 - h, h) for k in range(half * hh, half * hh + half)]
+
+    def bits(es):
+        return sum(1 << e for e in es)
+
+    def far(r, d):
+        a, b = topo.chip(cores[r]), topo.chip(cores[d])
+        return (3 if a == b else 2 if topo.same_plane(a, b) else 1 if topo.mates(a, b) else 0, r ^ d)
+
+    def masks(r, dests):
+        src = cores[r]
+        off = [d for d in dests if topo.chip(cores[d]) != topo.chip(src)]
+        out, taken = {}, []
+        for i, d in enumerate(off):
+            es = topo.engines(src, cores[d])
+            w = len(es) // len(off)
+            out[d] = es[i * w:i * w + w]
+            taken = es
+        for d in dests:
+            if d not in off:
+                out[d] = [e for e in topo.engines(src, cores[d]) if e not in taken][:2]
+        return out
+
+    def halves(r):
+        o = order(r)
+        return [d for d in o[:half] if d != r], [d for d in o[half:] if d != r]
+
+    def others(r):
+        return sorted([d for d in range(n) if d != r], key=lambda d: far(r, d))
+
+    def coarse_masks(r):
+        src = cores[r]
+        off = [d for d in others(r) if topo.chip(cores[d]) != topo.chip(src)]
+        on = [d for d in others(r) if d not in off]
+        oe = topo.engines(src, cores[off[0]])
+        ne = [e for e in topo.engines(src, cores[on[0]]) if e not in oe][:2] if on else []
+        return off, oe, on, ne
+
+    def dst(d):
+        rid, pid, _ = topo.addr(cores[d])
+        return DstId(rid=rid, pnc=pid)
+
+    korder = order(rank)
+    h0 = korder[0] // half
+    h1 = korder[half] // half
+    hs = [(korder[half * h], slice(64 * h, 64 * h + 64)) for h in range(2)]
+    off, oe, on, ne = coarse_masks(rank)
+
+    fin(Y.dma_start(T.posi[:], T.pos[:]), "s_pos", 16)
+    fin(S.dma_start(T.row[:], T.tau[:]), "s_row", 16)
+    for s in range(8):
+        q = Y if s < 4 else S
+        fin(q.dma_start(T.pin[:, s, :], T.tau[s:s + 1, :]), "s_tau", 16)
+    fin(Y.dma_start(T.trs[:], T.tr[:]), "s_tr", 16)
+
+    def iota(ap, pat, base, cm, name):
+        fin(g.iota(ap, pat, base, cm, allow_small_or_imprecise_dtypes=True), name)
+
+    fin(g.iota(T.ints[:, 0:1], [[1, 1]], 0, 1), "i_p")
+    iota(T.gsel[:], [[1, 8], [0, 16]], 0, -1, "i_sel")
+    iota(T.cu[:], [[1, 144]], -16, 0, "i_u")
+    iota(T.aj[:], [[0, 16], [-16, 16]], 248, 0, "i_aj")
+    iota(T.bj[:], [[32, 8], [-16, 2], [0, 16]], 24, 0, "i_bj")
+    pair = [d for d in on if d // half == rank // half]
+    both = sorted(pair[:1] + [rank])
+    if rank == both[0]:
+        iota(T.kyi[:], [[32 * half * (h1 - h0), 2], [32, half], [1, 16]], 32 * half * h0, 0, "i_ky")
+    if rank == both[-1]:
+        iota(T.kcol[:], [[h1 - h0, 2], [2, half], [0, 16]], h0, 0, "i_k")
+    if pair:
+        tab, nm = (T.kyi, "i_ky") if rank == both[0] else (T.kcol, "i_k")
+        need("g", nm)
+        g.remote_dma_fused([RemoteDMATransfer(dst_ids=[dst(pair[0])], dma_engine_mask=bits(es), remote_sem=T.sem["r_t"],
+                                              srcs=[tab[:, c:c + 64]], dsts=[tab[:, c:c + 64]])
+                            for es, c in ((oe, 0), (ne, 64))], local_sem=T.sem["l_t"])
+        cnt["l_t"] = len(oe) + len(ne)
+    cnt["r_t"] = cnt.get("l_t", 0)
+    cnt.setdefault("i_ky", 0)
+    cnt.setdefault("i_k", 0)
+    iota(T.rrow[:], [[0, 8], [1, 16]], 0, 0, "i_rr")
+
+    def ms(ap, x, name):
+        fin(V.memset(ap, x), name)
+
+    def eq(out, in0, col, name):
+        fin(V.tensor_scalar(out, in0, col, None, A.is_equal), name)
+
+    ms(T.feat[:], 1.0, "m_ft")
+    ms(T.trow[:], 0.0, "m_tr0")
+    need("v", "i_p")
+    for i, b in ((1, 15), (2, 7), (3, 112)):
+        fin(V.tensor_scalar(T.ints[:, i:i + 1], T.ints[:, 0:1], b, None, A.bitwise_and), "v_int")
+    need("v", "i_sel")
+    fin(V.tensor_scalar(T.sel8[:], T.gsel[:], 0.0, None, A.is_equal), "v_sel")
+    need("v", "v_int", "m_tr0")
+    fin(V.tensor_copy(T.cols[:], T.ints[:]), "v_col")
+    ms(T.trow[:, 32:64], 1.0, "m_tr1")
+    ms(T.lhw[:], 0.0, "m_lw0")
+    need("v", "v_col")
+    fin(V.tensor_scalar(T.cmid[:], T.cols[:, 1:2], -16.0, 248.0, A.mult, A.add), "v_cmid")
+    fin(V.tensor_scalar(T.wcol[:], T.cols[:, 1:2], -2.0, -4095.5 / 4096, A.mult, A.add), "v_wcol")
+    need("v", "i_u")
+    eq(T.bsel[:], T.cu[:, 16:144:16], T.cols[:, 3:4], "v_bs")
+    eq(T.idh[:], T.cu[:, 16:144], T.cols[:, 0:1], "v_idh")
+    eq(T.qs[:], T.cu[:, 0:48], T.cols[:, 1:2], "v_qs")
+    need("v", "m_lw0")
+    ms(T.lhw[32:64, :], 1.0 / 32, "m_lw1")
+    ms(T.lhw[96:128, :], 0.5, "m_lw1")
+
+    def table(ap, x, k, b, name):
+        fin(S.activation(ap, x, F.Copy, bias=b, scale=k), name)
+
+    need("s", "i_u")
+    table(T.one[:], T.cu[:, 0:128], 0.0, 1.0, "a_one")
+    for c in (0, 16):
+        table(T.dfw[0:32, c:c + 16], T.cu[0:32, 16:32], -2.0, 29.0, "a_d")
+    table(T.dfw[32:64, :], T.cu[32:64, 0:32], 0.0, 1.0, "a_d")
+    table(T.dfw[64:128, :], T.cu[64:128, 0:32], 0.0, 0.0, "a_d")
+    table(T.ccol[:], T.cu[:, 0:1], 0.0, 8.0, "a_d")
+    need("s", "a_d")
+    for c, p0, p1, x in ((15, 0, 32, -225.0), (15, 32, 64, -15.0), (15, 64, 128, 1.0), (31, 0, 64, 0.0)):
+        table(T.dfw[p0:p1, c:c + 1], T.cu[p0:p1, 0:1], 0.0, x, "a_d1")
+    table(T.ccol[0:32, :], T.cu[0:32, 0:1], 0.0, 64.0, "a_d1")
+    need("g", "a_one")
+    fin(g.affine_select(T.em0[:], T.one[:], [[0, 16], [-16, 8]], A.is_ge, 0.0, 0, 1), "i_e0")
+    need("g", "i_e0")
+    fin(g.affine_select(T.em[:], T.em0[:], [[0, 16], [16, 8]], A.is_ge, 0.0, 15, -1), "i_em")
+
+    need("v", "s_pos")
+    fin(V.tensor_copy(T.posb[:], T.posi[:]), "v_posb")
+    fin(V.tensor_copy(T.posf[:], T.posi[:]), "v_posf")
+    need("t", "v_sel", "v_posb")
+    fin(E.matmul(T.pm[:, 0:2], T.sel8[:], T.posb[:], True, True), "t_pos")
+    need("s", "t_pos")
+    fin(S.activation(T.neg[:], T.pm[:, 0:2], F.Copy, scale=-1.0), "a_neg")
+    need("s", "a_neg", "i_aj", "i_bj", "v_cmid", "v_col")
+    for h in range(2):
+        c = slice(128 * h, 128 * h + 128)
+        fin(S.activation(T["pf%d" % h][:, 0:128], T.aj[:, c], F.Square, bias=T.neg[:, 0:1]), "a_xx%d" % h)
+        fin(S.activation(T.yy[:, c], T.bj[:, c], F.Square, bias=T.neg[:, 1:2]), "a_xx%d" % h)
+        if h == 0:
+            fin(S.activation(T.dyc[:], T.bj[:, 0:256:16], F.Square, bias=T.neg[:, 1:2]), "a_dc")
+            fin(S.activation(T.dxc[:], T.cmid[:], F.Square, bias=T.neg[:, 0:1]), "a_dc")
+    fin(S.activation(T.rx2[:], T.cols[:, 1:2], F.Square, bias=T.neg[:, 0:1]), "a_rx")
+    for h in range(2):
+        c = slice(128 * h, 128 * h + 128)
+        need("v", "a_xx%d" % h)
+        fin(V.tensor_tensor(T.ss[:, c], T["pf%d" % h][:, 0:128], T.yy[:, c], A.add), "v_ss%d" % h)
+        if h == 0:
+            need("v", "a_dc")
+            fin(V.tensor_scalar(T.sl[:], T.dyc[:], T.dxc[:, 0:1], None, A.add), "v_sl")
+            need("v", "v_sl")
+            fin(V.tensor_scalar(T.ci[:], T.sl[:], 4, 511, A.arith_shift_right, A.bitwise_and), "v_ci")
+            need("v", "v_ci")
+            fin(V.tensor_copy(T.cidx[:], T.ci[:]), "v_cidx")
+    for h in range(2):
+        c = slice(128 * h, 128 * h + 128)
+        need("s", "v_ss%d" % h, "v_wcol")
+        fin(S.activation(T.rj[:, c], T.ss[:, c], F.Square, bias=T.wcol[:, 0:1], scale=1.0 / 4096), "a_t%d" % h)
+    for h in range(2):
+        c = slice(128 * h, 128 * h + 128)
+        need("s", "a_t%d" % h)
+        fin(S.activation(T.mask[:, c], T.rj[:, c], F.Relu, bias=1e7, scale=-1e7), "a_m")
+    need("s", "a_rx")
+    fin(S.activation(T.rxo[:], T.rx2[:], F.Copy, bias=-15.0 / 32, scale=0.0625), "a_rxo")
+
+    def turn(cb):
+        need("v", "s_tau")
+        for i in (cb, cb + 1):
+            fin(V.tensor_copy(T.pf[:, i, :, :], T.pin[:, :, 16 * i:16 * i + 16]), "v_pf%d" % cb)
+        need("t", "v_pf%d" % cb, "v_idh")
+        for i in (cb, cb + 1):
+            ins = E.matmul(T.pe[:, i::4], T.pf[:, i, :, :], T.idh[:], True, True)
+        if cb == 2:
+            fin(ins, "t_n")
+
+    turn(0)
+    turn(2)
+    need("v", "v_cidx", "a_m", "s_row")
+    fin(V.tensor_tensor(T.yg[:], T.row[:, 0:512].indirect(T.cidx[:, 0:16]), T.mask[:], A.min), "v_yg")
+    need("t", "v_yg", "v_bs")
+    for r in range(16):
+        ins = E.matmul(T.po[0:16, r:128:16], T.yg[:, r::16], T.bsel[:], True, True)
+    fin(ins, "t_o1")
+    need("v", "t_n")
+    fin(V.tensor_copy(T.off[:, 0:256], T.pe[:, 0:256]), "v_off0")
+    need("v", "t_o1")
+    fin(V.tensor_copy(T.cgt[:], T.po[0:16, 0:128]), "v_cgt")
+    need("t", "v_cgt", "v_idh")
+    fin(E.matmul(T.pt[:, 0:16], T.cgt[:], T.idh[0:16, 0:16], True, True), "t_off")
+    fin(V.tensor_copy(T.off[:, 256:512], T.pe[:, 256:512]), "v_off1")
+    need("v", "t_off")
+    fin(V.tensor_copy(T.off2[:], T.pt[:, 0:16]), "v_off2")
+    need("v", "v_off2", "s_tr")
+    fin(V.tensor_copy(T.cg[:], T.trs[:, 0:2048].indirect(T.off2[:])), "v_cg")
+    need("t", "v_qs", "v_cg")
+    for b in range(4):
+        for h in range(2):
+            c = 128 * h + 32 * b
+            ins = E.matmul(T.pc[32 * b:32 * b + 32, 0:32], T.qs[:, 16 - 16 * h:48 - 16 * h], T.cg[:, c:c + 32], h == 0, h == 1)
+    fin(ins, "t_c")
+
+    def zs(a, b):
+        need("s", "v_off0", "s_tr")
+        if b > 256:
+            need("s", "v_off1")
+        fin(S.activation(T.zed[:, 16 * a:16 * b], T.trs[:, 0:2048].indirect(T.off[:, a:b]), F.Copy), "a_z")
+
+    def zv(a, b):
+        need("v", "v_off0", "v_off1", "s_tr")
+        fin(V.tensor_copy(T.zed[:, 16 * a:16 * b], T.trs[:, 0:2048].indirect(T.off[:, a:b])), "v_z")
+
+    zv(Z3, ZG)
+    need("v", "t_c")
+    fin(V.tensor_copy(T.sendc[:], T.pc[:, 0:32]), "v_sendc")
+    need("v", "v_posf", "m_ft")
+    fin(V.tensor_scalar(T.feat[:, 32:64], T.feat[:, 0:32], T.posf[:, 0:1], -1.0, A.mult, A.mult), "v_feat")
+    fin(V.tensor_scalar(T.feat[:, 96:128], T.feat[:, 0:32], T.posf[:, 1:2], -1.0, A.mult, A.mult), "v_feat")
+    mine = slice(32 * rank, 32 * rank + 32)
+    rc = T.sem["r_c%d" % rank]
+    tr = [RemoteDMATransfer(dst_ids=[dst(d) for d in off], dma_engine_mask=bits(oe), remote_sem=rc,
+                            srcs=[T.sendc[:]], dsts=[T.landc[:, mine] for d in off])]
+    if on:
+        tr.append(RemoteDMATransfer(dst_ids=[dst(d) for d in on], dma_engine_mask=bits(ne), remote_sem=rc,
+                                    srcs=[T.sendc[:]], dsts=[T.landc[:, mine] for d in on]))
+    need("g", "v_sendc")
+    g.remote_dma_fused(tr, local_sem=T.sem["l_c"])
+    cnt["l_c"] = len(oe) + (len(ne) if on else 0)
+    for r in others(rank):
+        o, e1, o2, e2 = coarse_masks(r)
+        cnt["r_c%d" % r] = len(e1) if rank in o else len(e2)
+    iota(T.coef[:], [[32 * half * (h1 - h0), 2], [32, half], [1, 16]], 8 + 32 * half * h0, 0, "i_c")
+    fin(g.affine_select(T.idf[:], T.one[:], [[-1, 128]], A.is_equal, 0.0, 0, 1), "i_id")
+    iota(T.kw[:], [[32, 8]], 0, 0, "i_kw")
+
+    zs(0, Z1)
+    need("t", "v_feat", "m_ft", "m_tr1", "i_rr", "a_neg")
+    E.matmul(T.pm[:, 128:256], T.feat[:], T.sel8[:], True, False)
+    fin(E.matmul(T.pm[:, 128:256], T.trow[:], T.rrow[:], False, True), "t_lh4")
+    need("s", "t_lh4")
+    fin(S.activation(T.lh4[:], T.pm[:, 128:256], F.Copy), "a_lh4")
+    need("s", "i_ky", "r_t")
+    fin(S.activation(T.kysq[:], T.kyi[:], F.Square, bias=T.neg[:, 1:2]), "a_ky")
+    zs(Z1, Z2)
+    zv(ZG, ZV)
+    need("v", "i_k", "r_t", "a_d1")
+    fin(V.tensor_scalar(T.gee[:], T.kcol[:], T.cols[:, 2:3], T.ccol[:, 0:1], A.is_equal, A.mult), "v_km")
+    need("v", "v_km", "i_c")
+    fin(V.tensor_tensor(T.gee[64:96, :], T.gee[64:96, :], T.coef[64:96, :], A.mult), "v_g")
+    zv(ZV, ZC)
+
+    need("t", "v_off0", "v_off1", "v_sendc")
+    E.matmul(T.pe[:, 0:32], T.idh[:], T.sendc[:], True, False)
+    for i, r in enumerate([r for r in others(rank) if r in on] + [r for r in others(rank) if r not in on]):
+        need("t", "r_c%d" % r)
+        ins = E.matmul(T.pe[:, 0:32], T.idh[:], T.landc[:, 32 * r:32 * r + 32], False, i == n - 2)
+    fin(ins, "t_sum")
+    need("s", "t_sum")
+    fin(S.activation(T.sq[:], T.pe[:, 0:32], F.Square), "a_sq")
+    need("t", "a_sq", "i_em")
+    zs(Z2, Z3)
+    fin(E.matmul(T.pe[:, 64:96], T.em[:], T.sq[:], True, True), "t_e")
+    need("t", "i_id", "a_ky")
+    E.matmul(T.ps[:, 0:128], T.idf[:], T.kysq[:], True, False)
+    need("v", "t_e")
+    fin(V.tensor_reduce(T.mx[:], T.pe[:, 64:96], AxisListType.X, A.max), "v_mx")
+    need("v", "v_mx")
+    fin(V.tensor_scalar(T.uu[:], T.pe[:, 64:96], T.mx[:, 0:1], None, A.is_lt), "v_u")
+    need("v", "v_u", "a_d1")
+    fin(V.tensor_tensor_scan(T.ff[:], T.uu[:], T.dfw[:], 0.0, A.mult, A.add), "v_f")
+    need("v", "v_f", "v_g")
+    fin(V.tensor_scalar(T.rhs[:], T.gee[:], T.ff[:, 31:32], None, A.mult), "v_rhs")
+    need("t", "v_rhs", "a_lh4")
+    fin(E.matmul(T.ps[:, 0:128], T.lh4[:], T.rhs[:], False, True), "t_s")
+    need("t", "m_lw1")
+    for k0, c in hs:
+        fin(E.matmul(T.pm[0:1, 300 + k0:304 + k0], T.lhw[:], T.rhs[:, c.start:c.stop:16], True, True), "t_w")
+    need("v", "t_s", "a_rxo")
+    for h, (k0, c) in enumerate(hs):
+        fin(V.tensor_scalar(T.lst[:, c], T.ps[:, c], 0.0625, T.rxo[:, 0:1], A.mult, A.add), "v_l%d" % h)
+
+    need("v", "v_z", "a_z")
+    need("s", "v_z", "a_z")
+
+    def pick(q, i):
+        o = T.fg[:, 256 * i:256 * i + 256]
+        w = T.zed[:, 0:ZL].indirect(T.lst[:, 16 * i:16 * i + 16])
+        need(q, "v_l%d" % (i // half))
+        if q == "s":
+            fin(S.activation(o, w, F.Copy), "p%d" % i)
+        else:
+            fin(V.tensor_copy(o, w), "p%d" % i)
+
+    def add_up(h):
+        for i in [half * h + x for x in (2, 0, 3, 1)]:
+            need("t", "p%d" % i)
+            for u in range(2):
+                c = 32 * (i - half * h) + u
+                ins = E.matmul(T["pf%d" % h][:, c:c + 31:2], T.fg[:, 256 * i + 128 * u:256 * i + 128 * u + 128],
+                               T.qs[:, 16:32], True, True)
+        fin(ins, "t_f%d" % h)
+
+    def ready(h):
+        need("v", "t_f%d" % h)
+        fin(V.tensor_copy(T.sendf[:, 128 * h:128 * h + 128], T["pf%d" % h][:, 0:128]), "v_e%d" % h)
+
+    for i in (0, 1, 4, 5):
+        pick("s", i)
+    for i in (2, 3):
+        pick("v", i)
+    add_up(0)
+    pick("v", 6)
+    ready(0)
+    pick("v", 7)
+    add_up(1)
+    ready(1)
+
+    for h in range(2):
+        dests = sorted(halves(rank)[h], key=lambda d: far(rank, d))
+        em = masks(rank, dests)
+        need("g", "v_e%d" % h)
+        tr = []
+        for d in dests:
+            k = korder.index(d)
+            tr.append(RemoteDMATransfer(dst_ids=[dst(d)], dma_engine_mask=bits(em[d]), remote_sem=T.sem["r_f%d" % rank],
+                                        srcs=[T.sendf[:, 32 * k:32 * k + 32]], dsts=[T.landf[:, mine]]))
+            cnt["l_f"] = cnt.get("l_f", 0) + len(em[d])
+        g.remote_dma_fused(tr, local_sem=T.sem["l_f"])
+    early = [r for r in others(rank) if rank in halves(r)[0]]
+    late = [r for r in others(rank) if rank in halves(r)[1]]
+    late = [r for r in late if r in on] + [r for r in late if r not in on]
+    for h, rs in enumerate([early, late]):
+        for r in rs:
+            cnt["r_f%d" % r] = len(masks(r, halves(r)[h])[rank])
+
+    need("v", "t_w", "i_kw")
+    fin(V.tensor_tensor(T.wout[:], T.pm[0:1, 300:308], T.kw[:], A.add), "v_w")
+    need("y", "v_w")
+    fin(Y.dma_start(T.w[:], T.wout[:]), "s_w", 16)
+
+    need("t", "v_e1")
+    k = korder.index(rank)
+    E.matmul(T.pc[0:32, 0:128], T.sendf[:, 32 * k:32 * k + 32], T.idh[:], True, False)
+    for i, r in enumerate(early + late):
+        need("t", "r_f%d" % r)
+        ins = E.matmul(T.pc[0:32, 0:128], T.landf[:, 32 * r:32 * r + 32], T.idh[:], False, i == n - 2)
+    fin(ins, "t_y")
+    need("v", "t_y")
+    fin(V.tensor_copy(T.yout[:], T.pc[0:32, 0:128]), "v_y")
+    need("y", "v_y")
+    fin(Y.dma_start(T.y[:], T.yout[:]), "s_y", 16)
+    need("y", "s_w", "s_y")
+    done = {}
+    for (q, nm), k in seen.items():
+        done[nm] = max(done.get(nm, 0), k)
+    for nm in list(cnt):
+        if done.get(nm, 0) < cnt[nm]:
+            need("g", nm)

@@ -1,45 +1,48 @@
 from concourse.bass import DstId, RemoteDMATransfer
 from concourse.mybir import AluOpType, AxisListType, ActivationFunctionType
 
-ZC = 510
-ZL = 16 * ZC
-Z1, Z2, Z3 = 156, 246, 304
-ZG, ZV = 318, 414
+BIG = 1.5 * 2.0 ** 36
+MID = 1.5 * 2.0 ** 27
+ZS = (0, 256, 370)
+ZV = (370, 410, 502, 506, 512)
 
 F32, B16, H16, I32, U16 = "float32", "bfloat16", "float16", "int32", "uint16"
 SCRATCH = {
-    "pin": ("sbuf", [128, 8, 64], I32), "pf": ("sbuf", [128, 4, 8, 16], H16),
-    "posi": ("sbuf", [8, 2], I32), "posb": ("sbuf", [8, 2], B16), "posf": ("sbuf", [8, 2], F32),
-    "feat": ("sbuf", [8, 128], B16), "gsel": ("sbuf", [8, 128], F32), "sel8": ("sbuf", [8, 128], B16),
-    "rrow": ("sbuf", [1, 128], B16), "trow": ("sbuf", [1, 128], B16), "cgt": ("sbuf", [16, 128], H16),
+    "posi": ("sbuf", [16, 4], I32), "posc": ("sbuf", [16, 1], F32), "posb": ("sbuf", [8, 2], H16),
+    "posf": ("sbuf", [8, 2], F32), "feat": ("sbuf", [8, 128], H16), "sel": ("sbuf", [16, 128], H16),
+    "aa": ("sbuf", [128, 128], B16), "cc": ("sbuf", [96, 288], B16), "rall": ("sbuf", [96, 288], H16),
+    "lall": ("sbuf", [96, 128], H16), "l3b": ("sbuf", [8, 128], H16),
+    "fea2": ("sbuf", [8, 128], H16), "cgt": ("sbuf", [16, 128], H16),
     "kw": ("sbuf", [1, 8], F32), "wout": ("sbuf", [1, 8], F32), "yout": ("sbuf", [32, 128], F32),
 }
 for _nm, _w, _t in [
-        ("row", 512, I32), ("trs", 2048, B16), ("off", 512, U16), ("zed", ZL, B16), ("ints", 4, I32), ("cols", 4, F32),
-        ("cmid", 1, F32), ("cu", 144, F32), ("aj", 256, F32), ("bj", 256, F32), ("bsel", 8, H16), ("qs", 48, B16),
-        ("idh", 128, H16), ("idf", 128, F32), ("one", 128, F32), ("em0", 128, F32), ("em", 128, F32),
-        ("dfw", 32, F32), ("kcol", 128, B16), ("ccol", 1, F32), ("coef", 128, B16),
-        ("gee", 128, B16), ("kyi", 128, B16), ("kysq", 128, F32), ("lh4", 128, B16), ("lhw", 1, B16),
-        ("neg", 2, F32), ("yy", 256, F32), ("ss", 256, F32), ("rj", 256, F32), ("mask", 256, F32), ("wcol", 1, F32),
-        ("dxc", 1, F32), ("rx2", 1, F32), ("rxo", 1, F32), ("dyc", 16, F32), ("sl", 16, I32), ("ci", 16, I32),
-        ("cidx", 16, U16), ("yg", 256, H16), ("off2", 16, U16), ("cg", 256, B16), ("sendc", 32, H16),
-        ("landc", 256, H16), ("sq", 32, F32), ("mx", 1, F32), ("uu", 32, F32), ("ff", 32, F32), ("rhs", 128, B16),
-        ("lst", 128, U16), ("fg", 2048, B16), ("sendf", 256, H16), ("landf", 256, H16)]:
+        ("row", 512, I32), ("off", 512, U16), ("zed", 8192, B16), ("trs", 2048, B16), ("ints", 8, I32), ("cols", 8, F32),
+        ("cu", 144, F32), ("bsel", 8, H16), ("scol", 1, F32),
+        ("lc0", 1, F32), ("lcol", 1, F32), ("bcol", 1, F32), ("idn", 128, H16), ("neg8", 128, B16),
+        ("qs", 48, B16), ("idh", 128, H16), ("idf", 128, F32), ("one", 128, F32), ("em", 128, F32),
+        ("dfw", 32, F32), ("kcol", 128, B16), ("coef", 128, B16),
+        ("gee", 128, B16), ("kyi", 128, B16), ("kysq", 128, F32), ("ky1", 128, F32), ("ky2", 128, F32),
+        ("lh4", 128, B16), ("lhw", 1, B16), ("neg", 2, F32), ("mask", 256, F32), ("rx2", 1, F32),
+        ("sl", 16, I32), ("ci", 16, I32), ("cidx", 16, U16), ("yg", 256, H16), ("off2", 16, U16), ("cg", 256, B16),
+        ("sendc", 32, H16), ("landc", 256, H16), ("sq", 32, F32), ("mx", 1, F32), ("uu", 32, F32), ("ff", 32, F32),
+        ("rhs", 128, B16), ("wb", 128, H16), ("lst", 128, U16),
+        ("fg", 2048, B16), ("sendf", 256, H16), ("landf", 256, H16)]:
     SCRATCH[_nm] = ("sbuf", [128, _w], _t)
 for _nm in ["pt", "po", "pc", "pe", "ps", "pf0", "pf1", "pm"]:
     SCRATCH[_nm] = ("psum", [128, 512], F32)
-SEMAPHORES = ["s_pos", "s_row", "s_tau", "s_tr", "s_w", "s_y",
-              "i_p", "i_sel", "i_aj", "i_bj", "i_u", "i_k", "i_ky", "i_c", "i_rr", "i_kw", "i_e0", "i_em", "i_id",
-              "m_lw0", "m_lw1", "m_ft", "m_tr0", "m_tr1",
-              "v_int", "v_col", "v_cmid", "v_wcol", "v_sel", "v_bs", "v_qs", "v_idh", "v_km", "v_g", "v_posb",
-              "v_posf", "v_feat", "v_sl", "v_ci", "v_cidx", "v_ss0", "v_ss1", "v_pf0", "v_pf2",
-              "v_yg", "v_cgt", "v_off0", "v_off1", "v_off2", "v_cg", "v_sendc", "v_z", "v_mx", "v_u", "v_f", "v_rhs",
-              "v_l0", "v_l1", "v_e0", "v_e1", "v_w", "v_y",
-              "a_one", "a_d", "a_d1", "a_neg", "a_xx0", "a_xx1", "a_dc", "a_rx", "a_rxo", "a_t0", "a_t1", "a_m",
-              "a_ky", "a_lh4", "a_z", "a_sq",
-              "t_pos", "t_n", "t_o1", "t_off", "t_c", "t_lh4", "t_sum", "t_e", "t_s", "t_w",
-              "t_f0", "t_f1", "t_y", "l_t", "l_c", "l_f", "r_t"] + ["p%d" % _i for _i in range(8)] \
-    + ["r_c%d" % _i for _i in range(8)] + ["r_f%d" % _i for _i in range(8)]
+SEMAPHORES = ["s_pos", "s_row", "s_tr", "s_y",
+              "i_p", "i_a", "i_b", "i_l3", "i_u", "i_k", "i_ky", "i_one", "i_idf", "i_e0", "i_em",
+              "i_g0", "i_g", "i_n0", "i_idn", "i_kw",
+              "m_all", "m_lw0", "m_lw1", "m_tr0", "m_tr1",
+              "v_int", "v_col", "v_sc", "v_bc", "v_sel", "v_cc", "v_posc", "v_rall", "v_bs", "v_qs", "v_idh", "v_g",
+              "v_off", "v_sl", "v_ci", "v_cidx", "v_m", "v_k1", "v_k2", "v_z",
+              "v_yg", "v_cgt", "v_off2", "v_cg", "v_sendc", "v_mx", "v_u", "v_f", "v_rhs",
+              "v_w0", "v_w1", "v_l0", "v_l1", "v_e0", "v_e1", "v_w", "v_y",
+              "a_cg", "a_c", "a_d", "a_d1", "m_ft", "m_r", "m_l", "a_lc0", "a_lc", "a_lall", "a_neg", "a_rx", "a_ky",
+              "a_lh4", "a_sq", "a_off", "a_z", "a_e1", "a_e2", "a_pos", "a_pf", "a_feat",
+              "t_l", "t_m", "t_pos", "t_o1", "t_off", "t_c", "t_lh4", "t_sum", "t_e", "t_s0",
+              "t_s1", "t_r0", "t_r1", "t_w", "t_f0", "t_f1", "t_f2", "t_f3", "t_y", "l_c", "l_f", "l_t", "p8", "t_f4", "v_e2"] \
+    + [_a + str(_i) for _a in ("p", "r_c", "r_f") for _i in range(8)]
 
 
 def rank_program(g, core, T, topo):
@@ -86,12 +89,12 @@ def rank_program(g, core, T, topo):
             taken = es
         for d in dests:
             if d not in off:
-                out[d] = [e for e in topo.engines(src, cores[d]) if e not in taken][:2]
+                out[d] = [e for e in topo.engines(src, cores[d]) if e not in taken][:4]
         return out
 
-    def halves(r):
+    def calls(r):
         o = order(r)
-        return [d for d in o[:half] if d != r], [d for d in o[half:] if d != r]
+        return o[:2], o[2:half], [d for d in o[half:] if d != r]
 
     def others(r):
         return sorted([d for d in range(n) if d != r], key=lambda d: far(r, d))
@@ -101,7 +104,7 @@ def rank_program(g, core, T, topo):
         off = [d for d in others(r) if topo.chip(cores[d]) != topo.chip(src)]
         on = [d for d in others(r) if d not in off]
         oe = topo.engines(src, cores[off[0]])
-        ne = [e for e in topo.engines(src, cores[on[0]]) if e not in oe][:2] if on else []
+        ne = [e for e in topo.engines(src, cores[on[0]]) if e not in oe][:4] if on else []
         return off, oe, on, ne
 
     def dst(d):
@@ -114,149 +117,159 @@ def rank_program(g, core, T, topo):
     hs = [(korder[half * h], slice(64 * h, 64 * h + 64)) for h in range(2)]
     off, oe, on, ne = coarse_masks(rank)
 
-    fin(Y.dma_start(T.posi[:], T.pos[:]), "s_pos", 16)
+    fin(Y.dma_start(T.posi[0:8, 1:3], T.pos[:]), "s_pos", 16)
+    fin(S.dma_start(T.posi[8:16, 0:2], T.pos[:]), "s_pos", 16)
     fin(S.dma_start(T.row[:], T.tau[:]), "s_row", 16)
-    for s in range(8):
-        q = Y if s < 4 else S
-        fin(q.dma_start(T.pin[:, s, :], T.tau[s:s + 1, :]), "s_tau", 16)
     fin(Y.dma_start(T.trs[:], T.tr[:]), "s_tr", 16)
 
     def iota(ap, pat, base, cm, name):
         fin(g.iota(ap, pat, base, cm, allow_small_or_imprecise_dtypes=True), name)
 
-    fin(g.iota(T.ints[:, 0:1], [[1, 1]], 0, 1), "i_p")
-    iota(T.gsel[:], [[1, 8], [0, 16]], 0, -1, "i_sel")
-    iota(T.cu[:], [[1, 144]], -16, 0, "i_u")
-    iota(T.aj[:], [[0, 16], [-16, 16]], 248, 0, "i_aj")
-    iota(T.bj[:], [[32, 8], [-16, 2], [0, 16]], 24, 0, "i_bj")
-    pair = [d for d in on if d // half == rank // half]
-    both = sorted(pair[:1] + [rank])
-    if rank == both[0]:
-        iota(T.kyi[:], [[32 * half * (h1 - h0), 2], [32, half], [1, 16]], 32 * half * h0, 0, "i_ky")
-    if rank == both[-1]:
-        iota(T.kcol[:], [[h1 - h0, 2], [2, half], [0, 16]], h0, 0, "i_k")
-    if pair:
-        tab, nm = (T.kyi, "i_ky") if rank == both[0] else (T.kcol, "i_k")
-        need("g", nm)
-        g.remote_dma_fused([RemoteDMATransfer(dst_ids=[dst(pair[0])], dma_engine_mask=bits(es), remote_sem=T.sem["r_t"],
-                                              srcs=[tab[:, c:c + 64]], dsts=[tab[:, c:c + 64]])
-                            for es, c in ((oe, 0), (ne, 64))], local_sem=T.sem["l_t"])
-        cnt["l_t"] = len(oe) + len(ne)
-    cnt["r_t"] = cnt.get("l_t", 0)
-    cnt.setdefault("i_ky", 0)
-    cnt.setdefault("i_k", 0)
-    iota(T.rrow[:], [[0, 8], [1, 16]], 0, 0, "i_rr")
+    def select(out, in_, pat, op, base, cm, name):
+        fin(g.affine_select(out, in_, pat, op, 0.0, base, cm), name)
 
     def ms(ap, x, name):
         fin(V.memset(ap, x), name)
 
-    def eq(out, in0, col, name):
-        fin(V.tensor_scalar(out, in0, col, None, A.is_equal), name)
+    def eq(out, in0, col, name, k=None):
+        fin(V.tensor_scalar(out, in0, col, None, A.is_equal) if k is None else
+            V.tensor_scalar(out, in0, col, k, A.is_equal, A.mult), name)
 
-    ms(T.feat[:], 1.0, "m_ft")
-    ms(T.trow[:], 0.0, "m_tr0")
-    need("v", "i_p")
-    for i, b in ((1, 15), (2, 7), (3, 112)):
-        fin(V.tensor_scalar(T.ints[:, i:i + 1], T.ints[:, 0:1], b, None, A.bitwise_and), "v_int")
-    need("v", "i_sel")
-    fin(V.tensor_scalar(T.sel8[:], T.gsel[:], 0.0, None, A.is_equal), "v_sel")
-    need("v", "v_int", "m_tr0")
-    fin(V.tensor_copy(T.cols[:], T.ints[:]), "v_col")
-    ms(T.trow[:, 32:64], 1.0, "m_tr1")
-    ms(T.lhw[:], 0.0, "m_lw0")
-    need("v", "v_col")
-    fin(V.tensor_scalar(T.cmid[:], T.cols[:, 1:2], -16.0, 248.0, A.mult, A.add), "v_cmid")
-    fin(V.tensor_scalar(T.wcol[:], T.cols[:, 1:2], -2.0, -4095.5 / 4096, A.mult, A.add), "v_wcol")
-    need("v", "i_u")
-    eq(T.bsel[:], T.cu[:, 16:144:16], T.cols[:, 3:4], "v_bs")
-    eq(T.idh[:], T.cu[:, 16:144], T.cols[:, 0:1], "v_idh")
-    eq(T.qs[:], T.cu[:, 0:48], T.cols[:, 1:2], "v_qs")
-    need("v", "m_lw0")
-    ms(T.lhw[32:64, :], 1.0 / 32, "m_lw1")
-    ms(T.lhw[96:128, :], 0.5, "m_lw1")
+    def lin(out, in0, k, b, name):
+        fin(V.tensor_scalar(out, in0, k, b, A.mult, A.add), name)
 
     def table(ap, x, k, b, name):
         fin(S.activation(ap, x, F.Copy, bias=b, scale=k), name)
 
-    need("s", "i_u")
-    table(T.one[:], T.cu[:, 0:128], 0.0, 1.0, "a_one")
-    for c in (0, 16):
-        table(T.dfw[0:32, c:c + 16], T.cu[0:32, 16:32], -2.0, 29.0, "a_d")
-    table(T.dfw[32:64, :], T.cu[32:64, 0:32], 0.0, 1.0, "a_d")
-    table(T.dfw[64:128, :], T.cu[64:128, 0:32], 0.0, 0.0, "a_d")
-    table(T.ccol[:], T.cu[:, 0:1], 0.0, 8.0, "a_d")
-    need("s", "a_d")
-    for c, p0, p1, x in ((15, 0, 32, -225.0), (15, 32, 64, -15.0), (15, 64, 128, 1.0), (31, 0, 64, 0.0)):
-        table(T.dfw[p0:p1, c:c + 1], T.cu[p0:p1, 0:1], 0.0, x, "a_d1")
-    table(T.ccol[0:32, :], T.cu[0:32, 0:1], 0.0, 64.0, "a_d1")
-    need("g", "a_one")
-    fin(g.affine_select(T.em0[:], T.one[:], [[0, 16], [-16, 8]], A.is_ge, 0.0, 0, 1), "i_e0")
-    need("g", "i_e0")
-    fin(g.affine_select(T.em[:], T.em0[:], [[0, 16], [16, 8]], A.is_ge, 0.0, 15, -1), "i_em")
+    def square(ap, x, k, b, name):
+        fin(S.activation(ap, x, F.Square, bias=b, scale=k), name)
+
+    fin(g.iota(T.ints[:, 0:1], [[1, 1]], 0, 1), "i_p")
+    iota(T.cc[:, 0:256], [[32, 16], [0, 16]], -496, 0, "i_b")
+    iota(T.aa[:], [[0, 8], [32, 16]], -496, 0, "i_a")
+    need("g", "i_a")
+    select(T.l3b[:], T.aa[0:8, :], [[1, 8], [0, 16]], A.is_equal, 0, -1, "i_l3")
+    ms(T.rall[:], 64.5, "m_r")
+    ms(T.lall[:], 2.0, "m_l")
+    ms(T.cc[0:16, 272:288], 0.0, "v_cc")
+    need("v", "i_p")
+    for i, b in ((1, 15), (2, 7), (4, 8), (3, 112)):
+        fin(V.tensor_scalar(T.ints[:, i:i + 1], T.ints[:, 0:1], b, None, A.bitwise_and), "v_int")
+    need("v", "m_r", "m_l")
+    ms(T.lall[0:32, :], -63.5 / 16, "m_all")
+    ms(T.rall[32:64, 256:272], 0.0, "m_all")
+    need("v", "v_int")
+    lin(T.scol[:], T.ints[:, 2:3], 32.0, -496.0, "v_sc")
+    fin(V.tensor_copy(T.cols[:, 0:5], T.ints[:, 0:5]), "v_col")
+    lin(T.bcol[:], T.ints[:, 1:2], 8192.0, BIG, "v_bc")
+    ms(T.fea2[:], 0.0, "m_tr0")
+    need("v", "v_sc", "i_b")
+    eq(T.sel[:], T.cc[0:16, 0:128], T.scol[0:16, :], "v_sel")
+    need("v", "v_col")
+    fin(V.tensor_scalar(T.cc[0:16, 256:272], T.cc[0:16, 0:256:16], T.cols[0:16, 4:5], 0.125, A.mult, A.mult), "v_sel")
+    ms(T.feat[:], 1.0, "m_ft")
+    need("s", "v_int")
+    square(T.lc0[:], T.ints[:, 1:2], -4.0, 62.0, "a_lc0")
+    need("s", "a_lc0")
+    table(T.lcol[:], T.lc0[:], 1.0, 4095.75 / 16 - 15.0 / 32, "a_lc")
+    need("s", "i_b", "m_r")
+    square(T.rall[64:96, 0:256], T.cc[64:96, 0:256], 0.0625, 0.0, "a_c")
+    square(T.rall[64:96, 256:272], T.cc[64:96, 0:256:16], 0.0625, 0.0, "a_c")
+    need("s", "i_a")
+    for c in (0, 128):
+        square(T.rall[32:64, c:c + 128], T.aa[32:64, :], 0.0625, 0.0, "a_c")
+
+    iota(T.kyi[:], [[32 * half * (h1 - h0), 2], [32, half], [1, 16]], 32 * half * h0, 0, "i_ky")
+    iota(T.cu[:], [[1, 144]], -16, 0, "i_u")
+    iota(T.kcol[:], [[h0 - h1, 2], [-2, half], [0, 16]], 7 - h0, 0, "i_k")
+    low = rank < on[0]
+    full, tab, nm, got = (T.one, T.idf, "i_idf", "i_idn") if low else (T.neg8, T.idn, "i_idn", "i_idf")
+    iota(full[:], [[0, 128]], 1 if low else -8192, 0, "i_one" if low else "i_n0")
+    need("g", "i_one" if low else "i_n0")
+    select(tab[:], full[:], [[-1, 128]], A.is_equal, 0, 1, nm)
+    need("g", nm)
+    g.remote_dma_fused([RemoteDMATransfer(dst_ids=[dst(on[0])], dma_engine_mask=bits(es), remote_sem=T.sem[nm],
+                                          srcs=[tab[:, c:c + 64]], dsts=[tab[:, c:c + 64]])
+                        for es, c in ((oe, 0), (ne, 64))], local_sem=T.sem["l_t"])
+    cnt["l_t"] = cnt[got] = len(oe) + len(ne)
 
     need("v", "s_pos")
-    fin(V.tensor_copy(T.posb[:], T.posi[:]), "v_posb")
-    fin(V.tensor_copy(T.posf[:], T.posi[:]), "v_posf")
-    need("t", "v_sel", "v_posb")
-    fin(E.matmul(T.pm[:, 0:2], T.sel8[:], T.posb[:], True, True), "t_pos")
+    fin(V.tensor_copy(T.posc[:], T.posi[:, 1:2]), "v_posc")
+    need("v", "v_sel", "i_a")
+    for c in (0, 128):
+        fin(V.tensor_copy(T.cc[0:8, c:c + 128], T.aa[0:8, :]), "v_cc")
+    fin(V.tensor_copy(T.posb[:], T.posi[0:8, 1:3]), "a_pos")
+    need("v", "v_posc", "v_cc", "m_all")
+    fin(V.tensor_scalar(T.rall[0:16, :], T.cc[0:16, :], T.posc[:], None, A.add), "v_rall")
+    need("s", "v_posc", "v_sel", "m_all")
+    fin(S.activation(T.lall[0:16, :], T.sel[:], F.Copy, scale=T.posc[:]), "a_lall")
+    need("v", "m_tr0")
+    ms(T.fea2[:, 32:64], 1.0 / 32, "m_tr1")
+    ms(T.lhw[:], 0.0, "m_lw0")
+    need("t", "a_pos", "v_sel")
+    fin(E.matmul(T.pm[:, 0:2], T.sel[0:8, :], T.posb[:], True, True), "t_pos")
+    need("t", "v_rall", "a_lall", "a_c", "i_l3")
+    E.matmul(T.pt[:, 0:16], T.lall[:], T.rall[:, 256:272], True, False)
+    fin(E.matmul(T.pt[:, 0:16], T.l3b[:], T.rall[0:8, 272:288], False, True), "t_l")
+    fin(E.matmul(T.pf0[:, 0:256], T.lall[:], T.rall[:, 0:256], True, True), "t_m")
+    need("v", "t_l", "a_lc")
+    lin(T.sl[:], T.pt[:, 0:16], 0.0625, T.lcol[:], "v_sl")
+    need("v", "m_lw0")
+    ms(T.lhw[32:64, :], 1.0 / 32, "m_lw1")
+    ms(T.lhw[96:128, :], 0.5, "m_lw1")
+    need("v", "v_sl")
+    fin(V.tensor_scalar(T.ci[:], T.sl[:], 511, None, A.bitwise_and), "v_ci")
+    need("v", "t_m", "v_bc")
+    fin(V.tensor_scalar(T.mask[:], T.pf0[:, 0:256], BIG, T.bcol[:], A.add, A.is_equal), "v_m")
+    need("v", "v_ci")
+    fin(V.tensor_copy(T.cidx[:], T.ci[:]), "v_cidx")
+    need("v", "i_u")
+    eq(T.bsel[:], T.cu[:, 16:144:16], T.cols[:, 3:4], "v_bs")
+
+    table(T.posf[:], T.posi[0:8, 1:3], -1.0, 0.0, "a_pf")
     need("s", "t_pos")
-    fin(S.activation(T.neg[:], T.pm[:, 0:2], F.Copy, scale=-1.0), "a_neg")
-    need("s", "a_neg", "i_aj", "i_bj", "v_cmid", "v_col")
-    for h in range(2):
-        c = slice(128 * h, 128 * h + 128)
-        fin(S.activation(T["pf%d" % h][:, 0:128], T.aj[:, c], F.Square, bias=T.neg[:, 0:1]), "a_xx%d" % h)
-        fin(S.activation(T.yy[:, c], T.bj[:, c], F.Square, bias=T.neg[:, 1:2]), "a_xx%d" % h)
-        if h == 0:
-            fin(S.activation(T.dyc[:], T.bj[:, 0:256:16], F.Square, bias=T.neg[:, 1:2]), "a_dc")
-            fin(S.activation(T.dxc[:], T.cmid[:], F.Square, bias=T.neg[:, 0:1]), "a_dc")
-    fin(S.activation(T.rx2[:], T.cols[:, 1:2], F.Square, bias=T.neg[:, 0:1]), "a_rx")
-    for h in range(2):
-        c = slice(128 * h, 128 * h + 128)
-        need("v", "a_xx%d" % h)
-        fin(V.tensor_tensor(T.ss[:, c], T["pf%d" % h][:, 0:128], T.yy[:, c], A.add), "v_ss%d" % h)
-        if h == 0:
-            need("v", "a_dc")
-            fin(V.tensor_scalar(T.sl[:], T.dyc[:], T.dxc[:, 0:1], None, A.add), "v_sl")
-            need("v", "v_sl")
-            fin(V.tensor_scalar(T.ci[:], T.sl[:], 4, 511, A.arith_shift_right, A.bitwise_and), "v_ci")
-            need("v", "v_ci")
-            fin(V.tensor_copy(T.cidx[:], T.ci[:]), "v_cidx")
-    for h in range(2):
-        c = slice(128 * h, 128 * h + 128)
-        need("s", "v_ss%d" % h, "v_wcol")
-        fin(S.activation(T.rj[:, c], T.ss[:, c], F.Square, bias=T.wcol[:, 0:1], scale=1.0 / 4096), "a_t%d" % h)
-    for h in range(2):
-        c = slice(128 * h, 128 * h + 128)
-        need("s", "a_t%d" % h)
-        fin(S.activation(T.mask[:, c], T.rj[:, c], F.Relu, bias=1e7, scale=-1e7), "a_m")
-    need("s", "a_rx")
-    fin(S.activation(T.rxo[:], T.rx2[:], F.Copy, bias=-15.0 / 32, scale=0.0625), "a_rxo")
+    table(T.neg[:], T.pm[:, 0:2], -1.0, 0.0, "a_neg")
+    for p0, p1, k, b in ((0, 32, -0.5, -16.0), (32, 64, 0.0, 1.0), (64, 128, 0.0, 0.0)):
+        table(T.dfw[p0:p1, :], T.aa[p0:p1, 0:32], k, b, "a_d")
+    need("s", "a_pf", "m_ft")
+    fin(S.activation(T.feat[:, 32:64], T.feat[:, 0:32], F.Copy, bias=15.5, scale=T.posf[:, 0:1]), "a_feat")
+    fin(S.activation(T.feat[:, 96:128], T.feat[:, 0:32], F.Copy, scale=T.posf[:, 1:2]), "a_feat")
+    need("s", "s_row")
+    table(T.off[:, 0:256], T.row[:, 0:256], 1.0, 0.0, "a_off")
+    need("t", "a_feat", "m_tr1", "a_neg")
+    E.matmul(T.pm[:, 128:256], T.feat[:], T.sel[0:8, :], True, False)
+    fin(E.matmul(T.pm[:, 128:256], T.fea2[:], T.l3b[:], False, True), "t_lh4")
+    need("s", "a_neg", "v_col", "i_ky", "a_d")
+    square(T.rx2[:], T.cols[:, 1:2], 1.0, T.neg[:, 0:1], "a_rx")
+    square(T.kysq[:], T.kyi[:], 1.0, T.neg[:, 1:2], "a_ky")
+    for c, p0, p1, x in ((15, 0, 32, -1800.0), (15, 32, 64, -15.0), (15, 64, 128, 1.0), (31, 0, 64, 0.0)):
+        table(T.dfw[p0:p1, c:c + 1], T.aa[p0:p1, 0:1], 0.0, x, "a_d1")
+    need("s", "t_lh4")
+    table(T.lh4[:], T.pm[:, 128:256], 1.0, 0.0, "a_lh4")
 
-    def turn(cb):
-        need("v", "s_tau")
-        for i in (cb, cb + 1):
-            fin(V.tensor_copy(T.pf[:, i, :, :], T.pin[:, :, 16 * i:16 * i + 16]), "v_pf%d" % cb)
-        need("t", "v_pf%d" % cb, "v_idh")
-        for i in (cb, cb + 1):
-            ins = E.matmul(T.pe[:, i::4], T.pf[:, i, :, :], T.idh[:], True, True)
-        if cb == 2:
-            fin(ins, "t_n")
+    def zs(a, b):
+        need("s", "a_off", "s_tr", *(["v_off"] if b > 256 else []))
+        fin(S.activation(T.zed[:, 16 * a:16 * b], T.trs[:, 0:2048].indirect(T.off[:, a:b]), F.Copy), "a_z")
 
-    turn(0)
-    turn(2)
-    need("v", "v_cidx", "a_m", "s_row")
-    fin(V.tensor_tensor(T.yg[:], T.row[:, 0:512].indirect(T.cidx[:, 0:16]), T.mask[:], A.min), "v_yg")
+    def zv(a, b):
+        need("v", "v_off", "s_tr")
+        fin(V.tensor_copy(T.zed[:, 16 * a:16 * b], T.trs[:, 0:2048].indirect(T.off[:, a:b])), "v_z")
+
+    zs(ZS[0], ZS[1])
+
+    need("v", "v_cidx", "v_m", "s_row")
+    fin(V.tensor_tensor(T.yg[:], T.row[:, 0:512].indirect(T.cidx[:, 0:16]), T.mask[:], A.mult), "v_yg")
+    eq(T.idh[:], T.cu[:, 16:144], T.cols[:, 0:1], "v_idh")
+    eq(T.qs[:], T.cu[:, 0:48], T.cols[:, 1:2], "v_qs")
     need("t", "v_yg", "v_bs")
     for r in range(16):
         ins = E.matmul(T.po[0:16, r:128:16], T.yg[:, r::16], T.bsel[:], True, True)
     fin(ins, "t_o1")
-    need("v", "t_n")
-    fin(V.tensor_copy(T.off[:, 0:256], T.pe[:, 0:256]), "v_off0")
     need("v", "t_o1")
     fin(V.tensor_copy(T.cgt[:], T.po[0:16, 0:128]), "v_cgt")
     need("t", "v_cgt", "v_idh")
     fin(E.matmul(T.pt[:, 0:16], T.cgt[:], T.idh[0:16, 0:16], True, True), "t_off")
-    fin(V.tensor_copy(T.off[:, 256:512], T.pe[:, 256:512]), "v_off1")
+    fin(V.tensor_copy(T.off[:, 256:384], T.row[:, 256:384]), "v_off")
     need("v", "t_off")
     fin(V.tensor_copy(T.off2[:], T.pt[:, 0:16]), "v_off2")
     need("v", "v_off2", "s_tr")
@@ -267,23 +280,14 @@ def rank_program(g, core, T, topo):
             c = 128 * h + 32 * b
             ins = E.matmul(T.pc[32 * b:32 * b + 32, 0:32], T.qs[:, 16 - 16 * h:48 - 16 * h], T.cg[:, c:c + 32], h == 0, h == 1)
     fin(ins, "t_c")
-
-    def zs(a, b):
-        need("s", "v_off0", "s_tr")
-        if b > 256:
-            need("s", "v_off1")
-        fin(S.activation(T.zed[:, 16 * a:16 * b], T.trs[:, 0:2048].indirect(T.off[:, a:b]), F.Copy), "a_z")
-
-    def zv(a, b):
-        need("v", "v_off0", "v_off1", "s_tr")
-        fin(V.tensor_copy(T.zed[:, 16 * a:16 * b], T.trs[:, 0:2048].indirect(T.off[:, a:b])), "v_z")
-
-    zv(Z3, ZG)
+    fin(V.tensor_copy(T.off[:, 384:512], T.row[:, 384:512]), "v_off")
+    need("v", "a_ky", "a_rx", "i_k")
+    fin(V.tensor_scalar(T.ky1[:], T.kysq[:], T.rx2[:, 0:1], -7.5, A.add, A.add), "v_k1")
+    eq(T.gee[0:64, :], T.kcol[0:64, :], T.cols[0:64, 2:3], "v_g", 8.0)
+    eq(T.gee[96:128, :], T.kcol[96:128, :], T.cols[96:128, 2:3], "v_g", 8.0)
     need("v", "t_c")
     fin(V.tensor_copy(T.sendc[:], T.pc[:, 0:32]), "v_sendc")
-    need("v", "v_posf", "m_ft")
-    fin(V.tensor_scalar(T.feat[:, 32:64], T.feat[:, 0:32], T.posf[:, 0:1], -1.0, A.mult, A.mult), "v_feat")
-    fin(V.tensor_scalar(T.feat[:, 96:128], T.feat[:, 0:32], T.posf[:, 1:2], -1.0, A.mult, A.mult), "v_feat")
+
     mine = slice(32 * rank, 32 * rank + 32)
     rc = T.sem["r_c%d" % rank]
     tr = [RemoteDMATransfer(dst_ids=[dst(d) for d in off], dma_engine_mask=bits(oe), remote_sem=rc,
@@ -297,27 +301,26 @@ def rank_program(g, core, T, topo):
     for r in others(rank):
         o, e1, o2, e2 = coarse_masks(r)
         cnt["r_c%d" % r] = len(e1) if rank in o else len(e2)
-    iota(T.coef[:], [[32 * half * (h1 - h0), 2], [32, half], [1, 16]], 8 + 32 * half * h0, 0, "i_c")
-    fin(g.affine_select(T.idf[:], T.one[:], [[-1, 128]], A.is_equal, 0.0, 0, 1), "i_id")
+
+    if not low:
+        iota(T.one[:], [[0, 128]], 1, 0, "i_one")
+        need("g", "i_one")
+    select(T.em[:], T.one[:], [[0, 16], [-16, 8]], A.is_ge, 0, 1, "i_e0")
+    iota(T.coef[:], [[1024 * half * (h1 - h0), 2], [1024, half], [32, 16]], 256 + 1024 * half * h0, 0, "i_g0")
+    need("g", "i_e0")
+    select(T.em[:], T.em[:], [[0, 16], [16, 8]], A.is_ge, 15, -1, "i_em")
     iota(T.kw[:], [[32, 8]], 0, 0, "i_kw")
+    need("g", "i_kw", "i_g0")
+    select(T.gee[64:96, :], T.coef[64:96, :], [[h0 - h1, 2], [-2, half], [0, 16]], A.is_equal, 7 - h0, -1, "i_g")
+    need("v", "v_k1")
+    fin(V.tensor_scalar(T.ky2[:], T.ky1[:], MID, MID, A.add, A.subtract), "v_k2")
+    zv(ZV[0], ZV[2])
 
-    zs(0, Z1)
-    need("t", "v_feat", "m_ft", "m_tr1", "i_rr", "a_neg")
-    E.matmul(T.pm[:, 128:256], T.feat[:], T.sel8[:], True, False)
-    fin(E.matmul(T.pm[:, 128:256], T.trow[:], T.rrow[:], False, True), "t_lh4")
-    need("s", "t_lh4")
-    fin(S.activation(T.lh4[:], T.pm[:, 128:256], F.Copy), "a_lh4")
-    need("s", "i_ky", "r_t")
-    fin(S.activation(T.kysq[:], T.kyi[:], F.Square, bias=T.neg[:, 1:2]), "a_ky")
-    zs(Z1, Z2)
-    zv(ZG, ZV)
-    need("v", "i_k", "r_t", "a_d1")
-    fin(V.tensor_scalar(T.gee[:], T.kcol[:], T.cols[:, 2:3], T.ccol[:, 0:1], A.is_equal, A.mult), "v_km")
-    need("v", "v_km", "i_c")
-    fin(V.tensor_tensor(T.gee[64:96, :], T.gee[64:96, :], T.coef[64:96, :], A.mult), "v_g")
-    zv(ZV, ZC)
-
-    need("t", "v_off0", "v_off1", "v_sendc")
+    pa, pb = [T.ps, T.pc], [T.po, T.pt]
+    need("t", "i_idf", "v_k2", "v_sendc")
+    for b in (pa, pb):
+        for h, (k0, c) in enumerate(hs):
+            E.matmul(b[h][:, 0:64], T.idf[:], T.ky2[:, c], True, False)
     E.matmul(T.pe[:, 0:32], T.idh[:], T.sendc[:], True, False)
     for i, r in enumerate([r for r in others(rank) if r in on] + [r for r in others(rank) if r not in on]):
         need("t", "r_c%d" % r)
@@ -325,91 +328,117 @@ def rank_program(g, core, T, topo):
     fin(ins, "t_sum")
     need("s", "t_sum")
     fin(S.activation(T.sq[:], T.pe[:, 0:32], F.Square), "a_sq")
+    zs(ZS[1], ZS[2])
     need("t", "a_sq", "i_em")
-    zs(Z2, Z3)
     fin(E.matmul(T.pe[:, 64:96], T.em[:], T.sq[:], True, True), "t_e")
-    need("t", "i_id", "a_ky")
-    E.matmul(T.ps[:, 0:128], T.idf[:], T.kysq[:], True, False)
     need("v", "t_e")
     fin(V.tensor_reduce(T.mx[:], T.pe[:, 64:96], AxisListType.X, A.max), "v_mx")
     need("v", "v_mx")
     fin(V.tensor_scalar(T.uu[:], T.pe[:, 64:96], T.mx[:, 0:1], None, A.is_lt), "v_u")
     need("v", "v_u", "a_d1")
     fin(V.tensor_tensor_scan(T.ff[:], T.uu[:], T.dfw[:], 0.0, A.mult, A.add), "v_f")
-    need("v", "v_f", "v_g")
+    need("v", "v_f", "v_g", "i_g")
     fin(V.tensor_scalar(T.rhs[:], T.gee[:], T.ff[:, 31:32], None, A.mult), "v_rhs")
-    need("t", "v_rhs", "a_lh4")
-    fin(E.matmul(T.ps[:, 0:128], T.lh4[:], T.rhs[:], False, True), "t_s")
+    zv(ZV[2], ZV[3])
+    need("t", "v_rhs", "a_lh4", "i_idn")
+    for h, (k0, c) in enumerate(hs):
+        fin(E.matmul(pa[h][:, 0:64], T.lh4[:], T.rhs[:, c], False, True), "t_s%d" % h)
+    for h, (k0, c) in enumerate(hs):
+        need("v", "t_s%d" % h)
+        lin(T.wb[:, c], pa[h][:, 0:64], 1.0 / 8192, 1100 - 4088.0 / 8192, "v_w%d" % h)
+    zv(ZV[3], ZV[4])
+    for h, (k0, c) in enumerate(hs):
+        E.matmul(pb[h][:, 0:64], T.lh4[:], T.rhs[:, c], False, False)
+        need("t", "v_w%d" % h)
+        E.matmul(pb[h][:, 0:64], T.idn[:], T.wb[:, c], False, False)
+        fin(E.matmul(pb[h][:, 0:64], T.idh[:], T.wb[:, c], False, True), "t_r%d" % h)
     need("t", "m_lw1")
     for k0, c in hs:
         fin(E.matmul(T.pm[0:1, 300 + k0:304 + k0], T.lhw[:], T.rhs[:, c.start:c.stop:16], True, True), "t_w")
-    need("v", "t_s", "a_rxo")
-    for h, (k0, c) in enumerate(hs):
-        fin(V.tensor_scalar(T.lst[:, c], T.ps[:, c], 0.0625, T.rxo[:, 0:1], A.mult, A.add), "v_l%d" % h)
 
-    need("v", "v_z", "a_z")
-    need("s", "v_z", "a_z")
+    def places(h):
+        need("v", "t_r%d" % h)
+        fin(V.tensor_scalar(T.lst[:, hs[h][1]], pb[h][:, 0:64], 8191.0 * 1100, None, A.add), "v_l%d" % h)
 
-    def pick(q, i):
-        o = T.fg[:, 256 * i:256 * i + 256]
-        w = T.zed[:, 0:ZL].indirect(T.lst[:, 16 * i:16 * i + 16])
-        need(q, "v_l%d" % (i // half))
-        if q == "s":
-            fin(S.activation(o, w, F.Copy), "p%d" % i)
-        else:
-            fin(V.tensor_copy(o, w), "p%d" % i)
+    def pick(q, d, a=0, b=16, name=None):
+        i = korder.index(d)
+        o = T.fg[:, 256 * i + 16 * a:256 * i + 16 * b]
+        w = T.zed[:].indirect(T.lst[:, 16 * i + a:16 * i + b])
+        need(q, "v_l%d" % (i // half), "v_z", "a_z")
+        fin(S.activation(o, w, F.Copy) if q == "s" else V.tensor_copy(o, w), name or "p%d" % i)
 
-    def add_up(h):
-        for i in [half * h + x for x in (2, 0, 3, 1)]:
-            need("t", "p%d" % i)
-            for u in range(2):
-                c = 32 * (i - half * h) + u
-                ins = E.matmul(T["pf%d" % h][:, c:c + 31:2], T.fg[:, 256 * i + 128 * u:256 * i + 128 * u + 128],
-                               T.qs[:, 16:32], True, True)
-        fin(ins, "t_f%d" % h)
+    first = korder[:half]
+    far1 = [d for d in korder[half:] if d in off]
+    mate = on[0]
+    home = {d: ((T.pf0, T.po)[i // 2], 32 * (i % 2), i) for i, d in enumerate(first)}
+    home.update({d: (T.pf1, 32 * i, half + i) for i, d in enumerate(far1)})
+    home.update({mate: (T.pe, 0, n - 2), rank: (T.ps, 0, n - 1)})
 
-    def ready(h):
-        need("v", "t_f%d" % h)
-        fin(V.tensor_copy(T.sendf[:, 128 * h:128 * h + 128], T["pf%d" % h][:, 0:128]), "v_e%d" % h)
+    def add_up(d, name=None, more=()):
+        i = korder.index(d)
+        b, c, _ = home[d]
+        for u in range(2):
+            need("t", *(["p%d" % i] + list(more[:u])))
+            ins = E.matmul(b[:, c + u:c + u + 31:2], T.fg[:, 256 * i + 128 * u:256 * i + 128 * u + 128], T.qs[:, 16:32], True, True)
+        if name:
+            fin(ins, name)
 
-    for i in (0, 1, 4, 5):
-        pick("s", i)
-    for i in (2, 3):
-        pick("v", i)
-    add_up(0)
-    pick("v", 6)
-    ready(0)
-    pick("v", 7)
-    add_up(1)
-    ready(1)
+    places(0)
+    pick("v", first[0])
+    places(1)
+    pick("s", first[1])
+    pick("v", first[2])
+    pick("s", first[3])
+    add_up(first[0])
+    add_up(first[1], "t_f0")
+    need("v", "t_f0")
+    fin(V.tensor_copy(T.sendf[:, 0:64], T.pf0[:, 0:64]), "v_e0")
+    pick("v", far1[0])
+    pick("s", far1[1])
+    add_up(first[2])
+    add_up(first[3], "t_f4")
+    need("s", "t_f4")
+    table(T.sendf[:, 64:128], T.po[:, 0:64], 1.0, 0.0, "v_e2")
+    pick("v", mate, 0, 8)
+    pick("s", mate, 8, 16, "p8")
+    need("t", "v_u", "v_w0")
+    add_up(far1[0])
+    add_up(far1[1], "t_f1")
+    add_up(mate, "t_f2", ("p8",))
+    need("v", "t_f1")
+    fin(V.tensor_copy(T.sendf[:, 128:192], T.pf1[:, 0:64]), "v_e1")
+    need("s", "t_f2")
+    table(T.sendf[:, 192:224], T.pe[:, 0:32], 1.0, 0.0, "a_e1")
+    pick("s", rank)
+    add_up(rank, "t_f3")
+    need("s", "t_f3")
+    table(T.sendf[:, 224:256], T.ps[:, 0:32], 1.0, 0.0, "a_e2")
 
-    for h in range(2):
-        dests = sorted(halves(rank)[h], key=lambda d: far(rank, d))
+    for h, dests in enumerate(calls(rank)):
         em = masks(rank, dests)
-        need("g", "v_e%d" % h)
+        need("g", *(("v_e0",), ("v_e2",), ("v_e1", "a_e1"))[h])
         tr = []
         for d in dests:
-            k = korder.index(d)
+            k = home[d][2]
             tr.append(RemoteDMATransfer(dst_ids=[dst(d)], dma_engine_mask=bits(em[d]), remote_sem=T.sem["r_f%d" % rank],
                                         srcs=[T.sendf[:, 32 * k:32 * k + 32]], dsts=[T.landf[:, mine]]))
             cnt["l_f"] = cnt.get("l_f", 0) + len(em[d])
         g.remote_dma_fused(tr, local_sem=T.sem["l_f"])
-    early = [r for r in others(rank) if rank in halves(r)[0]]
-    late = [r for r in others(rank) if rank in halves(r)[1]]
-    late = [r for r in late if r in on] + [r for r in late if r not in on]
-    for h, rs in enumerate([early, late]):
+    coming = []
+    for h in range(3):
+        rs = [r for r in others(rank) if rank in calls(r)[h]]
+        coming += [r for r in rs if r in on] + [r for r in rs if r not in on]
         for r in rs:
-            cnt["r_f%d" % r] = len(masks(r, halves(r)[h])[rank])
+            cnt["r_f%d" % r] = len(masks(r, calls(r)[h])[rank])
 
     need("v", "t_w", "i_kw")
     fin(V.tensor_tensor(T.wout[:], T.pm[0:1, 300:308], T.kw[:], A.add), "v_w")
     need("y", "v_w")
-    fin(Y.dma_start(T.w[:], T.wout[:]), "s_w", 16)
+    fin(Y.dma_start(T.w[:], T.wout[:]), "s_y", 16)
 
-    need("t", "v_e1")
-    k = korder.index(rank)
-    E.matmul(T.pc[0:32, 0:128], T.sendf[:, 32 * k:32 * k + 32], T.idh[:], True, False)
-    for i, r in enumerate(early + late):
+    need("t", "a_e2", "v_w1")
+    E.matmul(T.pc[0:32, 0:128], T.sendf[:, 224:256], T.idh[:], True, False)
+    for i, r in enumerate(coming):
         need("t", "r_f%d" % r)
         ins = E.matmul(T.pc[0:32, 0:128], T.landf[:, 32 * r:32 * r + 32], T.idh[:], False, i == n - 2)
     fin(ins, "t_y")
@@ -417,7 +446,7 @@ def rank_program(g, core, T, topo):
     fin(V.tensor_copy(T.yout[:], T.pc[0:32, 0:128]), "v_y")
     need("y", "v_y")
     fin(Y.dma_start(T.y[:], T.yout[:]), "s_y", 16)
-    need("y", "s_w", "s_y")
+    need("y", "s_y")
     done = {}
     for (q, nm), k in seen.items():
         done[nm] = max(done.get(nm, 0), k)

@@ -3,8 +3,8 @@ from concourse.mybir import AluOpType, AxisListType, ActivationFunctionType
 
 BIG = 1.5 * 2.0 ** 36
 MID = 1.5 * 2.0 ** 27
-ZS = (0, 256, 370)
-ZV = (370, 410, 502, 506, 512)
+ZS = (0, 54, 220, 306)
+ONE, TWO = 8, 16
 
 F32, B16, H16, I32, U16 = "float32", "bfloat16", "float16", "int32", "uint16"
 SCRATCH = {
@@ -17,7 +17,7 @@ SCRATCH = {
 }
 for _nm, _w, _t in [
         ("row", 512, I32), ("off", 512, U16), ("zed", 8192, B16), ("trs", 2048, B16), ("ints", 8, I32), ("cols", 8, F32),
-        ("cu", 144, F32), ("bsel", 8, H16), ("scol", 1, F32),
+        ("cu", 144, F32), ("st", 143, H16), ("scol", 2, F32),
         ("lc0", 1, F32), ("lcol", 1, F32), ("bcol", 1, F32), ("idn", 128, H16), ("neg8", 128, B16),
         ("qs", 48, B16), ("idh", 128, H16), ("idf", 128, F32), ("one", 128, F32), ("em", 128, F32),
         ("dfw", 32, F32), ("kcol", 128, B16), ("coef", 128, B16),
@@ -34,9 +34,9 @@ SEMAPHORES = ["s_pos", "s_row", "s_tr", "s_y",
               "i_p", "i_a", "i_b", "i_l3", "i_u", "i_k", "i_ky", "i_one", "i_idf", "i_e0", "i_em",
               "i_g0", "i_g", "i_n0", "i_idn", "i_kw",
               "m_all", "m_lw0", "m_lw1", "m_tr0", "m_tr1",
-              "v_int", "v_col", "v_sc", "v_bc", "v_sel", "v_cc", "v_posc", "v_rall", "v_bs", "v_qs", "v_idh", "v_g",
+              "v_int", "v_in0", "v_cg1", "t_y1", "a_y", "v_col", "v_sc", "v_bc", "v_sel", "v_cc", "v_posc", "v_rall", "v_bs", "v_qs", "v_idh", "v_g",
               "v_off", "v_sl", "v_ci", "v_cidx", "v_m", "v_k1", "v_k2", "v_z",
-              "v_yg", "v_cgt", "v_off2", "v_cg", "v_sendc", "v_mx", "v_u", "v_f", "v_rhs",
+              "v_yg0", "v_yg1", "v_off2", "v_cg", "v_sendc", "v_mx", "v_u", "v_f", "v_rhs",
               "v_w0", "v_w1", "v_l0", "v_l1", "v_e0", "v_e1", "v_w", "v_y",
               "a_cg", "a_c", "a_d", "a_d1", "m_ft", "m_r", "m_l", "a_lc0", "a_lc", "a_lall", "a_neg", "a_rx", "a_ky",
               "a_lh4", "a_sq", "a_off", "a_z", "a_e1", "a_e2", "a_pos", "a_pf", "a_feat",
@@ -94,7 +94,8 @@ def rank_program(g, core, T, topo):
 
     def calls(r):
         o = order(r)
-        return o[:2], o[2:half], [d for d in o[half:] if d != r]
+        a = sorted(o[:half], key=lambda d: far(r, d))
+        return a[:2], a[2:], [d for d in o[half:] if d != r]
 
     def others(r):
         return sorted([d for d in range(n) if d != r], key=lambda d: far(r, d))
@@ -117,8 +118,8 @@ def rank_program(g, core, T, topo):
     hs = [(korder[half * h], slice(64 * h, 64 * h + 64)) for h in range(2)]
     off, oe, on, ne = coarse_masks(rank)
 
-    fin(Y.dma_start(T.posi[0:8, 1:3], T.pos[:]), "s_pos", 16)
-    fin(S.dma_start(T.posi[8:16, 0:2], T.pos[:]), "s_pos", 16)
+    fin(Y.dma_start(T.posi[0:8, 0:2], T.pos[:]), "s_pos", 16)
+    fin(S.dma_start(T.posi[8:16, 1:3], T.pos[:]), "s_pos", 16)
     fin(S.dma_start(T.row[:], T.tau[:]), "s_row", 16)
     fin(Y.dma_start(T.trs[:], T.tr[:]), "s_tr", 16)
 
@@ -153,28 +154,29 @@ def rank_program(g, core, T, topo):
     ms(T.lall[:], 2.0, "m_l")
     ms(T.cc[0:16, 272:288], 0.0, "v_cc")
     need("v", "i_p")
-    for i, b in ((1, 15), (2, 7), (4, 8), (3, 112)):
-        fin(V.tensor_scalar(T.ints[:, i:i + 1], T.ints[:, 0:1], b, None, A.bitwise_and), "v_int")
+    for i, b, nm in ((2, 7, "v_in0"), (4, 8, "v_in0"), (1, 15, "v_int"), (3, 112, "v_int")):
+        fin(V.tensor_scalar(T.ints[:, i:i + 1], T.ints[:, 0:1], b, None, A.bitwise_and), nm)
     need("v", "m_r", "m_l")
     ms(T.lall[0:32, :], -63.5 / 16, "m_all")
     ms(T.rall[32:64, 256:272], 0.0, "m_all")
+    need("v", "v_in0")
+    lin(T.scol[:, 0:1], T.ints[:, 2:3], 32.0, -496.0, "v_sc")
+    lin(T.scol[:, 1:2], T.ints[:, 4:5], 0.125, 0.0, "v_cg1")
     need("v", "v_int")
-    lin(T.scol[:], T.ints[:, 2:3], 32.0, -496.0, "v_sc")
-    fin(V.tensor_copy(T.cols[:, 0:5], T.ints[:, 0:5]), "v_col")
+    fin(V.tensor_copy(T.cols[:, 0:4], T.ints[:, 0:4]), "v_col")
     lin(T.bcol[:], T.ints[:, 1:2], 8192.0, BIG, "v_bc")
     ms(T.fea2[:], 0.0, "m_tr0")
     need("v", "v_sc", "i_b")
-    eq(T.sel[:], T.cc[0:16, 0:128], T.scol[0:16, :], "v_sel")
-    need("v", "v_col")
-    fin(V.tensor_scalar(T.cc[0:16, 256:272], T.cc[0:16, 0:256:16], T.cols[0:16, 4:5], 0.125, A.mult, A.mult), "v_sel")
-    ms(T.feat[:], 1.0, "m_ft")
+    eq(T.sel[:], T.cc[0:16, 0:128], T.scol[0:16, 0:1], "v_sel")
+    need("v", "v_cg1")
+    fin(V.tensor_scalar(T.cc[0:16, 256:272], T.cc[0:16, 0:256:16], T.scol[0:16, 1:2], None, A.mult), "v_sel")
     need("s", "v_int")
     square(T.lc0[:], T.ints[:, 1:2], -4.0, 62.0, "a_lc0")
-    need("s", "a_lc0")
-    table(T.lcol[:], T.lc0[:], 1.0, 4095.75 / 16 - 15.0 / 32, "a_lc")
     need("s", "i_b", "m_r")
     square(T.rall[64:96, 0:256], T.cc[64:96, 0:256], 0.0625, 0.0, "a_c")
     square(T.rall[64:96, 256:272], T.cc[64:96, 0:256:16], 0.0625, 0.0, "a_c")
+    need("s", "a_lc0")
+    table(T.lcol[:], T.lc0[:], 1.0, 4095.75 / 16 - 15.0 / 32, "a_lc")
     need("s", "i_a")
     for c in (0, 128):
         square(T.rall[32:64, c:c + 128], T.aa[32:64, :], 0.0625, 0.0, "a_c")
@@ -195,10 +197,11 @@ def rank_program(g, core, T, topo):
 
     need("v", "s_pos")
     fin(V.tensor_copy(T.posc[:], T.posi[:, 1:2]), "v_posc")
+    ms(T.feat[:], 1.0, "m_ft")
     need("v", "v_sel", "i_a")
     for c in (0, 128):
         fin(V.tensor_copy(T.cc[0:8, c:c + 128], T.aa[0:8, :]), "v_cc")
-    fin(V.tensor_copy(T.posb[:], T.posi[0:8, 1:3]), "a_pos")
+    fin(V.tensor_copy(T.posb[:], T.posi[0:8, 0:2]), "a_pos")
     need("v", "v_posc", "v_cc", "m_all")
     fin(V.tensor_scalar(T.rall[0:16, :], T.cc[0:16, :], T.posc[:], None, A.add), "v_rall")
     need("s", "v_posc", "v_sel", "m_all")
@@ -214,19 +217,20 @@ def rank_program(g, core, T, topo):
     fin(E.matmul(T.pf0[:, 0:256], T.lall[:], T.rall[:, 0:256], True, True), "t_m")
     need("v", "t_l", "a_lc")
     lin(T.sl[:], T.pt[:, 0:16], 0.0625, T.lcol[:], "v_sl")
-    need("v", "m_lw0")
-    ms(T.lhw[32:64, :], 1.0 / 32, "m_lw1")
-    ms(T.lhw[96:128, :], 0.5, "m_lw1")
+    need("v", "t_m", "v_bc")
+    fin(V.tensor_scalar(T.mask[:, 0:128], T.pf0[:, 0:128], BIG, T.bcol[:], A.add, A.is_equal), "v_m")
     need("v", "v_sl")
     fin(V.tensor_scalar(T.ci[:], T.sl[:], 511, None, A.bitwise_and), "v_ci")
-    need("v", "t_m", "v_bc")
-    fin(V.tensor_scalar(T.mask[:], T.pf0[:, 0:256], BIG, T.bcol[:], A.add, A.is_equal), "v_m")
+    fin(V.tensor_scalar(T.mask[:, 128:256], T.pf0[:, 128:256], BIG, T.bcol[:], A.add, A.is_equal), "v_m")
     need("v", "v_ci")
     fin(V.tensor_copy(T.cidx[:], T.ci[:]), "v_cidx")
     need("v", "i_u")
-    eq(T.bsel[:], T.cu[:, 16:144:16], T.cols[:, 3:4], "v_bs")
+    eq(T.st[:], T.cu[:, 1:144], T.cols[:, 3:4], "v_bs")
+    need("v", "m_lw0")
+    ms(T.lhw[32:64, :], 1.0 / 32, "m_lw1")
+    ms(T.lhw[96:128, :], 0.5, "m_lw1")
 
-    table(T.posf[:], T.posi[0:8, 1:3], -1.0, 0.0, "a_pf")
+    table(T.posf[:], T.posi[0:8, 0:2], -1.0, 0.0, "a_pf")
     need("s", "t_pos")
     table(T.neg[:], T.pm[:, 0:2], -1.0, 0.0, "a_neg")
     for p0, p1, k, b in ((0, 32, -0.5, -16.0), (32, 64, 0.0, 1.0), (64, 128, 0.0, 0.0)):
@@ -251,40 +255,46 @@ def rank_program(g, core, T, topo):
         need("s", "a_off", "s_tr", *(["v_off"] if b > 256 else []))
         fin(S.activation(T.zed[:, 16 * a:16 * b], T.trs[:, 0:2048].indirect(T.off[:, a:b]), F.Copy), "a_z")
 
-    def zv(a, b):
+    at = [ZS[-1]]
+
+    def zv(k):
+        a, b = at[0], at[0] + k
+        at[0] = b
         need("v", "v_off", "s_tr")
         fin(V.tensor_copy(T.zed[:, 16 * a:16 * b], T.trs[:, 0:2048].indirect(T.off[:, a:b])), "v_z")
 
     zs(ZS[0], ZS[1])
 
     need("v", "v_cidx", "v_m", "s_row")
-    fin(V.tensor_tensor(T.yg[:], T.row[:, 0:512].indirect(T.cidx[:, 0:16]), T.mask[:], A.mult), "v_yg")
+    for x, (a, b) in enumerate(((0, 8), (8, 16))):
+        c = slice(16 * a, 16 * b)
+        fin(V.tensor_tensor(T.yg[:, c], T.row[:, 0:512].indirect(T.cidx[:, a:b]), T.mask[:, c], A.mult), "v_yg%d" % x)
+        need("t", "v_yg%d" % x, "v_bs")
+        for r in range(a, b):
+            ins = E.matmul(T.po[:, 0:16], T.st[:, 15 - r:143 - r], T.yg[:, 16 * r:16 * r + 16], r == 0, r == 15)
+    fin(ins, "t_off")
     eq(T.idh[:], T.cu[:, 16:144], T.cols[:, 0:1], "v_idh")
     eq(T.qs[:], T.cu[:, 0:48], T.cols[:, 1:2], "v_qs")
-    need("t", "v_yg", "v_bs")
-    for r in range(16):
-        ins = E.matmul(T.po[0:16, r:128:16], T.yg[:, r::16], T.bsel[:], True, True)
-    fin(ins, "t_o1")
-    need("v", "t_o1")
-    fin(V.tensor_copy(T.cgt[:], T.po[0:16, 0:128]), "v_cgt")
-    need("t", "v_cgt", "v_idh")
-    fin(E.matmul(T.pt[:, 0:16], T.cgt[:], T.idh[0:16, 0:16], True, True), "t_off")
-    fin(V.tensor_copy(T.off[:, 256:384], T.row[:, 256:384]), "v_off")
+    fin(V.tensor_copy(T.off[:, 256:512], T.row[:, 256:512]), "v_off")
     need("v", "t_off")
-    fin(V.tensor_copy(T.off2[:], T.pt[:, 0:16]), "v_off2")
+    fin(V.tensor_copy(T.off2[:], T.po[:, 0:16]), "v_off2")
+    zv(ONE)
     need("v", "v_off2", "s_tr")
-    fin(V.tensor_copy(T.cg[:], T.trs[:, 0:2048].indirect(T.off2[:])), "v_cg")
-    need("t", "v_qs", "v_cg")
+    fin(V.tensor_copy(T.cg[:, 0:128], T.trs[:, 0:2048].indirect(T.off2[:, 0:8])), "v_cg")
+    need("s", "v_off2")
+    fin(S.activation(T.cg[:, 128:256], T.trs[:, 0:2048].indirect(T.off2[:, 8:16]), F.Copy), "a_cg")
+    zs(ZS[1], ZS[2])
+    need("t", "v_qs", "v_cg", "a_cg")
     for b in range(4):
         for h in range(2):
             c = 128 * h + 32 * b
             ins = E.matmul(T.pc[32 * b:32 * b + 32, 0:32], T.qs[:, 16 - 16 * h:48 - 16 * h], T.cg[:, c:c + 32], h == 0, h == 1)
     fin(ins, "t_c")
-    fin(V.tensor_copy(T.off[:, 384:512], T.row[:, 384:512]), "v_off")
     need("v", "a_ky", "a_rx", "i_k")
     fin(V.tensor_scalar(T.ky1[:], T.kysq[:], T.rx2[:, 0:1], -7.5, A.add, A.add), "v_k1")
     eq(T.gee[0:64, :], T.kcol[0:64, :], T.cols[0:64, 2:3], "v_g", 8.0)
     eq(T.gee[96:128, :], T.kcol[96:128, :], T.cols[96:128, 2:3], "v_g", 8.0)
+    zv(ONE)
     need("v", "t_c")
     fin(V.tensor_copy(T.sendc[:], T.pc[:, 0:32]), "v_sendc")
 
@@ -314,10 +324,10 @@ def rank_program(g, core, T, topo):
     select(T.gee[64:96, :], T.coef[64:96, :], [[h0 - h1, 2], [-2, half], [0, 16]], A.is_equal, 7 - h0, -1, "i_g")
     need("v", "v_k1")
     fin(V.tensor_scalar(T.ky2[:], T.ky1[:], MID, MID, A.add, A.subtract), "v_k2")
-    zv(ZV[0], ZV[2])
+    zv(512 - ZS[-1] - 5 * ONE - 2 * TWO)
 
     pa, pb = [T.ps, T.pc], [T.po, T.pt]
-    need("t", "i_idf", "v_k2", "v_sendc")
+    need("t", "i_idf", "v_k2", "v_sendc", "v_idh")
     for b in (pa, pb):
         for h, (k0, c) in enumerate(hs):
             E.matmul(b[h][:, 0:64], T.idf[:], T.ky2[:, c], True, False)
@@ -328,25 +338,28 @@ def rank_program(g, core, T, topo):
     fin(ins, "t_sum")
     need("s", "t_sum")
     fin(S.activation(T.sq[:], T.pe[:, 0:32], F.Square), "a_sq")
-    zs(ZS[1], ZS[2])
+    zs(ZS[2], ZS[3])
     need("t", "a_sq", "i_em")
     fin(E.matmul(T.pe[:, 64:96], T.em[:], T.sq[:], True, True), "t_e")
     need("v", "t_e")
     fin(V.tensor_reduce(T.mx[:], T.pe[:, 64:96], AxisListType.X, A.max), "v_mx")
+    zv(ONE)
     need("v", "v_mx")
     fin(V.tensor_scalar(T.uu[:], T.pe[:, 64:96], T.mx[:, 0:1], None, A.is_lt), "v_u")
+    zv(ONE)
     need("v", "v_u", "a_d1")
     fin(V.tensor_tensor_scan(T.ff[:], T.uu[:], T.dfw[:], 0.0, A.mult, A.add), "v_f")
+    zv(ONE)
     need("v", "v_f", "v_g", "i_g")
     fin(V.tensor_scalar(T.rhs[:], T.gee[:], T.ff[:, 31:32], None, A.mult), "v_rhs")
-    zv(ZV[2], ZV[3])
+    zv(TWO)
     need("t", "v_rhs", "a_lh4", "i_idn")
     for h, (k0, c) in enumerate(hs):
         fin(E.matmul(pa[h][:, 0:64], T.lh4[:], T.rhs[:, c], False, True), "t_s%d" % h)
     for h, (k0, c) in enumerate(hs):
         need("v", "t_s%d" % h)
         lin(T.wb[:, c], pa[h][:, 0:64], 1.0 / 8192, 1100 - 4088.0 / 8192, "v_w%d" % h)
-    zv(ZV[3], ZV[4])
+    zv(TWO)
     for h, (k0, c) in enumerate(hs):
         E.matmul(pb[h][:, 0:64], T.lh4[:], T.rhs[:, c], False, False)
         need("t", "v_w%d" % h)
@@ -367,12 +380,11 @@ def rank_program(g, core, T, topo):
         need(q, "v_l%d" % (i // half), "v_z", "a_z")
         fin(S.activation(o, w, F.Copy) if q == "s" else V.tensor_copy(o, w), name or "p%d" % i)
 
-    first = korder[:half]
+    first = calls(rank)[0] + calls(rank)[1]
     far1 = [d for d in korder[half:] if d in off]
     mate = on[0]
     home = {d: ((T.pf0, T.po)[i // 2], 32 * (i % 2), i) for i, d in enumerate(first)}
-    home.update({d: (T.pf1, 32 * i, half + i) for i, d in enumerate(far1)})
-    home.update({mate: (T.pe, 0, n - 2), rank: (T.ps, 0, n - 1)})
+    home.update({far1[0]: (T.pf1, 0, half), far1[1]: (T.pe, 0, half + 1), mate: (T.pe, 32, half + 2), rank: (T.ps, 0, n - 1)})
 
     def add_up(d, name=None, more=()):
         i = korder.index(d)
@@ -391,26 +403,28 @@ def rank_program(g, core, T, topo):
     pick("s", first[3])
     add_up(first[0])
     add_up(first[1], "t_f0")
+    pick("v", mate, 0, 8)
     need("v", "t_f0")
     fin(V.tensor_copy(T.sendf[:, 0:64], T.pf0[:, 0:64]), "v_e0")
     pick("v", far1[0])
     pick("s", far1[1])
+    pick("s", mate, 8, 16, "p8")
     add_up(first[2])
     add_up(first[3], "t_f4")
     need("s", "t_f4")
     table(T.sendf[:, 64:128], T.po[:, 0:64], 1.0, 0.0, "v_e2")
-    pick("v", mate, 0, 8)
-    pick("s", mate, 8, 16, "p8")
-    need("t", "v_u", "v_w0")
-    add_up(far1[0])
-    add_up(far1[1], "t_f1")
-    add_up(mate, "t_f2", ("p8",))
-    need("v", "t_f1")
-    fin(V.tensor_copy(T.sendf[:, 128:192], T.pf1[:, 0:64]), "v_e1")
-    need("s", "t_f2")
-    table(T.sendf[:, 192:224], T.pe[:, 0:32], 1.0, 0.0, "a_e1")
     pick("s", rank)
+    need("t", "v_u", "v_w0")
+    add_up(far1[1])
+    add_up(mate, "t_f2", ("p8",))
+    add_up(far1[0], "t_f1")
     add_up(rank, "t_f3")
+    need("v", "t_w", "i_kw")
+    fin(V.tensor_tensor(T.wout[:], T.pm[0:1, 300:308], T.kw[:], A.add), "v_w")
+    need("v", "t_f1")
+    fin(V.tensor_copy(T.sendf[:, 128:160], T.pf1[:, 0:32]), "v_e1")
+    need("s", "t_f2")
+    table(T.sendf[:, 160:224], T.pe[:, 0:64], 1.0, 0.0, "a_e1")
     need("s", "t_f3")
     table(T.sendf[:, 224:256], T.ps[:, 0:32], 1.0, 0.0, "a_e2")
 
@@ -431,20 +445,24 @@ def rank_program(g, core, T, topo):
         for r in rs:
             cnt["r_f%d" % r] = len(masks(r, calls(r)[h])[rank])
 
-    need("v", "t_w", "i_kw")
-    fin(V.tensor_tensor(T.wout[:], T.pm[0:1, 300:308], T.kw[:], A.add), "v_w")
     need("y", "v_w")
     fin(Y.dma_start(T.w[:], T.wout[:]), "s_y", 16)
 
     need("t", "a_e2", "v_w1")
-    E.matmul(T.pc[0:32, 0:128], T.sendf[:, 224:256], T.idh[:], True, False)
-    for i, r in enumerate(coming):
-        need("t", "r_f%d" % r)
-        ins = E.matmul(T.pc[0:32, 0:128], T.landf[:, 32 * r:32 * r + 32], T.idh[:], False, i == n - 2)
-    fin(ins, "t_y")
+    need("t", "v_l1")
+    for i, r in enumerate([rank] + coming):
+        if i:
+            need("t", "r_f%d" % r)
+        part = T.landf[:, 32 * r:32 * r + 32] if i else T.sendf[:, 224:256]
+        for x, b in enumerate((T.pc, T.pt)):
+            ins = E.matmul(b[0:32, 0:64], part, T.idh[:, 64 * x:64 * x + 64], i == 0, i == n - 1)
+            if i == n - 1:
+                fin(ins, ("t_y1", "t_y")[x])
+    need("s", "t_y1")
+    table(T.yout[:, 0:64], T.pc[0:32, 0:64], 1.0, 0.0, "a_y")
     need("v", "t_y")
-    fin(V.tensor_copy(T.yout[:], T.pc[0:32, 0:128]), "v_y")
-    need("y", "v_y")
+    fin(V.tensor_copy(T.yout[:, 64:128], T.pt[0:32, 0:64]), "v_y")
+    need("y", "v_y", "a_y")
     fin(Y.dma_start(T.y[:], T.yout[:]), "s_y", 16)
     need("y", "s_y")
     done = {}

@@ -2,8 +2,8 @@ from concourse.bass import DstId, RemoteDMATransfer
 from concourse.mybir import AluOpType, AxisListType, ActivationFunctionType
 
 BIG = 1.5 * 2.0 ** 36
-MID = 1.5 * 2.0 ** 27
-ZS = (0, 54, 220, 306)
+ZC = 510
+ZS = (0, 36, 200, 288)
 ONE, TWO = 8, 16
 
 F32, B16, H16, I32, U16 = "float32", "bfloat16", "float16", "int32", "uint16"
@@ -12,36 +12,36 @@ SCRATCH = {
     "posf": ("sbuf", [8, 2], F32), "feat": ("sbuf", [8, 128], H16), "sel": ("sbuf", [16, 128], H16),
     "aa": ("sbuf", [128, 128], B16), "cc": ("sbuf", [96, 288], B16), "rall": ("sbuf", [96, 288], H16),
     "lall": ("sbuf", [96, 128], H16), "l3b": ("sbuf", [8, 128], H16),
-    "fea2": ("sbuf", [8, 128], H16), "cgt": ("sbuf", [16, 128], H16),
+    "fea2": ("sbuf", [8, 128], H16), "pin": ("sbuf", [128, 4, 128], I32), "pf": ("sbuf", [128, 8, 4, 16], H16),
     "kw": ("sbuf", [1, 8], F32), "wout": ("sbuf", [1, 8], F32), "yout": ("sbuf", [32, 128], F32),
 }
 for _nm, _w, _t in [
-        ("row", 512, I32), ("off", 512, U16), ("zed", 8192, B16), ("trs", 2048, B16), ("ints", 8, I32), ("cols", 8, F32),
-        ("cu", 144, F32), ("st", 143, H16), ("scol", 2, F32),
-        ("lc0", 1, F32), ("lcol", 1, F32), ("bcol", 1, F32), ("idn", 128, H16), ("neg8", 128, B16),
+        ("row", 512, I32), ("off", 512, U16), ("zed", 16 * ZC, B16), ("trs", 2048, B16), ("ints", 8, I32), ("cols", 8, F32),
+        ("cu", 144, F32), ("st", 143, H16), ("scol", 2, F32), ("ecol", 1, F32),
+        ("lc0", 1, F32), ("lcol", 1, F32), ("bcol", 1, F32), ("r64", 64, F32), ("id64", 64, H16),
         ("qs", 48, B16), ("idh", 128, H16), ("idf", 128, F32), ("one", 128, F32), ("em", 128, F32),
         ("dfw", 32, F32), ("kcol", 128, B16), ("coef", 128, B16),
-        ("gee", 128, B16), ("kyi", 128, B16), ("kysq", 128, F32), ("ky1", 128, F32), ("ky2", 128, F32),
+        ("gee", 128, B16), ("kyi", 128, B16), ("kysq", 128, F32), ("rxo", 1, F32),
         ("lh4", 128, B16), ("lhw", 1, B16), ("neg", 2, F32), ("mask", 256, F32), ("rx2", 1, F32),
         ("sl", 16, I32), ("ci", 16, I32), ("cidx", 16, U16), ("yg", 256, H16), ("off2", 16, U16), ("cg", 256, B16),
         ("sendc", 32, H16), ("landc", 256, H16), ("sq", 32, F32), ("mx", 1, F32), ("uu", 32, F32), ("ff", 32, F32),
-        ("rhs", 128, B16), ("wb", 128, H16), ("lst", 128, U16),
+        ("rhs", 128, B16), ("lst", 128, U16),
         ("fg", 2048, B16), ("sendf", 256, H16), ("landf", 256, H16)]:
     SCRATCH[_nm] = ("sbuf", [128, _w], _t)
 for _nm in ["pt", "po", "pc", "pe", "ps", "pf0", "pf1", "pm"]:
     SCRATCH[_nm] = ("psum", [128, 512], F32)
 SEMAPHORES = ["s_pos", "s_row", "s_tr", "s_y",
               "i_p", "i_a", "i_b", "i_l3", "i_u", "i_k", "i_ky", "i_one", "i_idf", "i_e0", "i_em",
-              "i_g0", "i_g", "i_n0", "i_idn", "i_kw",
+              "i_g0", "i_g", "i_r", "i_kw", "s_tau", "v_i64", "a_p0", "a_p1", "t_n", "a_rxo",
               "m_all", "m_lw0", "m_lw1", "m_tr0", "m_tr1",
               "v_int", "v_in0", "v_cg1", "t_y1", "a_y", "v_col", "v_sc", "v_bc", "v_sel", "v_cc", "v_posc", "v_rall", "v_bs", "v_qs", "v_idh", "v_g",
-              "v_off", "v_sl", "v_ci", "v_cidx", "v_m", "v_k1", "v_k2", "v_z",
+              "v_off", "v_of0", "v_sl", "v_ci", "v_cidx", "v_m", "v_k1", "v_k2", "v_z",
               "v_yg0", "v_yg1", "v_off2", "v_cg", "v_sendc", "v_mx", "v_u", "v_f", "v_rhs",
               "v_w0", "v_w1", "v_l0", "v_l1", "v_e0", "v_e1", "v_w", "v_y",
               "a_cg", "a_c", "a_d", "a_d1", "m_ft", "m_r", "m_l", "a_lc0", "a_lc", "a_lall", "a_neg", "a_rx", "a_ky",
               "a_lh4", "a_sq", "a_off", "a_z", "a_e1", "a_e2", "a_pos", "a_pf", "a_feat",
               "t_l", "t_m", "t_pos", "t_o1", "t_off", "t_c", "t_lh4", "t_sum", "t_e", "t_s0",
-              "t_s1", "t_r0", "t_r1", "t_w", "t_f0", "t_f1", "t_f2", "t_f3", "t_y", "l_c", "l_f", "l_t", "p8", "t_f4", "v_e2"] \
+              "t_s1", "t_r0", "t_r1", "t_w", "t_f0", "t_f1", "t_f2", "t_f3", "t_y", "l_c", "l_f", "l_t", "p8", "p9", "p10", "t_f4", "v_e2"] \
     + [_a + str(_i) for _a in ("p", "r_c", "r_f") for _i in range(8)]
 
 
@@ -81,21 +81,18 @@ def rank_program(g, core, T, topo):
     def masks(r, dests):
         src = cores[r]
         off = [d for d in dests if topo.chip(cores[d]) != topo.chip(src)]
-        out, taken = {}, []
+        out = {d: coarse_masks(r)[3] for d in dests}
         for i, d in enumerate(off):
             es = topo.engines(src, cores[d])
             w = len(es) // len(off)
             out[d] = es[i * w:i * w + w]
-            taken = es
-        for d in dests:
-            if d not in off:
-                out[d] = [e for e in topo.engines(src, cores[d]) if e not in taken][:4]
         return out
 
     def calls(r):
         o = order(r)
         a = sorted(o[:half], key=lambda d: far(r, d))
-        return a[:2], a[2:], [d for d in o[half:] if d != r]
+        b = sorted([d for d in o[half:] if d != r], key=lambda d: far(r, d))
+        return a[:2], a[2:], b[:2], b[2:]
 
     def others(r):
         return sorted([d for d in range(n) if d != r], key=lambda d: far(r, d))
@@ -105,7 +102,7 @@ def rank_program(g, core, T, topo):
         off = [d for d in others(r) if topo.chip(cores[d]) != topo.chip(src)]
         on = [d for d in others(r) if d not in off]
         oe = topo.engines(src, cores[off[0]])
-        ne = [e for e in topo.engines(src, cores[on[0]]) if e not in oe][:4] if on else []
+        ne = [e for e in topo.engines(src, cores[on[0]]) if e not in oe]
         return off, oe, on, ne
 
     def dst(d):
@@ -120,7 +117,9 @@ def rank_program(g, core, T, topo):
 
     fin(Y.dma_start(T.posi[0:8, 0:2], T.pos[:]), "s_pos", 16)
     fin(S.dma_start(T.posi[8:16, 1:3], T.pos[:]), "s_pos", 16)
-    fin(S.dma_start(T.row[:], T.tau[:]), "s_row", 16)
+    for s in range(8):
+        fin((Y, S)[s % 2].dma_start(T.pin[64 * (s // 4):64 * (s // 4) + 64, s % 4, :], T.tau[s:s + 1, :]), "s_tau", 16)
+    fin(Y.dma_start(T.row[:], T.tau[:]), "s_row", 16)
     fin(Y.dma_start(T.trs[:], T.tr[:]), "s_tr", 16)
 
     def iota(ap, pat, base, cm, name):
@@ -148,24 +147,24 @@ def rank_program(g, core, T, topo):
     fin(g.iota(T.ints[:, 0:1], [[1, 1]], 0, 1), "i_p")
     iota(T.cc[:, 0:256], [[32, 16], [0, 16]], -496, 0, "i_b")
     iota(T.aa[:], [[0, 8], [32, 16]], -496, 0, "i_a")
+    iota(T.r64[:], [[1, 64]], 0, 0, "i_r")
     need("g", "i_a")
     select(T.l3b[:], T.aa[0:8, :], [[1, 8], [0, 16]], A.is_equal, 0, -1, "i_l3")
     ms(T.rall[:], 64.5, "m_r")
     ms(T.lall[:], 2.0, "m_l")
     ms(T.cc[0:16, 272:288], 0.0, "v_cc")
     need("v", "i_p")
-    for i, b, nm in ((2, 7, "v_in0"), (4, 8, "v_in0"), (1, 15, "v_int"), (3, 112, "v_int")):
+    for i, b, nm in ((2, 7, "v_in0"), (4, 8, "v_in0"), (1, 15, "v_int"), (3, 112, "v_int"), (5, 63, "v_int")):
         fin(V.tensor_scalar(T.ints[:, i:i + 1], T.ints[:, 0:1], b, None, A.bitwise_and), nm)
     need("v", "m_r", "m_l")
     ms(T.lall[0:32, :], -63.5 / 16, "m_all")
-    ms(T.rall[32:64, 256:272], 0.0, "m_all")
     need("v", "v_in0")
     lin(T.scol[:, 0:1], T.ints[:, 2:3], 32.0, -496.0, "v_sc")
     lin(T.scol[:, 1:2], T.ints[:, 4:5], 0.125, 0.0, "v_cg1")
+    ms(T.rall[32:64, 256:272], 0.0, "m_all")
     need("v", "v_int")
-    fin(V.tensor_copy(T.cols[:, 0:4], T.ints[:, 0:4]), "v_col")
+    fin(V.tensor_copy(T.cols[:, 0:6], T.ints[:, 0:6]), "v_col")
     lin(T.bcol[:], T.ints[:, 1:2], 8192.0, BIG, "v_bc")
-    ms(T.fea2[:], 0.0, "m_tr0")
     need("v", "v_sc", "i_b")
     eq(T.sel[:], T.cc[0:16, 0:128], T.scol[0:16, 0:1], "v_sel")
     need("v", "v_cg1")
@@ -185,10 +184,13 @@ def rank_program(g, core, T, topo):
     iota(T.cu[:], [[1, 144]], -16, 0, "i_u")
     iota(T.kcol[:], [[h0 - h1, 2], [-2, half], [0, 16]], 7 - h0, 0, "i_k")
     low = rank < on[0]
-    full, tab, nm, got = (T.one, T.idf, "i_idf", "i_idn") if low else (T.neg8, T.idn, "i_idn", "i_idf")
-    iota(full[:], [[0, 128]], 1 if low else -8192, 0, "i_one" if low else "i_n0")
-    need("g", "i_one" if low else "i_n0")
-    select(tab[:], full[:], [[-1, 128]], A.is_equal, 0, 1, nm)
+    tab, nm, got = (T.idf, "i_idf", "i_g0") if low else (T.coef, "i_g0", "i_idf")
+    if low:
+        iota(T.one[:], [[0, 128]], 1, 0, "i_one")
+        need("g", "i_one")
+        select(T.idf[:], T.one[:], [[-1, 128]], A.is_equal, 0, 1, nm)
+    else:
+        iota(T.coef[:], [[1024 * half * (h1 - h0), 2], [1024, half], [32, 16]], 256 + 1024 * half * h0, 0, nm)
     need("g", nm)
     g.remote_dma_fused([RemoteDMATransfer(dst_ids=[dst(on[0])], dma_engine_mask=bits(es), remote_sem=T.sem[nm],
                                           srcs=[tab[:, c:c + 64]], dsts=[tab[:, c:c + 64]])
@@ -198,6 +200,7 @@ def rank_program(g, core, T, topo):
     need("v", "s_pos")
     fin(V.tensor_copy(T.posc[:], T.posi[:, 1:2]), "v_posc")
     ms(T.feat[:], 1.0, "m_ft")
+    ms(T.fea2[:], 0.0, "m_tr0")
     need("v", "v_sel", "i_a")
     for c in (0, 128):
         fin(V.tensor_copy(T.cc[0:8, c:c + 128], T.aa[0:8, :]), "v_cc")
@@ -209,6 +212,12 @@ def rank_program(g, core, T, topo):
     need("v", "m_tr0")
     ms(T.fea2[:, 32:64], 1.0 / 32, "m_tr1")
     ms(T.lhw[:], 0.0, "m_lw0")
+    need("v", "v_col")
+    lin(T.ecol[:], T.cols[:, 3:4], 2.0, -496.0, "i_e0")
+    need("v", "i_r")
+    eq(T.id64[:], T.r64[:], T.cols[:, 5:6], "v_i64")
+    need("v", "i_e0")
+    eq(T.em[:], T.aa[:], T.ecol[:], "i_em")
     need("t", "a_pos", "v_sel")
     fin(E.matmul(T.pm[:, 0:2], T.sel[0:8, :], T.posb[:], True, True), "t_pos")
     need("t", "v_rall", "a_lall", "a_c", "i_l3")
@@ -226,33 +235,42 @@ def rank_program(g, core, T, topo):
     fin(V.tensor_copy(T.cidx[:], T.ci[:]), "v_cidx")
     need("v", "i_u")
     eq(T.st[:], T.cu[:, 1:144], T.cols[:, 3:4], "v_bs")
-    need("v", "m_lw0")
-    ms(T.lhw[32:64, :], 1.0 / 32, "m_lw1")
-    ms(T.lhw[96:128, :], 0.5, "m_lw1")
+    eq(T.qs[:], T.cu[:, 0:48], T.cols[:, 1:2], "v_qs")
 
     table(T.posf[:], T.posi[0:8, 0:2], -1.0, 0.0, "a_pf")
-    need("s", "t_pos")
-    table(T.neg[:], T.pm[:, 0:2], -1.0, 0.0, "a_neg")
     for p0, p1, k, b in ((0, 32, -0.5, -16.0), (32, 64, 0.0, 1.0), (64, 128, 0.0, 0.0)):
         table(T.dfw[p0:p1, :], T.aa[p0:p1, 0:32], k, b, "a_d")
-    need("s", "a_pf", "m_ft")
+    need("s", "s_tau")
+    need("t", "v_i64")
+    for x in range(2):
+        for c in range(4 * x, 4 * x + 4):
+            table(T.pf[:, c, :, :], T.pin[:, :, 16 * c:16 * c + 16], 1.0, 0.0, "a_p%d" % x)
+        need("t", "a_p%d" % x)
+        for c in range(4 * x, 4 * x + 4):
+            for p in (slice(0, 64), slice(64, 128)):
+                ins = E.matmul(T.pf1[p, c::8], T.pf[p, c, :, :], T.id64[p, :], True, True)
+    fin(ins, "t_n")
+    need("s", "t_pos", "a_pf", "m_ft")
+    table(T.neg[:], T.pm[:, 0:2], -1.0, 0.0, "a_neg")
     fin(S.activation(T.feat[:, 32:64], T.feat[:, 0:32], F.Copy, bias=15.5, scale=T.posf[:, 0:1]), "a_feat")
     fin(S.activation(T.feat[:, 96:128], T.feat[:, 0:32], F.Copy, scale=T.posf[:, 1:2]), "a_feat")
-    need("s", "s_row")
-    table(T.off[:, 0:256], T.row[:, 0:256], 1.0, 0.0, "a_off")
     need("t", "a_feat", "m_tr1", "a_neg")
     E.matmul(T.pm[:, 128:256], T.feat[:], T.sel[0:8, :], True, False)
     fin(E.matmul(T.pm[:, 128:256], T.fea2[:], T.l3b[:], False, True), "t_lh4")
-    need("s", "a_neg", "v_col", "i_ky", "a_d")
-    square(T.rx2[:], T.cols[:, 1:2], 1.0, T.neg[:, 0:1], "a_rx")
-    square(T.kysq[:], T.kyi[:], 1.0, T.neg[:, 1:2], "a_ky")
+    need("s", "a_d")
     for c, p0, p1, x in ((15, 0, 32, -1800.0), (15, 32, 64, -15.0), (15, 64, 128, 1.0), (31, 0, 64, 0.0)):
         table(T.dfw[p0:p1, c:c + 1], T.aa[p0:p1, 0:1], 0.0, x, "a_d1")
-    need("s", "t_lh4")
+    need("s", "a_neg", "v_col", "i_ky")
+    square(T.rx2[:], T.cols[:, 1:2], 1.0, T.neg[:, 0:1], "a_rx")
+    square(T.kysq[:], T.kyi[:], 1.0, T.neg[:, 1:2], "a_ky")
+    need("s", "t_n")
+    table(T.off[:, 0:64], T.pf1[:, 0:64], 1.0, 0.0, "a_off")
+    need("s", "t_lh4", "a_rx")
     table(T.lh4[:], T.pm[:, 128:256], 1.0, 0.0, "a_lh4")
+    table(T.rxo[:], T.rx2[:], 0.0625, -15.0 / 32, "a_rxo")
 
     def zs(a, b):
-        need("s", "a_off", "s_tr", *(["v_off"] if b > 256 else []))
+        need("s", "a_off", "s_tr", *(["v_of0"] if b > 64 else []))
         fin(S.activation(T.zed[:, 16 * a:16 * b], T.trs[:, 0:2048].indirect(T.off[:, a:b]), F.Copy), "a_z")
 
     at = [ZS[-1]]
@@ -260,7 +278,7 @@ def rank_program(g, core, T, topo):
     def zv(k):
         a, b = at[0], at[0] + k
         at[0] = b
-        need("v", "v_off", "s_tr")
+        need("v", "v_of0", "s_tr", *(["v_off"] if b > 352 else []))
         fin(V.tensor_copy(T.zed[:, 16 * a:16 * b], T.trs[:, 0:2048].indirect(T.off[:, a:b])), "v_z")
 
     zs(ZS[0], ZS[1])
@@ -274,11 +292,17 @@ def rank_program(g, core, T, topo):
             ins = E.matmul(T.po[:, 0:16], T.st[:, 15 - r:143 - r], T.yg[:, 16 * r:16 * r + 16], r == 0, r == 15)
     fin(ins, "t_off")
     eq(T.idh[:], T.cu[:, 16:144], T.cols[:, 0:1], "v_idh")
-    eq(T.qs[:], T.cu[:, 0:48], T.cols[:, 1:2], "v_qs")
-    fin(V.tensor_copy(T.off[:, 256:512], T.row[:, 256:512]), "v_off")
+    need("v", "i_k")
+    eq(T.gee[0:64, :], T.kcol[0:64, :], T.cols[0:64, 1:2], "v_g", 16.0)
+    eq(T.gee[96:128, :], T.kcol[96:128, :], T.cols[96:128, 1:2], "v_g", 16.0)
+    need("v", "a_off")
+    fin(V.tensor_copy(T.off[:, 64:352], T.pf1[:, 64:352]), "v_of0")
+    need("v", "m_lw0")
+    ms(T.lhw[32:64, :], 1.0 / 32, "m_lw1")
+    ms(T.lhw[96:128, :], 0.5, "m_lw1")
     need("v", "t_off")
     fin(V.tensor_copy(T.off2[:], T.po[:, 0:16]), "v_off2")
-    zv(ONE)
+    fin(V.tensor_copy(T.off[:, 352:512], T.pf1[:, 352:512]), "v_off")
     need("v", "v_off2", "s_tr")
     fin(V.tensor_copy(T.cg[:, 0:128], T.trs[:, 0:2048].indirect(T.off2[:, 0:8])), "v_cg")
     need("s", "v_off2")
@@ -290,49 +314,29 @@ def rank_program(g, core, T, topo):
             c = 128 * h + 32 * b
             ins = E.matmul(T.pc[32 * b:32 * b + 32, 0:32], T.qs[:, 16 - 16 * h:48 - 16 * h], T.cg[:, c:c + 32], h == 0, h == 1)
     fin(ins, "t_c")
-    need("v", "a_ky", "a_rx", "i_k")
-    fin(V.tensor_scalar(T.ky1[:], T.kysq[:], T.rx2[:, 0:1], -7.5, A.add, A.add), "v_k1")
-    eq(T.gee[0:64, :], T.kcol[0:64, :], T.cols[0:64, 2:3], "v_g", 8.0)
-    eq(T.gee[96:128, :], T.kcol[96:128, :], T.cols[96:128, 2:3], "v_g", 8.0)
-    zv(ONE)
+    zv(TWO)
     need("v", "t_c")
     fin(V.tensor_copy(T.sendc[:], T.pc[:, 0:32]), "v_sendc")
 
     mine = slice(32 * rank, 32 * rank + 32)
     rc = T.sem["r_c%d" % rank]
-    tr = [RemoteDMATransfer(dst_ids=[dst(d) for d in off], dma_engine_mask=bits(oe), remote_sem=rc,
-                            srcs=[T.sendc[:]], dsts=[T.landc[:, mine] for d in off])]
-    if on:
-        tr.append(RemoteDMATransfer(dst_ids=[dst(d) for d in on], dma_engine_mask=bits(ne), remote_sem=rc,
-                                    srcs=[T.sendc[:]], dsts=[T.landc[:, mine] for d in on]))
     need("g", "v_sendc")
-    g.remote_dma_fused(tr, local_sem=T.sem["l_c"])
-    cnt["l_c"] = len(oe) + (len(ne) if on else 0)
+    g.remote_dma_fused([RemoteDMATransfer(dst_ids=[dst(d) for d in ds], dma_engine_mask=bits(es), remote_sem=rc,
+                                          srcs=[T.sendc[:]], dsts=[T.landc[:, mine] for d in ds])
+                        for ds, es in ((off, oe), (on, ne))], local_sem=T.sem["l_c"])
+    cnt["l_c"] = len(oe) + len(ne)
     for r in others(rank):
-        o, e1, o2, e2 = coarse_masks(r)
-        cnt["r_c%d" % r] = len(e1) if rank in o else len(e2)
+        cnt["r_c%d" % r] = len(oe) if r in off else len(ne)
 
-    if not low:
-        iota(T.one[:], [[0, 128]], 1, 0, "i_one")
-        need("g", "i_one")
-    select(T.em[:], T.one[:], [[0, 16], [-16, 8]], A.is_ge, 0, 1, "i_e0")
-    iota(T.coef[:], [[1024 * half * (h1 - h0), 2], [1024, half], [32, 16]], 256 + 1024 * half * h0, 0, "i_g0")
-    need("g", "i_e0")
-    select(T.em[:], T.em[:], [[0, 16], [16, 8]], A.is_ge, 15, -1, "i_em")
     iota(T.kw[:], [[32, 8]], 0, 0, "i_kw")
     need("g", "i_kw", "i_g0")
     select(T.gee[64:96, :], T.coef[64:96, :], [[h0 - h1, 2], [-2, half], [0, 16]], A.is_equal, 7 - h0, -1, "i_g")
-    need("v", "v_k1")
-    fin(V.tensor_scalar(T.ky2[:], T.ky1[:], MID, MID, A.add, A.subtract), "v_k2")
-    zv(512 - ZS[-1] - 5 * ONE - 2 * TWO)
+    zv(ZC - ZS[-1] - 3 * ONE - 2 * TWO)
 
-    pa, pb = [T.ps, T.pc], [T.po, T.pt]
-    need("t", "i_idf", "v_k2", "v_sendc", "v_idh")
-    for b in (pa, pb):
-        for h, (k0, c) in enumerate(hs):
-            E.matmul(b[h][:, 0:64], T.idf[:], T.ky2[:, c], True, False)
+    pa = [T.ps, T.pc]
+    need("t", "v_sendc", "v_idh")
     E.matmul(T.pe[:, 0:32], T.idh[:], T.sendc[:], True, False)
-    for i, r in enumerate([r for r in others(rank) if r in on] + [r for r in others(rank) if r not in on]):
+    for i, r in enumerate(on + off):
         need("t", "r_c%d" % r)
         ins = E.matmul(T.pe[:, 0:32], T.idh[:], T.landc[:, 32 * r:32 * r + 32], False, i == n - 2)
     fin(ins, "t_sum")
@@ -341,6 +345,9 @@ def rank_program(g, core, T, topo):
     zs(ZS[2], ZS[3])
     need("t", "a_sq", "i_em")
     fin(E.matmul(T.pe[:, 64:96], T.em[:], T.sq[:], True, True), "t_e")
+    need("t", "i_idf", "a_ky")
+    for h, (k0, c) in enumerate(hs):
+        E.matmul(pa[h][:, 0:64], T.idf[:], T.kysq[:, c], True, False)
     need("v", "t_e")
     fin(V.tensor_reduce(T.mx[:], T.pe[:, 64:96], AxisListType.X, A.max), "v_mx")
     zv(ONE)
@@ -353,25 +360,16 @@ def rank_program(g, core, T, topo):
     need("v", "v_f", "v_g", "i_g")
     fin(V.tensor_scalar(T.rhs[:], T.gee[:], T.ff[:, 31:32], None, A.mult), "v_rhs")
     zv(TWO)
-    need("t", "v_rhs", "a_lh4", "i_idn")
+    need("t", "v_rhs", "a_lh4")
     for h, (k0, c) in enumerate(hs):
         fin(E.matmul(pa[h][:, 0:64], T.lh4[:], T.rhs[:, c], False, True), "t_s%d" % h)
-    for h, (k0, c) in enumerate(hs):
-        need("v", "t_s%d" % h)
-        lin(T.wb[:, c], pa[h][:, 0:64], 1.0 / 8192, 1100 - 4088.0 / 8192, "v_w%d" % h)
-    zv(TWO)
-    for h, (k0, c) in enumerate(hs):
-        E.matmul(pb[h][:, 0:64], T.lh4[:], T.rhs[:, c], False, False)
-        need("t", "v_w%d" % h)
-        E.matmul(pb[h][:, 0:64], T.idn[:], T.wb[:, c], False, False)
-        fin(E.matmul(pb[h][:, 0:64], T.idh[:], T.wb[:, c], False, True), "t_r%d" % h)
     need("t", "m_lw1")
     for k0, c in hs:
         fin(E.matmul(T.pm[0:1, 300 + k0:304 + k0], T.lhw[:], T.rhs[:, c.start:c.stop:16], True, True), "t_w")
 
     def places(h):
-        need("v", "t_r%d" % h)
-        fin(V.tensor_scalar(T.lst[:, hs[h][1]], pb[h][:, 0:64], 8191.0 * 1100, None, A.add), "v_l%d" % h)
+        need("v", "t_s%d" % h, "a_rxo")
+        lin(T.lst[:, hs[h][1]], pa[h][:, 0:64], 0.0625, T.rxo[:], "v_l%d" % h)
 
     def pick(q, d, a=0, b=16, name=None):
         i = korder.index(d)
@@ -384,7 +382,7 @@ def rank_program(g, core, T, topo):
     far1 = [d for d in korder[half:] if d in off]
     mate = on[0]
     home = {d: ((T.pf0, T.po)[i // 2], 32 * (i % 2), i) for i, d in enumerate(first)}
-    home.update({far1[0]: (T.pf1, 0, half), far1[1]: (T.pe, 0, half + 1), mate: (T.pe, 32, half + 2), rank: (T.ps, 0, n - 1)})
+    home.update({far1[0]: (T.pf1, 0, half), far1[1]: (T.pf1, 32, half + 1), mate: (T.pe, 0, half + 2), rank: (T.ps, 0, n - 1)})
 
     def add_up(d, name=None, more=()):
         i = korder.index(d)
@@ -396,41 +394,44 @@ def rank_program(g, core, T, topo):
             fin(ins, name)
 
     places(0)
-    pick("v", first[0])
     places(1)
+    pick("v", first[0])
     pick("s", first[1])
     pick("v", first[2])
     pick("s", first[3])
     add_up(first[0])
     add_up(first[1], "t_f0")
-    pick("v", mate, 0, 8)
+    pick("v", far1[0], 0, 4, "p8")
     need("v", "t_f0")
     fin(V.tensor_copy(T.sendf[:, 0:64], T.pf0[:, 0:64]), "v_e0")
-    pick("v", far1[0])
+    pick("v", far1[0], 4, 16)
     pick("s", far1[1])
-    pick("s", mate, 8, 16, "p8")
+    pick("v", mate, 0, 8)
     add_up(first[2])
     add_up(first[3], "t_f4")
     need("s", "t_f4")
     table(T.sendf[:, 64:128], T.po[:, 0:64], 1.0, 0.0, "v_e2")
-    pick("s", rank)
-    need("t", "v_u", "v_w0")
+    pick("s", mate, 8, 16, "p9")
+    need("t", "v_u", "v_l0", "v_off", "p8")
     add_up(far1[1])
-    add_up(mate, "t_f2", ("p8",))
     add_up(far1[0], "t_f1")
+    add_up(mate, "t_f2", ("p9",))
+    pick("v", rank, 0, 4)
+    need("v", "t_f1")
+    fin(V.tensor_copy(T.sendf[:, 128:192], T.pf1[:, 0:64]), "v_e1")
+    pick("s", rank, 4, 16, "p10")
+    need("s", "t_f2")
+    table(T.sendf[:, 192:224], T.pe[:, 0:32], 1.0, 0.0, "a_e1")
+    need("t", "p10")
     add_up(rank, "t_f3")
     need("v", "t_w", "i_kw")
     fin(V.tensor_tensor(T.wout[:], T.pm[0:1, 300:308], T.kw[:], A.add), "v_w")
-    need("v", "t_f1")
-    fin(V.tensor_copy(T.sendf[:, 128:160], T.pf1[:, 0:32]), "v_e1")
-    need("s", "t_f2")
-    table(T.sendf[:, 160:224], T.pe[:, 0:64], 1.0, 0.0, "a_e1")
-    need("s", "t_f3")
-    table(T.sendf[:, 224:256], T.ps[:, 0:32], 1.0, 0.0, "a_e2")
+    need("v", "t_f3")
+    fin(V.tensor_copy(T.sendf[:, 224:256], T.ps[:, 0:32]), "a_e2")
 
     for h, dests in enumerate(calls(rank)):
         em = masks(rank, dests)
-        need("g", *(("v_e0",), ("v_e2",), ("v_e1", "a_e1"))[h])
+        need("g", ("v_e0", "v_e2", "v_e1", "a_e1")[h])
         tr = []
         for d in dests:
             k = home[d][2]
@@ -439,7 +440,7 @@ def rank_program(g, core, T, topo):
             cnt["l_f"] = cnt.get("l_f", 0) + len(em[d])
         g.remote_dma_fused(tr, local_sem=T.sem["l_f"])
     coming = []
-    for h in range(3):
+    for h in (0, 1, 3, 2):
         rs = [r for r in others(rank) if rank in calls(r)[h]]
         coming += [r for r in rs if r in on] + [r for r in rs if r not in on]
         for r in rs:
@@ -448,12 +449,10 @@ def rank_program(g, core, T, topo):
     need("y", "v_w")
     fin(Y.dma_start(T.w[:], T.wout[:]), "s_y", 16)
 
-    need("t", "a_e2", "v_w1")
     need("t", "v_l1")
-    for i, r in enumerate([rank] + coming):
-        if i:
-            need("t", "r_f%d" % r)
-        part = T.landf[:, 32 * r:32 * r + 32] if i else T.sendf[:, 224:256]
+    for i, r in enumerate(coming[:half] + [rank] + coming[half:]):
+        need("t", "r_f%d" % r if r != rank else "a_e2")
+        part = T.landf[:, 32 * r:32 * r + 32] if r != rank else T.sendf[:, 224:256]
         for x, b in enumerate((T.pc, T.pt)):
             ins = E.matmul(b[0:32, 0:64], part, T.idh[:, 64 * x:64 * x + 64], i == 0, i == n - 1)
             if i == n - 1:

@@ -1,47 +1,50 @@
 from concourse.bass import DstId, RemoteDMATransfer
 from concourse.mybir import AluOpType, AxisListType, ActivationFunctionType
 
-BIG = 1.5 * 2.0 ** 36
+B32 = 1.5 * 2.0 ** 28
+B512 = 1.5 * 2.0 ** 32
+KA, KB, KC = 21.703125, 11.796875, 3114.0
 ZC = 510
-ZS = (0, 36, 200, 288)
+ZS = (0, 28, 186, 266)
 ONE, TWO = 8, 16
+YG = ((0, 6, 6, 6), (6, 16, 6, 8))
+MC = 96
+F1, F2, F3, F4 = 4, 12, 6, 4
+TURNS = (0, 1, 2, 4, 3)
+CG = 4
+ZV, ZW = 16, 24
 
 F32, B16, H16, I32, U16 = "float32", "bfloat16", "float16", "int32", "uint16"
 SCRATCH = {
-    "posi": ("sbuf", [16, 4], I32), "posc": ("sbuf", [16, 1], F32), "posb": ("sbuf", [8, 2], H16),
-    "posf": ("sbuf", [8, 2], F32), "feat": ("sbuf", [8, 128], H16), "sel": ("sbuf", [16, 128], H16),
-    "aa": ("sbuf", [128, 128], B16), "cc": ("sbuf", [96, 288], B16), "rall": ("sbuf", [96, 288], H16),
-    "lall": ("sbuf", [96, 128], H16), "l3b": ("sbuf", [8, 128], H16),
-    "fea2": ("sbuf", [8, 128], H16), "pin": ("sbuf", [128, 4, 128], I32), "pf": ("sbuf", [128, 8, 4, 16], H16),
+    "posi": ("sbuf", [64, 4], I32), "posc": ("sbuf", [64, 1], F32), "dd": ("sbuf", [64, 256], H16),
+    "cc": ("sbuf", [64, 256], H16), "sqc": ("sbuf", [64, 272], H16), "gp": ("sbuf", [64, 128], B16),
+    "sel": ("sbuf", [64, 128], H16), "self": ("sbuf", [32, 128], F32), "lall": ("sbuf", [96, 128], H16), "rall": ("sbuf", [96, 272], H16),
+    "kcol": ("sbuf", [96, 128], B16), "l3b": ("sbuf", [32, 128], H16), "kyi": ("sbuf", [32, 128], B16), "by": ("sbuf", [32, 128], F32),
+    "c32": ("sbuf", [1, 32], H16), "lhw": ("sbuf", [64, 1], H16), "em0": ("sbuf", [128, 128], H16),
+    "pin": ("sbuf", [128, 4, 128], I32), "pf": ("sbuf", [128, 8, 4, 16], U16),
     "kw": ("sbuf", [1, 8], F32), "wout": ("sbuf", [1, 8], F32), "yout": ("sbuf", [32, 128], F32),
 }
 for _nm, _w, _t in [
-        ("row", 512, I32), ("off", 512, U16), ("zed", 16 * ZC, B16), ("trs", 2048, B16), ("ints", 8, I32), ("cols", 8, F32),
-        ("cu", 144, F32), ("st", 143, H16), ("scol", 2, F32), ("ecol", 1, F32),
-        ("lc0", 1, F32), ("lcol", 1, F32), ("bcol", 1, F32), ("r64", 64, F32), ("id64", 64, H16),
-        ("qs", 48, B16), ("idh", 128, H16), ("idf", 128, F32), ("one", 128, F32), ("em", 128, F32),
-        ("dfw", 32, F32), ("kcol", 128, B16), ("coef", 128, B16),
-        ("gee", 128, B16), ("kyi", 128, B16), ("kysq", 128, F32), ("rxo", 1, F32),
-        ("lh4", 128, B16), ("lhw", 1, B16), ("neg", 2, F32), ("mask", 256, F32), ("rx2", 1, F32),
-        ("sl", 16, I32), ("ci", 16, I32), ("cidx", 16, U16), ("yg", 256, H16), ("off2", 16, U16), ("cg", 256, B16),
+        ("row", 512, I32), ("off", 512, U16), ("zed", 16 * ZC, B16), ("trs", 2048, B16),
+        ("vv", 1, F32), ("q2", 1, F32), ("r2", 1, F32), ("bcol", 2, F32), ("cu", 144, B16), ("st", 143, H16),
+        ("qs", 48, B16), ("idh", 128, H16), ("one", 128, H16), ("em", 128, F32), ("kc", 128, F32),
+        ("dfw", 32, F32), ("gee", 128, H16), ("rx", 1, F32), ("lh4", 128, H16), ("mask", 256, F32), ("qu", 34, B16), ("landm", 256, B16),
+        ("wb", 16, B16), ("cidx", 16, U16), ("yg", 256, H16), ("off2", 16, U16), ("cg", 256, B16),
         ("sendc", 32, H16), ("landc", 256, H16), ("sq", 32, F32), ("mx", 1, F32), ("uu", 32, F32), ("ff", 32, F32),
-        ("rhs", 128, B16), ("lst", 128, U16),
+        ("rhs", 128, H16), ("lst", 128, U16),
         ("fg", 2048, B16), ("sendf", 256, H16), ("landf", 256, H16)]:
     SCRATCH[_nm] = ("sbuf", [128, _w], _t)
 for _nm in ["pt", "po", "pc", "pe", "ps", "pf0", "pf1", "pm"]:
     SCRATCH[_nm] = ("psum", [128, 512], F32)
-SEMAPHORES = ["s_pos", "s_row", "s_tr", "s_y",
-              "i_p", "i_a", "i_b", "i_l3", "i_u", "i_k", "i_ky", "i_one", "i_idf", "i_e0", "i_em",
-              "i_g0", "i_g", "i_r", "i_kw", "s_tau", "v_i64", "a_p0", "a_p1", "t_n", "a_rxo",
-              "m_all", "m_lw0", "m_lw1", "m_tr0", "m_tr1",
-              "v_int", "v_in0", "v_cg1", "t_y1", "a_y", "v_col", "v_sc", "v_bc", "v_sel", "v_cc", "v_posc", "v_rall", "v_bs", "v_qs", "v_idh", "v_g",
-              "v_off", "v_of0", "v_sl", "v_ci", "v_cidx", "v_m", "v_k1", "v_k2", "v_z",
-              "v_yg0", "v_yg1", "v_off2", "v_cg", "v_sendc", "v_mx", "v_u", "v_f", "v_rhs",
-              "v_w0", "v_w1", "v_l0", "v_l1", "v_e0", "v_e1", "v_w", "v_y",
-              "a_cg", "a_c", "a_d", "a_d1", "m_ft", "m_r", "m_l", "a_lc0", "a_lc", "a_lall", "a_neg", "a_rx", "a_ky",
-              "a_lh4", "a_sq", "a_off", "a_z", "a_e1", "a_e2", "a_pos", "a_pf", "a_feat",
-              "t_l", "t_m", "t_pos", "t_o1", "t_off", "t_c", "t_lh4", "t_sum", "t_e", "t_s0",
-              "t_s1", "t_r0", "t_r1", "t_w", "t_f0", "t_f1", "t_f2", "t_f3", "t_y", "l_c", "l_f", "l_t", "p8", "p9", "p10", "t_f4", "v_e2"] \
+SEMAPHORES = ["s_pos", "s_row", "s_tr", "s_y", "s_t0", "s_t1", "s_t2", "s_t3", "v_of0",
+              "i_p", "i_gp", "i_u", "i_l3", "i_ky", "i_e0", "i_em", "i_kc", "i_d0", "i_d", "i_g", "i_kw",
+              "m_one", "m_d0", "m_d1", "m_pos", "m_r", "m_k", "m_w",
+              "v_cc", "v_q", "v_r", "v_bc", "v_sel", "v_posc", "v_rall", "v_bs", "v_qs", "v_idh", "v_g",
+              "v_wb", "v_cidx", "v_m0", "v_m1", "v_off", "v_z", "v_yg0", "v_yg1", "v_yg2", "i_k", "v_off2", "v_cg0", "v_cg1", "a_cg0", "a_cg1", "v_sendc",
+              "v_mx", "v_u", "v_f", "v_rhs", "v_l0", "v_l1", "v_e0", "v_e1", "v_e2", "v_w", "v_y",
+              "a_c", "a_c1", "a_lall", "a_p0", "a_p1", "a_ky", "a_rx", "a_lh4", "a_off", "a_cg", "a_sq", "a_z", "a_z1", "a_e1", "a_e2", "a_y",
+              "t_a", "t_l", "t_m0", "t_m1", "t_lh4", "t_n", "t_off", "t_c", "t_sum", "t_e", "t_s0", "t_s1", "t_w",
+              "t_f0", "t_f1", "t_f2", "t_f3", "t_f4", "t_y", "t_y1", "l_c", "l_f", "l_t", "p8", "p9", "p10", "p11", "a_d0", "a_d1", "p12", "t_f5", "v_e3"] \
     + [_a + str(_i) for _a in ("p", "r_c", "r_f") for _i in range(8)]
 
 
@@ -76,7 +79,7 @@ def rank_program(g, core, T, topo):
 
     def far(r, d):
         a, b = topo.chip(cores[r]), topo.chip(cores[d])
-        return (3 if a == b else 2 if topo.same_plane(a, b) else 1 if topo.mates(a, b) else 0, r ^ d)
+        return (3 if a == b else 1 if topo.same_plane(a, b) else 2 if topo.mates(a, b) else 0, r ^ d)
 
     def masks(r, dests):
         src = cores[r]
@@ -88,11 +91,15 @@ def rank_program(g, core, T, topo):
             out[d] = es[i * w:i * w + w]
         return out
 
+    def reach(k):
+        dy = max(32 * k + 31, 255 - 32 * k)
+        return (255 * 255 + dy * dy) // 256 + 1
+
     def calls(r):
         o = order(r)
         a = sorted(o[:half], key=lambda d: far(r, d))
         b = sorted([d for d in o[half:] if d != r], key=lambda d: far(r, d))
-        return a[:2], a[2:], b[:2], b[2:]
+        return a[:2], a[2:], b[:1], b[1:2], b[2:]
 
     def others(r):
         return sorted([d for d in range(n) if d != r], key=lambda d: far(r, d))
@@ -115,28 +122,24 @@ def rank_program(g, core, T, topo):
     hs = [(korder[half * h], slice(64 * h, 64 * h + 64)) for h in range(2)]
     off, oe, on, ne = coarse_masks(rank)
 
-    fin(Y.dma_start(T.posi[0:8, 0:2], T.pos[:]), "s_pos", 16)
-    fin(S.dma_start(T.posi[8:16, 1:3], T.pos[:]), "s_pos", 16)
-    for s in range(8):
-        fin((Y, S)[s % 2].dma_start(T.pin[64 * (s // 4):64 * (s // 4) + 64, s % 4, :], T.tau[s:s + 1, :]), "s_tau", 16)
+    fin(Y.dma_start(T.posi[24:32, 0:2], T.pos[:]), "s_pos", 16)
+    fin(S.dma_start(T.posi[56:64, 1:3], T.pos[:]), "s_pos", 16)
+    for s in range(4):
+        fin((Y, S)[s % 2].dma_start(T.pin[:, s, :], T.tau[s % 2::2, 4096 * (s // 2):4096 * (s // 2) + 4096]), "s_t%d" % s, 16)
     fin(Y.dma_start(T.row[:], T.tau[:]), "s_row", 16)
     fin(Y.dma_start(T.trs[:], T.tr[:]), "s_tr", 16)
 
     def iota(ap, pat, base, cm, name):
         fin(g.iota(ap, pat, base, cm, allow_small_or_imprecise_dtypes=True), name)
 
-    def select(out, in_, pat, op, base, cm, name):
-        fin(g.affine_select(out, in_, pat, op, 0.0, base, cm), name)
+    def select(out, in_, pat, op, base, cm, name, fill=0.0):
+        fin(g.affine_select(out, in_, pat, op, fill, base, cm), name)
 
     def ms(ap, x, name):
         fin(V.memset(ap, x), name)
 
-    def eq(out, in0, col, name, k=None):
-        fin(V.tensor_scalar(out, in0, col, None, A.is_equal) if k is None else
-            V.tensor_scalar(out, in0, col, k, A.is_equal, A.mult), name)
-
-    def lin(out, in0, k, b, name):
-        fin(V.tensor_scalar(out, in0, k, b, A.mult, A.add), name)
+    def ts(out, in0, a, b, op0, op1, name):
+        fin(V.tensor_scalar(out, in0, a, b, op0, op1), name)
 
     def table(ap, x, k, b, name):
         fin(S.activation(ap, x, F.Copy, bias=b, scale=k), name)
@@ -144,177 +147,160 @@ def rank_program(g, core, T, topo):
     def square(ap, x, k, b, name):
         fin(S.activation(ap, x, F.Square, bias=b, scale=k), name)
 
-    fin(g.iota(T.ints[:, 0:1], [[1, 1]], 0, 1), "i_p")
-    iota(T.cc[:, 0:256], [[32, 16], [0, 16]], -496, 0, "i_b")
-    iota(T.aa[:], [[0, 8], [32, 16]], -496, 0, "i_a")
-    iota(T.r64[:], [[1, 64]], 0, 0, "i_r")
-    need("g", "i_a")
-    select(T.l3b[:], T.aa[0:8, :], [[1, 8], [0, 16]], A.is_equal, 0, -1, "i_l3")
-    ms(T.rall[:], 64.5, "m_r")
-    ms(T.lall[:], 2.0, "m_l")
-    ms(T.cc[0:16, 272:288], 0.0, "v_cc")
-    need("v", "i_p")
-    for i, b, nm in ((2, 7, "v_in0"), (4, 8, "v_in0"), (1, 15, "v_int"), (3, 112, "v_int"), (5, 63, "v_int")):
-        fin(V.tensor_scalar(T.ints[:, i:i + 1], T.ints[:, 0:1], b, None, A.bitwise_and), nm)
-    need("v", "m_r", "m_l")
-    ms(T.lall[0:32, :], -63.5 / 16, "m_all")
-    need("v", "v_in0")
-    lin(T.scol[:, 0:1], T.ints[:, 2:3], 32.0, -496.0, "v_sc")
-    lin(T.scol[:, 1:2], T.ints[:, 4:5], 0.125, 0.0, "v_cg1")
-    ms(T.rall[32:64, 256:272], 0.0, "m_all")
-    need("v", "v_int")
-    fin(V.tensor_copy(T.cols[:, 0:6], T.ints[:, 0:6]), "v_col")
-    lin(T.bcol[:], T.ints[:, 1:2], 8192.0, BIG, "v_bc")
-    need("v", "v_sc", "i_b")
-    eq(T.sel[:], T.cc[0:16, 0:128], T.scol[0:16, 0:1], "v_sel")
-    need("v", "v_cg1")
-    fin(V.tensor_scalar(T.cc[0:16, 256:272], T.cc[0:16, 0:256:16], T.scol[0:16, 1:2], None, A.mult), "v_sel")
-    need("s", "v_int")
-    square(T.lc0[:], T.ints[:, 1:2], -4.0, 62.0, "a_lc0")
-    need("s", "i_b", "m_r")
-    square(T.rall[64:96, 0:256], T.cc[64:96, 0:256], 0.0625, 0.0, "a_c")
-    square(T.rall[64:96, 256:272], T.cc[64:96, 0:256:16], 0.0625, 0.0, "a_c")
-    need("s", "a_lc0")
-    table(T.lcol[:], T.lc0[:], 1.0, 4095.75 / 16 - 15.0 / 32, "a_lc")
-    need("s", "i_a")
-    for c in (0, 128):
-        square(T.rall[32:64, c:c + 128], T.aa[32:64, :], 0.0625, 0.0, "a_c")
+    def mm(out, lhs, rhs, start, stop, name=None):
+        ins = E.matmul(out, lhs, rhs, start, stop)
+        if name:
+            fin(ins, name)
 
-    iota(T.kyi[:], [[32 * half * (h1 - h0), 2], [32, half], [1, 16]], 32 * half * h0, 0, "i_ky")
-    iota(T.cu[:], [[1, 144]], -16, 0, "i_u")
-    iota(T.kcol[:], [[h0 - h1, 2], [-2, half], [0, 16]], 7 - h0, 0, "i_k")
+    iota(T.vv[:], [[1, 1]], -143, 2, "i_p")
+    iota(T.gp[:], [[1, 8], [0, 16]], 24, -1, "i_gp")
+    iota(T.cu[:], [[2, 144]], -175, 0, "i_u")
+    ms(T.dd[0:32, :], 1.0, "m_d0")
+    ms(T.dd[32:64, :], 0.0, "m_d0")
+    ms(T.one[:], 0.5, "m_one")
+    ms(T.posi[0:24, 1:2], 0, "m_pos")
+    ms(T.posi[32:56, 1:2], 0, "m_pos")
+    need("v", "m_d0")
+    ms(T.dd[0:32, 16::16], -15.0, "m_d1")
+    ms(T.dd[32:64, ::16], 1.0, "m_d1")
+    ms(T.rall[64:65, 0:256], KB, "m_r")
+    need("v", "i_p")
+    ts(T.q2[:], T.vv[:], B32, B32, A.add, A.subtract, "v_q")
+    need("v", "m_d1")
+    fin(V.tensor_tensor_scan(T.cc[:], T.dd[:], T.dd[:], -2.0, A.add, A.add), "v_cc")
+    need("v", "i_gp")
+    ts(T.sel[0:32, :], T.gp[0:32, :], 0.0, 0.0625, A.is_equal, A.mult, "v_sel")
+    ts(T.sel[32:64, :], T.gp[32:64, :], -32.0, 0.0625, A.is_equal, A.mult, "v_sel")
+    need("s", "m_one")
+    table(T.lall[64:65, :], T.one[64:65, :], 0.0, KA, "m_k")
+    table(T.rall[64:65, 256:272], T.one[64:65, 0:16], 0.0, KC, "m_k")
+    table(T.c32[:], T.one[0:1, 0:32], 0.0, -1.0 / 64, "m_k")
+    table(T.lh4[64:128, :], T.one[64:128, :], 0.0, -4.0, "m_w")
+    need("s", "v_cc")
+    square(T.sqc[:, 256:272], T.cc[:, ::16], 0.5, 0.0, "a_c")
+    square(T.sqc[:, 0:128], T.cc[:, 0:128], 0.5, 0.0, "a_c")
+    square(T.sqc[:, 128:256], T.cc[:, 128:256], 0.5, 0.0, "a_c1")
+    need("g", "v_cc")
+    select(T.l3b[:], T.cc[0:32, 0:128], [[1, 8], [0, 16]], A.is_equal, 24, -1, "i_l3")
+    iota(T.kcol[:], [[2 * (h0 - h1), 2], [-4, half], [0, 16]], 2 * (7 - h0), 0, "i_k")
+    iota(T.kyi[:], [[-32 * half * (h1 - h0), 2], [-32, half], [-1, 16]], 248 - 32 * half * h0, 0, "i_ky")
     low = rank < on[0]
-    tab, nm, got = (T.idf, "i_idf", "i_g0") if low else (T.coef, "i_g0", "i_idf")
+    tab, nm, got = (T.em0, "i_e0", "i_kc") if low else (T.kc, "i_kc", "i_e0")
     if low:
-        iota(T.one[:], [[0, 128]], 1, 0, "i_one")
-        need("g", "i_one")
-        select(T.idf[:], T.one[:], [[-1, 128]], A.is_equal, 0, 1, nm)
+        need("g", "m_one")
+        select(T.em0[:], T.one[:], [[0, 8], [-16, 16]], A.is_ge, 0, 1, nm)
     else:
-        iota(T.coef[:], [[1024 * half * (h1 - h0), 2], [1024, half], [32, 16]], 256 + 1024 * half * h0, 0, nm)
+        iota(T.kc[:], [[-32 * half * (h1 - h0), 2], [-32, half], [-1, 16]], 1784 - 32 * half * h0, 0, nm)
     need("g", nm)
     g.remote_dma_fused([RemoteDMATransfer(dst_ids=[dst(on[0])], dma_engine_mask=bits(es), remote_sem=T.sem[nm],
                                           srcs=[tab[:, c:c + 64]], dsts=[tab[:, c:c + 64]])
                         for es, c in ((oe, 0), (ne, 64))], local_sem=T.sem["l_t"])
     cnt["l_t"] = cnt[got] = len(oe) + len(ne)
 
-    need("v", "s_pos")
-    fin(V.tensor_copy(T.posc[:], T.posi[:, 1:2]), "v_posc")
-    ms(T.feat[:], 1.0, "m_ft")
-    ms(T.fea2[:], 0.0, "m_tr0")
-    need("v", "v_sel", "i_a")
-    for c in (0, 128):
-        fin(V.tensor_copy(T.cc[0:8, c:c + 128], T.aa[0:8, :]), "v_cc")
-    fin(V.tensor_copy(T.posb[:], T.posi[0:8, 0:2]), "a_pos")
-    need("v", "v_posc", "v_cc", "m_all")
-    fin(V.tensor_scalar(T.rall[0:16, :], T.cc[0:16, :], T.posc[:], None, A.add), "v_rall")
-    need("s", "v_posc", "v_sel", "m_all")
-    fin(S.activation(T.lall[0:16, :], T.sel[:], F.Copy, scale=T.posc[:]), "a_lall")
-    need("v", "m_tr0")
-    ms(T.fea2[:, 32:64], 1.0 / 32, "m_tr1")
-    ms(T.lhw[:], 0.0, "m_lw0")
-    need("v", "v_col")
-    lin(T.ecol[:], T.cols[:, 3:4], 2.0, -496.0, "i_e0")
-    need("v", "i_r")
-    eq(T.id64[:], T.r64[:], T.cols[:, 5:6], "v_i64")
-    need("v", "i_e0")
-    eq(T.em[:], T.aa[:], T.ecol[:], "i_em")
-    need("t", "a_pos", "v_sel")
-    fin(E.matmul(T.pm[:, 0:2], T.sel[0:8, :], T.posb[:], True, True), "t_pos")
-    need("t", "v_rall", "a_lall", "a_c", "i_l3")
-    E.matmul(T.pt[:, 0:16], T.lall[:], T.rall[:, 256:272], True, False)
-    fin(E.matmul(T.pt[:, 0:16], T.l3b[:], T.rall[0:8, 272:288], False, True), "t_l")
-    fin(E.matmul(T.pf0[:, 0:256], T.lall[:], T.rall[:, 0:256], True, True), "t_m")
-    need("v", "t_l", "a_lc")
-    lin(T.sl[:], T.pt[:, 0:16], 0.0625, T.lcol[:], "v_sl")
-    need("v", "t_m", "v_bc")
-    fin(V.tensor_scalar(T.mask[:, 0:128], T.pf0[:, 0:128], BIG, T.bcol[:], A.add, A.is_equal), "v_m")
-    need("v", "v_sl")
-    fin(V.tensor_scalar(T.ci[:], T.sl[:], 511, None, A.bitwise_and), "v_ci")
-    fin(V.tensor_scalar(T.mask[:, 128:256], T.pf0[:, 128:256], BIG, T.bcol[:], A.add, A.is_equal), "v_m")
-    need("v", "v_ci")
-    fin(V.tensor_copy(T.cidx[:], T.ci[:]), "v_cidx")
+    need("v", "s_pos", "m_pos")
+    fin(V.tensor_scalar(T.posc[:], T.posi[:, 1:2], -248.0, None, A.add), "v_posc")
+    need("v", "v_q")
+    ts(T.r2[:], T.vv[:], T.q2[:], 15.0, A.subtract, A.add, "v_r")
     need("v", "i_u")
-    eq(T.st[:], T.cu[:, 1:144], T.cols[:, 3:4], "v_bs")
-    eq(T.qs[:], T.cu[:, 0:48], T.cols[:, 1:2], "v_qs")
+    fin(V.tensor_scalar(T.idh[:], T.cu[:, 16:144], T.vv[:], None, A.is_equal), "v_idh")
+    ts(T.st[:], T.cu[:, 1:144], 15.0, T.q2[:], A.add, A.is_equal, "v_bs")
+    need("v", "v_posc", "v_cc")
+    ts(T.rall[0:64, 0:256], T.cc[:], 16.0, T.posc[:], A.mult, A.add, "v_rall")
+    need("s", "v_posc", "v_sel")
+    fin(S.activation(T.lall[0:64, :], T.sel[:], F.Copy, scale=T.posc[:]), "a_lall")
+    need("v", "v_r")
+    ts(T.bcol[:, 0:1], T.r2[:], 256.0, B512 + 512, A.mult, A.add, "v_bc")
+    ts(T.bcol[:, 1:2], T.r2[:], 1.0, -86.5, A.mult, A.add, "v_bc")
+    ts(T.qs[:], T.cu[:, 0:48], 143.0, T.r2[:], A.add, A.is_equal, "v_qs")
+    need("v", "v_bc")
+    ts(T.qu[:], T.cu[:, 0:34], 0.5, T.bcol[:, 1:2], A.mult, A.is_equal, "v_qs")
+    need("t", "v_cc", "m_k", "m_one")
+    mm(T.pt[:, 0:16], T.lall[64:65, :], T.rall[64:65, 256:272], True, False)
+    mm(T.pm[0:32, 128:256], T.c32[:], T.cc[0:1, 0:128], True, False)
+    mm(T.pe[:, 0:1], T.cc[0:1, 0:128], T.c32[:, 0:1], True, False, "t_a")
+    need("t", "t_a", "a_c")
+    mm(T.pt[:, 0:16], T.sqc[0:32, 0:128], T.one[0:32, 0:16], False, False)
+    mm(T.pt[:, 0:16], T.one[0:64, :], T.sqc[:, 256:272], False, False)
+    parts = ((T.pf0, slice(0, MC)), (T.pf1, slice(MC, 256)))
+    for x, (b, c) in enumerate(parts):
+        need("t", ("a_c", "a_c1")[x])
+        mm(b[:, c], T.one[0:64, :], T.sqc[:, c], True, False)
+    need("t", "v_rall", "a_lall", "i_l3", "m_r")
+    mm(T.pt[:, 0:16], T.lall[0:64, :], T.rall[0:64, 0:256:16], False, False)
+    mm(T.pt[:, 0:16], T.l3b[:], T.rall[0:32, 0:256:16], False, True, "t_l")
+    for x, (b, c) in enumerate(parts):
+        mm(b[:, c], T.lall[0:65, :], T.rall[0:65, c], False, True, "t_m%d" % x)
+    mm(T.pm[0:32, 128:256], T.one[32:64, 0:32], T.lall[32:64, :], False, True)
+    mm(T.pm[32:64, 128:256], T.one[0:32, 0:32], T.lall[0:32, :], True, True)
+    mm(T.pe[:, 0:1], T.lall[32:64, :], T.one[32:64, 0:1], False, True, "t_lh4")
+    need("v", "t_l")
+    fin(V.tensor_scalar(T.wb[:], T.pt[:, 0:16], -255.5, None, A.add), "v_wb")
 
-    table(T.posf[:], T.posi[0:8, 0:2], -1.0, 0.0, "a_pf")
-    for p0, p1, k, b in ((0, 32, -0.5, -16.0), (32, 64, 0.0, 1.0), (64, 128, 0.0, 0.0)):
-        table(T.dfw[p0:p1, :], T.aa[p0:p1, 0:32], k, b, "a_d")
-    need("s", "s_tau")
-    need("t", "v_i64")
-    for x in range(2):
-        for c in range(4 * x, 4 * x + 4):
-            table(T.pf[:, c, :, :], T.pin[:, :, 16 * c:16 * c + 16], 1.0, 0.0, "a_p%d" % x)
-        need("t", "a_p%d" % x)
-        for c in range(4 * x, 4 * x + 4):
-            for p in (slice(0, 64), slice(64, 128)):
-                ins = E.matmul(T.pf1[p, c::8], T.pf[p, c, :, :], T.id64[p, :], True, True)
-    fin(ins, "t_n")
-    need("s", "t_pos", "a_pf", "m_ft")
-    table(T.neg[:], T.pm[:, 0:2], -1.0, 0.0, "a_neg")
-    fin(S.activation(T.feat[:, 32:64], T.feat[:, 0:32], F.Copy, bias=15.5, scale=T.posf[:, 0:1]), "a_feat")
-    fin(S.activation(T.feat[:, 96:128], T.feat[:, 0:32], F.Copy, scale=T.posf[:, 1:2]), "a_feat")
-    need("t", "a_feat", "m_tr1", "a_neg")
-    E.matmul(T.pm[:, 128:256], T.feat[:], T.sel[0:8, :], True, False)
-    fin(E.matmul(T.pm[:, 128:256], T.fea2[:], T.l3b[:], False, True), "t_lh4")
-    need("s", "a_d")
-    for c, p0, p1, x in ((15, 0, 32, -1800.0), (15, 32, 64, -15.0), (15, 64, 128, 1.0), (31, 0, 64, 0.0)):
-        table(T.dfw[p0:p1, c:c + 1], T.aa[p0:p1, 0:1], 0.0, x, "a_d1")
-    need("s", "a_neg", "v_col", "i_ky")
-    square(T.rx2[:], T.cols[:, 1:2], 1.0, T.neg[:, 0:1], "a_rx")
-    square(T.kysq[:], T.kyi[:], 1.0, T.neg[:, 1:2], "a_ky")
-    need("s", "t_n")
-    table(T.off[:, 0:64], T.pf1[:, 0:64], 1.0, 0.0, "a_off")
-    need("s", "t_lh4", "a_rx")
-    table(T.lh4[:], T.pm[:, 128:256], 1.0, 0.0, "a_lh4")
-    table(T.rxo[:], T.rx2[:], 0.0625, -15.0 / 32, "a_rxo")
+    for s in range(4):
+        need("s", "s_t%d" % s)
+        table(T.pf[:, :, s, :], T.pin[:, s, :], 1.0, 0.0, "a_p0")
+    need("s", "v_sel")
+    table(T.self[:], T.sel[0:32, :], 1.0, 0.0, "a_ky")
+    table(T.lhw[0:32, :], T.one[0:32, 0:1], 0.0, -0.5, "m_w")
+    table(T.lhw[32:64, :], T.one[32:64, 0:1], 0.0, -8.0, "m_w")
+    need("s", "i_ky", "t_lh4")
+    square(T.by[:], T.kyi[:], 1.0, T.posc[0:32, :], "a_ky")
+    square(T.rx[:], T.pe[:, 0:1], 8.0, 66.0, "a_rx")
+    table(T.lh4[0:64, :], T.pm[0:64, 128:256], 32.0, 248.0, "a_lh4")
 
-    def zs(a, b):
-        need("s", "a_off", "s_tr", *(["v_of0"] if b > 64 else []))
-        fin(S.activation(T.zed[:, 16 * a:16 * b], T.trs[:, 0:2048].indirect(T.off[:, a:b]), F.Copy), "a_z")
+    def zs(a, b, name="a_z"):
+        need("s", "v_off", "s_tr")
+        fin(S.activation(T.zed[:, 16 * a:16 * b], T.trs[:, 0:2048].indirect(T.off[:, a:b]), F.Copy), name)
 
-    at = [ZS[-1]]
+    top = (reach(1) + 1) // 2 * 2
+    at = [ZS[-1] - (ZC - top)]
 
     def zv(k):
         a, b = at[0], at[0] + k
         at[0] = b
-        need("v", "v_of0", "s_tr", *(["v_off"] if b > 352 else []))
+        need("v", "v_off", "s_tr")
         fin(V.tensor_copy(T.zed[:, 16 * a:16 * b], T.trs[:, 0:2048].indirect(T.off[:, a:b])), "v_z")
 
-    zs(ZS[0], ZS[1])
-
-    need("v", "v_cidx", "v_m", "s_row")
-    for x, (a, b) in enumerate(((0, 8), (8, 16))):
+    need("v", "t_m0", "v_bc")
+    ts(T.mask[:, 0:MC], T.pf0[:, 0:MC], B512, T.bcol[:, 0:1], A.add, A.is_equal, "v_m0")
+    need("v", "t_m1")
+    ts(T.mask[:, MC:256], T.pf1[:, MC:256], B512, T.bcol[:, 0:1], A.add, A.is_equal, "v_m1")
+    need("v", "v_wb")
+    fin(V.tensor_tensor(T.cidx[:], T.pt[:, 0:16], T.wb[:], A.subtract), "v_cidx")
+    for c in range(YG[0][2]):
+        need("v", "a_p0")
+        fin(V.transpose(T.off[:, c::8], T.pf[:, c, :, :]), "v_off")
+    need("v", "v_cidx", "s_row")
+    for x, (a, b, t0, t1) in enumerate(YG):
         c = slice(16 * a, 16 * b)
+        need("v", "v_m%d" % (16 * b > MC))
         fin(V.tensor_tensor(T.yg[:, c], T.row[:, 0:512].indirect(T.cidx[:, a:b]), T.mask[:, c], A.mult), "v_yg%d" % x)
         need("t", "v_yg%d" % x, "v_bs")
         for r in range(a, b):
             ins = E.matmul(T.po[:, 0:16], T.st[:, 15 - r:143 - r], T.yg[:, 16 * r:16 * r + 16], r == 0, r == 15)
+        for c in range(t0, t1):
+            need("v", "a_p0")
+            fin(V.transpose(T.off[:, c::8], T.pf[:, c, :, :]), "v_off")
     fin(ins, "t_off")
-    eq(T.idh[:], T.cu[:, 16:144], T.cols[:, 0:1], "v_idh")
     need("v", "i_k")
-    eq(T.gee[0:64, :], T.kcol[0:64, :], T.cols[0:64, 1:2], "v_g", 16.0)
-    eq(T.gee[96:128, :], T.kcol[96:128, :], T.cols[96:128, 1:2], "v_g", 16.0)
-    need("v", "a_off")
-    fin(V.tensor_copy(T.off[:, 64:352], T.pf1[:, 64:352]), "v_of0")
-    need("v", "m_lw0")
-    ms(T.lhw[32:64, :], 1.0 / 32, "m_lw1")
-    ms(T.lhw[96:128, :], 0.5, "m_lw1")
+    ts(T.gee[0:96, :], T.kcol[:], T.r2[0:96, :], -2.0, A.is_equal, A.mult, "v_g")
+    zs(ZS[0], ZS[1])
+    zv(ZV)
     need("v", "t_off")
     fin(V.tensor_copy(T.off2[:], T.po[:, 0:16]), "v_off2")
-    fin(V.tensor_copy(T.off[:, 352:512], T.pf1[:, 352:512]), "v_off")
+    zv(ONE)
     need("v", "v_off2", "s_tr")
-    fin(V.tensor_copy(T.cg[:, 0:128], T.trs[:, 0:2048].indirect(T.off2[:, 0:8])), "v_cg")
     need("s", "v_off2")
-    fin(S.activation(T.cg[:, 128:256], T.trs[:, 0:2048].indirect(T.off2[:, 8:16]), F.Copy), "a_cg")
+    fin(V.tensor_copy(T.cg[:, 0:128], T.trs[:, 0:2048].indirect(T.off2[:, 0:8])), "v_cg0")
+    fin(S.activation(T.cg[:, 128:256], T.trs[:, 0:2048].indirect(T.off2[:, 8:16]), F.Copy), "a_cg0")
     zs(ZS[1], ZS[2])
-    need("t", "v_qs", "v_cg", "a_cg")
+    need("t", "v_qs", "v_cg0", "a_cg0")
     for b in range(4):
         for h in range(2):
             c = 128 * h + 32 * b
             ins = E.matmul(T.pc[32 * b:32 * b + 32, 0:32], T.qs[:, 16 - 16 * h:48 - 16 * h], T.cg[:, c:c + 32], h == 0, h == 1)
     fin(ins, "t_c")
-    zv(TWO)
+    zv(ZW)
     need("v", "t_c")
     fin(V.tensor_copy(T.sendc[:], T.pc[:, 0:32]), "v_sendc")
 
@@ -328,135 +314,146 @@ def rank_program(g, core, T, topo):
     for r in others(rank):
         cnt["r_c%d" % r] = len(oe) if r in off else len(ne)
 
-    iota(T.kw[:], [[32, 8]], 0, 0, "i_kw")
-    need("g", "i_kw", "i_g0")
-    select(T.gee[64:96, :], T.coef[64:96, :], [[h0 - h1, 2], [-2, half], [0, 16]], A.is_equal, 7 - h0, -1, "i_g")
-    zv(ZC - ZS[-1] - 3 * ONE - 2 * TWO)
+    need("g", "m_one", "i_e0")
+    select(T.em[:], T.em0[:], [[0, 8], [16, 16]], A.is_ge, 15, -1, "i_em")
+    select(T.dfw[:], T.one[:, 0:32], [[1, 32]], A.is_equal, -15, 0, "i_d0")
+    iota(T.kw[:], [[32, 8]], -1, 0, "i_kw")
+    need("g", "i_d0", "i_kc", "i_em")
+    select(T.dfw[0:32, :], T.one[0:32, 0:32], [[1, 32]], A.not_equal, -15, 0, "i_d", -7.5)
+    iota(T.dfw[64:96, :], [[0, 2], [-2, 16]], 29, 0, "i_d")
+    select(T.gee[96:128, :], T.kc[96:128, :], [[h0 - h1, 2], [-2, half], [0, 16]], A.is_equal, 7 - h0, -1, "i_g")
+    zv(ZC - ZS[-1] - 4 * ONE - TWO - ZV - ZW)
 
     pa = [T.ps, T.pc]
-    need("t", "v_sendc", "v_idh")
-    E.matmul(T.pe[:, 0:32], T.idh[:], T.sendc[:], True, False)
+    need("t", "v_sendc", "a_ky", "a_rx", "v_idh")
+    for h, (k0, c) in enumerate(hs):
+        mm(pa[h][:, 0:64], T.self[:], T.by[:, c], True, False)
+    mm(T.pe[:, 0:32], T.idh[:], T.sendc[:], True, False)
     for i, r in enumerate(on + off):
         need("t", "r_c%d" % r)
         ins = E.matmul(T.pe[:, 0:32], T.idh[:], T.landc[:, 32 * r:32 * r + 32], False, i == n - 2)
     fin(ins, "t_sum")
     need("s", "t_sum")
     fin(S.activation(T.sq[:], T.pe[:, 0:32], F.Square), "a_sq")
-    zs(ZS[2], ZS[3])
+    zs(ZS[2], ZS[3] - (ZC - top))
+    zs(top, reach(0), "a_z1")
     need("t", "a_sq", "i_em")
-    fin(E.matmul(T.pe[:, 64:96], T.em[:], T.sq[:], True, True), "t_e")
-    need("t", "i_idf", "a_ky")
-    for h, (k0, c) in enumerate(hs):
-        E.matmul(pa[h][:, 0:64], T.idf[:], T.kysq[:, c], True, False)
+    mm(T.pe[:, 64:96], T.em[:], T.sq[:], True, True, "t_e")
     need("v", "t_e")
     fin(V.tensor_reduce(T.mx[:], T.pe[:, 64:96], AxisListType.X, A.max), "v_mx")
     zv(ONE)
     need("v", "v_mx")
     fin(V.tensor_scalar(T.uu[:], T.pe[:, 64:96], T.mx[:, 0:1], None, A.is_lt), "v_u")
     zv(ONE)
-    need("v", "v_u", "a_d1")
+    need("v", "v_u", "i_d")
     fin(V.tensor_tensor_scan(T.ff[:], T.uu[:], T.dfw[:], 0.0, A.mult, A.add), "v_f")
     zv(ONE)
     need("v", "v_f", "v_g", "i_g")
     fin(V.tensor_scalar(T.rhs[:], T.gee[:], T.ff[:, 31:32], None, A.mult), "v_rhs")
     zv(TWO)
-    need("t", "v_rhs", "a_lh4")
+    need("t", "v_rhs", "a_lh4", "m_w", "a_rx")
     for h, (k0, c) in enumerate(hs):
-        fin(E.matmul(pa[h][:, 0:64], T.lh4[:], T.rhs[:, c], False, True), "t_s%d" % h)
-    need("t", "m_lw1")
+        mm(pa[h][:, 0:64], T.lh4[:], T.rhs[:, c], False, True, "t_s%d" % h)
     for k0, c in hs:
-        fin(E.matmul(T.pm[0:1, 300 + k0:304 + k0], T.lhw[:], T.rhs[:, c.start:c.stop:16], True, True), "t_w")
+        mm(T.pm[0:1, 300 + k0:304 + k0], T.lhw[:], T.rhs[0:64, c.start:c.stop:16], True, True, "t_w")
 
     def places(h):
-        need("v", "t_s%d" % h, "a_rxo")
-        lin(T.lst[:, hs[h][1]], pa[h][:, 0:64], 0.0625, T.rxo[:], "v_l%d" % h)
+        need("v", "t_s%d" % h, "a_rx")
+        ts(T.lst[:, hs[h][1]], pa[h][:, 0:64], T.rx[:], -15.0 / 32, A.add, A.add, "v_l%d" % h)
 
     def pick(q, d, a=0, b=16, name=None):
         i = korder.index(d)
         o = T.fg[:, 256 * i + 16 * a:256 * i + 16 * b]
-        w = T.zed[:].indirect(T.lst[:, 16 * i + a:16 * i + b])
-        need(q, "v_l%d" % (i // half), "v_z", "a_z")
+        w = T.zed[:, 0:16 * reach(d)].indirect(T.lst[:, 16 * i + a:16 * i + b])
+        need(q, "v_l%d" % (i // half), "v_z", "a_z", *(["a_z1"] if reach(d) > top else []))
         fin(S.activation(o, w, F.Copy) if q == "s" else V.tensor_copy(o, w), name or "p%d" % i)
 
-    first = calls(rank)[0] + calls(rank)[1]
-    far1 = [d for d in korder[half:] if d in off]
+    away = sum(calls(rank)[:4], [])
     mate = on[0]
-    home = {d: ((T.pf0, T.po)[i // 2], 32 * (i % 2), i) for i, d in enumerate(first)}
-    home.update({far1[0]: (T.pf1, 0, half), far1[1]: (T.pf1, 32, half + 1), mate: (T.pe, 0, half + 2), rank: (T.ps, 0, n - 1)})
+    banks = ((T.pf0, 0), (T.pf0, 32), (T.po, 0), (T.po, 32), (T.pf1, 0), (T.pt, 0), (T.pe, 0), (T.ps, 0))
+    home = {d: banks[i] + (i,) for i, d in enumerate(away + [mate, rank])}
 
-    def add_up(d, name=None, more=()):
+    def add_up(d, name=None, more=(), cut=16):
         i = korder.index(d)
         b, c, _ = home[d]
         for u in range(2):
-            need("t", *(["p%d" % i] + list(more[:u])))
+            need("t", "p%d" % i, *(more if cut < 8 * u + 8 else ()))
             ins = E.matmul(b[:, c + u:c + u + 31:2], T.fg[:, 256 * i + 128 * u:256 * i + 128 * u + 128], T.qs[:, 16:32], True, True)
         if name:
             fin(ins, name)
 
     places(0)
     places(1)
-    pick("v", first[0])
-    pick("s", first[1])
-    pick("v", first[2])
-    pick("s", first[3])
-    add_up(first[0])
-    add_up(first[1], "t_f0")
-    pick("v", far1[0], 0, 4, "p8")
+    a, b, c, d, e, f = away
+    near, wide = sorted((a, b), key=reach)
+    pick("v", near)
+    pick("s", wide)
+    pick("v", c)
+    pick("s", d)
+    add_up(near)
+    add_up(wide, "t_f0")
+    pick("v", e, 0, F1)
     need("v", "t_f0")
     fin(V.tensor_copy(T.sendf[:, 0:64], T.pf0[:, 0:64]), "v_e0")
-    pick("v", far1[0], 4, 16)
-    pick("s", far1[1])
-    pick("v", mate, 0, 8)
-    add_up(first[2])
-    add_up(first[3], "t_f4")
+    pick("s", e, F1, 16, "p8")
+    pick("v", f, 0, F2)
+    pick("s", f, F2, 16, "p11")
+    add_up(c)
+    add_up(d, "t_f4")
     need("s", "t_f4")
     table(T.sendf[:, 64:128], T.po[:, 0:64], 1.0, 0.0, "v_e2")
-    pick("s", mate, 8, 16, "p9")
-    need("t", "v_u", "v_l0", "v_off", "p8")
-    add_up(far1[1])
-    add_up(far1[0], "t_f1")
-    add_up(mate, "t_f2", ("p9",))
-    pick("v", rank, 0, 4)
+    need("t", "v_u", "v_l0", "v_off")
+    add_up(e, "t_f1", ("p8",), F1)
+    add_up(f, "t_f5", ("p11",), F2)
+    pick("v", mate, 0, F3)
     need("v", "t_f1")
-    fin(V.tensor_copy(T.sendf[:, 128:192], T.pf1[:, 0:64]), "v_e1")
-    pick("s", rank, 4, 16, "p10")
-    need("s", "t_f2")
-    table(T.sendf[:, 192:224], T.pe[:, 0:32], 1.0, 0.0, "a_e1")
-    need("t", "p10")
-    add_up(rank, "t_f3")
+    fin(V.tensor_copy(T.sendf[:, 128:160], T.pf1[:, 0:32]), "v_e1")
+    pick("s", mate, F3, 16, "p9")
+    pick("v", rank, 0, F4)
+    need("v", "t_f5")
+    fin(V.tensor_copy(T.sendf[:, 160:192], T.pt[:, 0:32]), "v_e3")
+    pick("s", rank, F4, 16, "p10")
     need("v", "t_w", "i_kw")
     fin(V.tensor_tensor(T.wout[:], T.pm[0:1, 300:308], T.kw[:], A.add), "v_w")
-    need("v", "t_f3")
-    fin(V.tensor_copy(T.sendf[:, 224:256], T.ps[:, 0:32]), "a_e2")
 
-    for h, dests in enumerate(calls(rank)):
+    def samples(d):
+        return T.fg[:, 256 * korder.index(d):256 * korder.index(d) + 256]
+
+    for h in TURNS:
+        dests = calls(rank)[h]
         em = masks(rank, dests)
-        need("g", ("v_e0", "v_e2", "v_e1", "a_e1")[h])
+        need("g", *(["v_e0"], ["v_e2"], ["v_e1"], ["v_e3"], ["p9", "p%d" % korder.index(mate)])[h])
         tr = []
         for d in dests:
             k = home[d][2]
+            src, to = (samples(d), T.landm[:]) if d == mate else (T.sendf[:, 32 * k:32 * k + 32], T.landf[:, mine])
             tr.append(RemoteDMATransfer(dst_ids=[dst(d)], dma_engine_mask=bits(em[d]), remote_sem=T.sem["r_f%d" % rank],
-                                        srcs=[T.sendf[:, 32 * k:32 * k + 32]], dsts=[T.landf[:, mine]]))
+                                        srcs=[src], dsts=[to]))
             cnt["l_f"] = cnt.get("l_f", 0) + len(em[d])
         g.remote_dma_fused(tr, local_sem=T.sem["l_f"])
     coming = []
-    for h in (0, 1, 3, 2):
+    for h in TURNS:
         rs = [r for r in others(rank) if rank in calls(r)[h]]
-        coming += [r for r in rs if r in on] + [r for r in rs if r not in on]
+        coming += rs
         for r in rs:
             cnt["r_f%d" % r] = len(masks(r, calls(r)[h])[rank])
 
     need("y", "v_w")
     fin(Y.dma_start(T.w[:], T.wout[:]), "s_y", 16)
 
-    need("t", "v_l1")
-    for i, r in enumerate(coming[:half] + [rank] + coming[half:]):
-        need("t", "r_f%d" % r if r != rank else "a_e2")
-        part = T.landf[:, 32 * r:32 * r + 32] if r != rank else T.sendf[:, 224:256]
+    need("t", "v_l1", "v_e3")
+    for i, r in enumerate([rank] + coming):
+        need("t", *(["r_f%d" % r] if r != rank else ["p10", "p%d" % korder.index(rank)]))
         for x, b in enumerate((T.pc, T.pt)):
-            ins = E.matmul(b[0:32, 0:64], part, T.idh[:, 64 * x:64 * x + 64], i == 0, i == n - 1)
-            if i == n - 1:
-                fin(ins, ("t_y1", "t_y")[x])
+            if r in off:
+                terms = [(T.landf[:, 32 * r:32 * r + 32], T.idh[:, 64 * x:64 * x + 64])]
+            else:
+                c = 256 * korder.index(rank) if r == rank else 0
+                terms = [(T.qu[:, 1 - u:33 - u], (T.fg if r == rank else T.landm)[:, c + 128 * u + 64 * x:c + 128 * u + 64 * x + 64])
+                         for u in range(2)]
+            for j, (lhs, rhs) in enumerate(terms):
+                last = i == n - 1 and j == len(terms) - 1
+                mm(b[0:32, 0:64], lhs, rhs, i == 0 and j == 0, last, ("t_y1", "t_y")[x] if last else None)
     need("s", "t_y1")
     table(T.yout[:, 0:64], T.pc[0:32, 0:64], 1.0, 0.0, "a_y")
     need("v", "t_y")

from concourse.bass import DstId, RemoteDMATransfer
from concourse.mybir import AluOpType, AxisListType, ActivationFunctionType

B32 = 1.5 * 2.0 ** 28
B512 = 1.5 * 2.0 ** 32
KA, KB, KC = 21.703125, 11.796875, 3114.0
ZC = 510
ZS = (0, 28, 186, 266)
ONE, TWO = 8, 16
YG = ((0, 6, 6, 6), (6, 16, 6, 8))
MC = 96
F1, F2, F3, F4 = 4, 12, 6, 4
TURNS = (0, 1, 2, 4, 3)
CG = 4
ZV, ZW = 16, 24

F32, B16, H16, I32, U16 = "float32", "bfloat16", "float16", "int32", "uint16"
SCRATCH = {
    "posi": ("sbuf", [64, 4], I32), "posc": ("sbuf", [64, 1], F32), "dd": ("sbuf", [64, 256], H16),
    "cc": ("sbuf", [64, 256], H16), "sqc": ("sbuf", [64, 272], H16), "gp": ("sbuf", [64, 128], B16),
    "sel": ("sbuf", [64, 128], H16), "self": ("sbuf", [32, 128], F32), "lall": ("sbuf", [96, 128], H16), "rall": ("sbuf", [96, 272], H16),
    "kcol": ("sbuf", [96, 128], B16), "l3b": ("sbuf", [32, 128], H16), "kyi": ("sbuf", [32, 128], B16), "by": ("sbuf", [32, 128], F32),
    "c32": ("sbuf", [1, 32], H16), "lhw": ("sbuf", [64, 1], H16), "em0": ("sbuf", [128, 128], H16),
    "pin": ("sbuf", [128, 4, 128], I32), "pf": ("sbuf", [128, 8, 4, 16], U16),
    "kw": ("sbuf", [1, 8], F32), "wout": ("sbuf", [1, 8], F32), "yout": ("sbuf", [32, 128], F32),
}
for _nm, _w, _t in [
        ("row", 512, I32), ("off", 512, U16), ("zed", 16 * ZC, B16), ("trs", 2048, B16),
        ("vv", 1, F32), ("q2", 1, F32), ("r2", 1, F32), ("bcol", 2, F32), ("cu", 144, B16), ("st", 143, H16),
        ("qs", 48, B16), ("idh", 128, H16), ("one", 128, H16), ("em", 128, F32), ("kc", 128, F32),
        ("dfw", 32, F32), ("gee", 128, H16), ("rx", 1, F32), ("lh4", 128, H16), ("mask", 256, F32), ("qu", 34, B16), ("landm", 256, B16),
        ("wb", 16, B16), ("cidx", 16, U16), ("yg", 256, H16), ("off2", 16, U16), ("cg", 256, B16),
        ("sendc", 32, H16), ("landc", 256, H16), ("sq", 32, F32), ("mx", 1, F32), ("uu", 32, F32), ("ff", 32, F32),
        ("rhs", 128, H16), ("lst", 128, U16),
        ("fg", 2048, B16), ("sendf", 256, H16), ("landf", 256, H16)]:
    SCRATCH[_nm] = ("sbuf", [128, _w], _t)
for _nm in ["pt", "po", "pc", "pe", "ps", "pf0", "pf1", "pm"]:
    SCRATCH[_nm] = ("psum", [128, 512], F32)
SEMAPHORES = ["s_pos", "s_row", "s_tr", "s_y", "s_t0", "s_t1", "s_t2", "s_t3", "v_of0",
              "i_p", "i_gp", "i_u", "i_l3", "i_ky", "i_e0", "i_em", "i_kc", "i_d0", "i_d", "i_g", "i_kw",
              "m_one", "m_d0", "m_d1", "m_pos", "m_r", "m_k", "m_w",
              "v_cc", "v_q", "v_r", "v_bc", "v_sel", "v_posc", "v_rall", "v_bs", "v_qs", "v_idh", "v_g",
              "v_wb", "v_cidx", "v_m0", "v_m1", "v_off", "v_z", "v_yg0", "v_yg1", "v_yg2", "i_k", "v_off2", "v_cg0", "v_cg1", "a_cg0", "a_cg1", "v_sendc",
              "v_mx", "v_u", "v_f", "v_rhs", "v_l0", "v_l1", "v_e0", "v_e1", "v_e2", "v_w", "v_y",
              "a_c", "a_c1", "a_lall", "a_p0", "a_p1", "a_ky", "a_rx", "a_lh4", "a_off", "a_cg", "a_sq", "a_z", "a_z1", "a_e1", "a_e2", "a_y",
              "t_a", "t_l", "t_m0", "t_m1", "t_lh4", "t_n", "t_off", "t_c", "t_sum", "t_e", "t_s0", "t_s1", "t_w",
              "t_f0", "t_f1", "t_f2", "t_f3", "t_f4", "t_y", "t_y1", "l_c", "l_f", "l_t", "p8", "p9", "p10", "p11", "a_d0", "a_d1", "p12", "t_f5", "v_e3"] \
    + [_a + str(_i) for _a in ("p", "r_c", "r_f") for _i in range(8)]


def rank_program(g, core, T, topo):
    rank = T.rank_of(core)
    if rank is None:
        return
    A, F = AluOpType, ActivationFunctionType
    cores = list(T.cores)
    n = len(cores)
    half = n // 2
    V, S, E, Y = g.vector, g.scalar, g.tensor, g.sync
    Q = {"g": g, "v": V, "s": S, "t": E, "y": Y}
    cnt, seen = {}, {}

    def fin(ins, name, k=1):
        ins.then_inc(T.sem[name], k)
        cnt[name] = cnt.get(name, 0) + k

    def need(q, *names):
        for nm in names:
            if seen.get((q, nm), 0) < cnt[nm]:
                Q[q].wait_ge(T.sem[nm], cnt[nm])
                seen[(q, nm)] = cnt[nm]

    def order(r):
        h = r // half
        return [k for hh in (1 - h, h) for k in range(half * hh, half * hh + half)]

    def bits(es):
        return sum(1 << e for e in es)

    def far(r, d):
        a, b = topo.chip(cores[r]), topo.chip(cores[d])
        return (3 if a == b else 1 if topo.same_plane(a, b) else 2 if topo.mates(a, b) else 0, r ^ d)

    def masks(r, dests):
        src = cores[r]
        off = [d for d in dests if topo.chip(cores[d]) != topo.chip(src)]
        out = {d: coarse_masks(r)[3] for d in dests}
        for i, d in enumerate(off):
            es = topo.engines(src, cores[d])
            w = len(es) // len(off)
            out[d] = es[i * w:i * w + w]
        return out

    def reach(k):
        dy = max(32 * k + 31, 255 - 32 * k)
        return (255 * 255 + dy * dy) // 256 + 1

    def calls(r):
        o = order(r)
        a = sorted(o[:half], key=lambda d: far(r, d))
        b = sorted([d for d in o[half:] if d != r], key=lambda d: far(r, d))
        return a[:2], a[2:], b[:1], b[1:2], b[2:]

    def others(r):
        return sorted([d for d in range(n) if d != r], key=lambda d: far(r, d))

    def coarse_masks(r):
        src = cores[r]
        off = [d for d in others(r) if topo.chip(cores[d]) != topo.chip(src)]
        on = [d for d in others(r) if d not in off]
        oe = topo.engines(src, cores[off[0]])
        ne = [e for e in topo.engines(src, cores[on[0]]) if e not in oe]
        return off, oe, on, ne

    def dst(d):
        rid, pid, _ = topo.addr(cores[d])
        return DstId(rid=rid, pnc=pid)

    korder = order(rank)
    h0 = korder[0] // half
    h1 = korder[half] // half
    hs = [(korder[half * h], slice(64 * h, 64 * h + 64)) for h in range(2)]
    off, oe, on, ne = coarse_masks(rank)

    fin(Y.dma_start(T.posi[24:32, 0:2], T.pos[:]), "s_pos", 16)
    fin(S.dma_start(T.posi[56:64, 1:3], T.pos[:]), "s_pos", 16)
    for s in range(4):
        fin((Y, S)[s % 2].dma_start(T.pin[:, s, :], T.tau[s % 2::2, 4096 * (s // 2):4096 * (s // 2) + 4096]), "s_t%d" % s, 16)
    fin(Y.dma_start(T.row[:], T.tau[:]), "s_row", 16)
    fin(Y.dma_start(T.trs[:], T.tr[:]), "s_tr", 16)

    def iota(ap, pat, base, cm, name):
        fin(g.iota(ap, pat, base, cm, allow_small_or_imprecise_dtypes=True), name)

    def select(out, in_, pat, op, base, cm, name, fill=0.0):
        fin(g.affine_select(out, in_, pat, op, fill, base, cm), name)

    def ms(ap, x, name):
        fin(V.memset(ap, x), name)

    def ts(out, in0, a, b, op0, op1, name):
        fin(V.tensor_scalar(out, in0, a, b, op0, op1), name)

    def table(ap, x, k, b, name):
        fin(S.activation(ap, x, F.Copy, bias=b, scale=k), name)

    def square(ap, x, k, b, name):
        fin(S.activation(ap, x, F.Square, bias=b, scale=k), name)

    def mm(out, lhs, rhs, start, stop, name=None):
        ins = E.matmul(out, lhs, rhs, start, stop)
        if name:
            fin(ins, name)

    iota(T.vv[:], [[1, 1]], -143, 2, "i_p")
    iota(T.gp[:], [[1, 8], [0, 16]], 24, -1, "i_gp")
    iota(T.cu[:], [[2, 144]], -175, 0, "i_u")
    ms(T.dd[0:32, :], 1.0, "m_d0")
    ms(T.dd[32:64, :], 0.0, "m_d0")
    ms(T.one[:], 0.5, "m_one")
    ms(T.posi[0:24, 1:2], 0, "m_pos")
    ms(T.posi[32:56, 1:2], 0, "m_pos")
    need("v", "m_d0")
    ms(T.dd[0:32, 16::16], -15.0, "m_d1")
    ms(T.dd[32:64, ::16], 1.0, "m_d1")
    ms(T.rall[64:65, 0:256], KB, "m_r")
    need("v", "i_p")
    ts(T.q2[:], T.vv[:], B32, B32, A.add, A.subtract, "v_q")
    need("v", "m_d1")
    fin(V.tensor_tensor_scan(T.cc[:], T.dd[:], T.dd[:], -2.0, A.add, A.add), "v_cc")
    need("v", "i_gp")
    ts(T.sel[0:32, :], T.gp[0:32, :], 0.0, 0.0625, A.is_equal, A.mult, "v_sel")
    ts(T.sel[32:64, :], T.gp[32:64, :], -32.0, 0.0625, A.is_equal, A.mult, "v_sel")
    need("s", "m_one")
    table(T.lall[64:65, :], T.one[64:65, :], 0.0, KA, "m_k")
    table(T.rall[64:65, 256:272], T.one[64:65, 0:16], 0.0, KC, "m_k")
    table(T.c32[:], T.one[0:1, 0:32], 0.0, -1.0 / 64, "m_k")
    table(T.lh4[64:128, :], T.one[64:128, :], 0.0, -4.0, "m_w")
    need("s", "v_cc")
    square(T.sqc[:, 256:272], T.cc[:, ::16], 0.5, 0.0, "a_c")
    square(T.sqc[:, 0:128], T.cc[:, 0:128], 0.5, 0.0, "a_c")
    square(T.sqc[:, 128:256], T.cc[:, 128:256], 0.5, 0.0, "a_c1")
    need("g", "v_cc")
    select(T.l3b[:], T.cc[0:32, 0:128], [[1, 8], [0, 16]], A.is_equal, 24, -1, "i_l3")
    iota(T.kcol[:], [[2 * (h0 - h1), 2], [-4, half], [0, 16]], 2 * (7 - h0), 0, "i_k")
    iota(T.kyi[:], [[-32 * half * (h1 - h0), 2], [-32, half], [-1, 16]], 248 - 32 * half * h0, 0, "i_ky")
    low = rank < on[0]
    tab, nm, got = (T.em0, "i_e0", "i_kc") if low else (T.kc, "i_kc", "i_e0")
    if low:
        need("g", "m_one")
        select(T.em0[:], T.one[:], [[0, 8], [-16, 16]], A.is_ge, 0, 1, nm)
    else:
        iota(T.kc[:], [[-32 * half * (h1 - h0), 2], [-32, half], [-1, 16]], 1784 - 32 * half * h0, 0, nm)
    need("g", nm)
    g.remote_dma_fused([RemoteDMATransfer(dst_ids=[dst(on[0])], dma_engine_mask=bits(es), remote_sem=T.sem[nm],
                                          srcs=[tab[:, c:c + 64]], dsts=[tab[:, c:c + 64]])
                        for es, c in ((oe, 0), (ne, 64))], local_sem=T.sem["l_t"])
    cnt["l_t"] = cnt[got] = len(oe) + len(ne)

    need("v", "s_pos", "m_pos")
    fin(V.tensor_scalar(T.posc[:], T.posi[:, 1:2], -248.0, None, A.add), "v_posc")
    need("v", "v_q")
    ts(T.r2[:], T.vv[:], T.q2[:], 15.0, A.subtract, A.add, "v_r")
    need("v", "i_u")
    fin(V.tensor_scalar(T.idh[:], T.cu[:, 16:144], T.vv[:], None, A.is_equal), "v_idh")
    ts(T.st[:], T.cu[:, 1:144], 15.0, T.q2[:], A.add, A.is_equal, "v_bs")
    need("v", "v_posc", "v_cc")
    ts(T.rall[0:64, 0:256], T.cc[:], 16.0, T.posc[:], A.mult, A.add, "v_rall")
    need("s", "v_posc", "v_sel")
    fin(S.activation(T.lall[0:64, :], T.sel[:], F.Copy, scale=T.posc[:]), "a_lall")
    need("v", "v_r")
    ts(T.bcol[:, 0:1], T.r2[:], 256.0, B512 + 512, A.mult, A.add, "v_bc")
    ts(T.bcol[:, 1:2], T.r2[:], 1.0, -86.5, A.mult, A.add, "v_bc")
    ts(T.qs[:], T.cu[:, 0:48], 143.0, T.r2[:], A.add, A.is_equal, "v_qs")
    need("v", "v_bc")
    ts(T.qu[:], T.cu[:, 0:34], 0.5, T.bcol[:, 1:2], A.mult, A.is_equal, "v_qs")
    need("t", "v_cc", "m_k", "m_one")
    mm(T.pt[:, 0:16], T.lall[64:65, :], T.rall[64:65, 256:272], True, False)
    mm(T.pm[0:32, 128:256], T.c32[:], T.cc[0:1, 0:128], True, False)
    mm(T.pe[:, 0:1], T.cc[0:1, 0:128], T.c32[:, 0:1], True, False, "t_a")
    need("t", "t_a", "a_c")
    mm(T.pt[:, 0:16], T.sqc[0:32, 0:128], T.one[0:32, 0:16], False, False)
    mm(T.pt[:, 0:16], T.one[0:64, :], T.sqc[:, 256:272], False, False)
    parts = ((T.pf0, slice(0, MC)), (T.pf1, slice(MC, 256)))
    for x, (b, c) in enumerate(parts):
        need("t", ("a_c", "a_c1")[x])
        mm(b[:, c], T.one[0:64, :], T.sqc[:, c], True, False)
    need("t", "v_rall", "a_lall", "i_l3", "m_r")
    mm(T.pt[:, 0:16], T.lall[0:64, :], T.rall[0:64, 0:256:16], False, False)
    mm(T.pt[:, 0:16], T.l3b[:], T.rall[0:32, 0:256:16], False, True, "t_l")
    for x, (b, c) in enumerate(parts):
        mm(b[:, c], T.lall[0:65, :], T.rall[0:65, c], False, True, "t_m%d" % x)
    mm(T.pm[0:32, 128:256], T.one[32:64, 0:32], T.lall[32:64, :], False, True)
    mm(T.pm[32:64, 128:256], T.one[0:32, 0:32], T.lall[0:32, :], True, True)
    mm(T.pe[:, 0:1], T.lall[32:64, :], T.one[32:64, 0:1], False, True, "t_lh4")
    need("v", "t_l")
    fin(V.tensor_scalar(T.wb[:], T.pt[:, 0:16], -255.5, None, A.add), "v_wb")

    for s in range(4):
        need("s", "s_t%d" % s)
        table(T.pf[:, :, s, :], T.pin[:, s, :], 1.0, 0.0, "a_p0")
    need("s", "v_sel")
    table(T.self[:], T.sel[0:32, :], 1.0, 0.0, "a_ky")
    table(T.lhw[0:32, :], T.one[0:32, 0:1], 0.0, -0.5, "m_w")
    table(T.lhw[32:64, :], T.one[32:64, 0:1], 0.0, -8.0, "m_w")
    need("s", "i_ky", "t_lh4")
    square(T.by[:], T.kyi[:], 1.0, T.posc[0:32, :], "a_ky")
    square(T.rx[:], T.pe[:, 0:1], 8.0, 66.0, "a_rx")
    table(T.lh4[0:64, :], T.pm[0:64, 128:256], 32.0, 248.0, "a_lh4")

    def zs(a, b, name="a_z"):
        need("s", "v_off", "s_tr")
        fin(S.activation(T.zed[:, 16 * a:16 * b], T.trs[:, 0:2048].indirect(T.off[:, a:b]), F.Copy), name)

    top = (reach(1) + 1) // 2 * 2
    at = [ZS[-1] - (ZC - top)]

    def zv(k):
        a, b = at[0], at[0] + k
        at[0] = b
        need("v", "v_off", "s_tr")
        fin(V.tensor_copy(T.zed[:, 16 * a:16 * b], T.trs[:, 0:2048].indirect(T.off[:, a:b])), "v_z")

    need("v", "t_m0", "v_bc")
    ts(T.mask[:, 0:MC], T.pf0[:, 0:MC], B512, T.bcol[:, 0:1], A.add, A.is_equal, "v_m0")
    need("v", "t_m1")
    ts(T.mask[:, MC:256], T.pf1[:, MC:256], B512, T.bcol[:, 0:1], A.add, A.is_equal, "v_m1")
    need("v", "v_wb")
    fin(V.tensor_tensor(T.cidx[:], T.pt[:, 0:16], T.wb[:], A.subtract), "v_cidx")
    for c in range(YG[0][2]):
        need("v", "a_p0")
        fin(V.transpose(T.off[:, c::8], T.pf[:, c, :, :]), "v_off")
    need("v", "v_cidx", "s_row")
    for x, (a, b, t0, t1) in enumerate(YG):
        c = slice(16 * a, 16 * b)
        need("v", "v_m%d" % (16 * b > MC))
        fin(V.tensor_tensor(T.yg[:, c], T.row[:, 0:512].indirect(T.cidx[:, a:b]), T.mask[:, c], A.mult), "v_yg%d" % x)
        need("t", "v_yg%d" % x, "v_bs")
        for r in range(a, b):
            ins = E.matmul(T.po[:, 0:16], T.st[:, 15 - r:143 - r], T.yg[:, 16 * r:16 * r + 16], r == 0, r == 15)
        for c in range(t0, t1):
            need("v", "a_p0")
            fin(V.transpose(T.off[:, c::8], T.pf[:, c, :, :]), "v_off")
    fin(ins, "t_off")
    need("v", "i_k")
    ts(T.gee[0:96, :], T.kcol[:], T.r2[0:96, :], -2.0, A.is_equal, A.mult, "v_g")
    zs(ZS[0], ZS[1])
    zv(ZV)
    need("v", "t_off")
    fin(V.tensor_copy(T.off2[:], T.po[:, 0:16]), "v_off2")
    zv(ONE)
    need("v", "v_off2", "s_tr")
    need("s", "v_off2")
    fin(V.tensor_copy(T.cg[:, 0:128], T.trs[:, 0:2048].indirect(T.off2[:, 0:8])), "v_cg0")
    fin(S.activation(T.cg[:, 128:256], T.trs[:, 0:2048].indirect(T.off2[:, 8:16]), F.Copy), "a_cg0")
    zs(ZS[1], ZS[2])
    need("t", "v_qs", "v_cg0", "a_cg0")
    for b in range(4):
        for h in range(2):
            c = 128 * h + 32 * b
            ins = E.matmul(T.pc[32 * b:32 * b + 32, 0:32], T.qs[:, 16 - 16 * h:48 - 16 * h], T.cg[:, c:c + 32], h == 0, h == 1)
    fin(ins, "t_c")
    zv(ZW)
    need("v", "t_c")
    fin(V.tensor_copy(T.sendc[:], T.pc[:, 0:32]), "v_sendc")

    mine = slice(32 * rank, 32 * rank + 32)
    rc = T.sem["r_c%d" % rank]
    need("g", "v_sendc")
    g.remote_dma_fused([RemoteDMATransfer(dst_ids=[dst(d) for d in ds], dma_engine_mask=bits(es), remote_sem=rc,
                                          srcs=[T.sendc[:]], dsts=[T.landc[:, mine] for d in ds])
                        for ds, es in ((off, oe), (on, ne))], local_sem=T.sem["l_c"])
    cnt["l_c"] = len(oe) + len(ne)
    for r in others(rank):
        cnt["r_c%d" % r] = len(oe) if r in off else len(ne)

    need("g", "m_one", "i_e0")
    select(T.em[:], T.em0[:], [[0, 8], [16, 16]], A.is_ge, 15, -1, "i_em")
    select(T.dfw[:], T.one[:, 0:32], [[1, 32]], A.is_equal, -15, 0, "i_d0")
    iota(T.kw[:], [[32, 8]], -1, 0, "i_kw")
    need("g", "i_d0", "i_kc", "i_em")
    select(T.dfw[0:32, :], T.one[0:32, 0:32], [[1, 32]], A.not_equal, -15, 0, "i_d", -7.5)
    iota(T.dfw[64:96, :], [[0, 2], [-2, 16]], 29, 0, "i_d")
    select(T.gee[96:128, :], T.kc[96:128, :], [[h0 - h1, 2], [-2, half], [0, 16]], A.is_equal, 7 - h0, -1, "i_g")
    zv(ZC - ZS[-1] - 4 * ONE - TWO - ZV - ZW)

    pa = [T.ps, T.pc]
    need("t", "v_sendc", "a_ky", "a_rx", "v_idh")
    for h, (k0, c) in enumerate(hs):
        mm(pa[h][:, 0:64], T.self[:], T.by[:, c], True, False)
    mm(T.pe[:, 0:32], T.idh[:], T.sendc[:], True, False)
    for i, r in enumerate(on + off):
        need("t", "r_c%d" % r)
        ins = E.matmul(T.pe[:, 0:32], T.idh[:], T.landc[:, 32 * r:32 * r + 32], False, i == n - 2)
    fin(ins, "t_sum")
    need("s", "t_sum")
    fin(S.activation(T.sq[:], T.pe[:, 0:32], F.Square), "a_sq")
    zs(ZS[2], ZS[3] - (ZC - top))
    zs(top, reach(0), "a_z1")
    need("t", "a_sq", "i_em")
    mm(T.pe[:, 64:96], T.em[:], T.sq[:], True, True, "t_e")
    need("v", "t_e")
    fin(V.tensor_reduce(T.mx[:], T.pe[:, 64:96], AxisListType.X, A.max), "v_mx")
    zv(ONE)
    need("v", "v_mx")
    fin(V.tensor_scalar(T.uu[:], T.pe[:, 64:96], T.mx[:, 0:1], None, A.is_lt), "v_u")
    zv(ONE)
    need("v", "v_u", "i_d")
    fin(V.tensor_tensor_scan(T.ff[:], T.uu[:], T.dfw[:], 0.0, A.mult, A.add), "v_f")
    zv(ONE)
    need("v", "v_f", "v_g", "i_g")
    fin(V.tensor_scalar(T.rhs[:], T.gee[:], T.ff[:, 31:32], None, A.mult), "v_rhs")
    zv(TWO)
    need("t", "v_rhs", "a_lh4", "m_w", "a_rx")
    for h, (k0, c) in enumerate(hs):
        mm(pa[h][:, 0:64], T.lh4[:], T.rhs[:, c], False, True, "t_s%d" % h)
    for k0, c in hs:
        mm(T.pm[0:1, 300 + k0:304 + k0], T.lhw[:], T.rhs[0:64, c.start:c.stop:16], True, True, "t_w")

    def places(h):
        need("v", "t_s%d" % h, "a_rx")
        ts(T.lst[:, hs[h][1]], pa[h][:, 0:64], T.rx[:], -15.0 / 32, A.add, A.add, "v_l%d" % h)

    def pick(q, d, a=0, b=16, name=None):
        i = korder.index(d)
        o = T.fg[:, 256 * i + 16 * a:256 * i + 16 * b]
        w = T.zed[:, 0:16 * reach(d)].indirect(T.lst[:, 16 * i + a:16 * i + b])
        need(q, "v_l%d" % (i // half), "v_z", "a_z", *(["a_z1"] if reach(d) > top else []))
        fin(S.activation(o, w, F.Copy) if q == "s" else V.tensor_copy(o, w), name or "p%d" % i)

    away = sum(calls(rank)[:4], [])
    mate = on[0]
    banks = ((T.pf0, 0), (T.pf0, 32), (T.po, 0), (T.po, 32), (T.pf1, 0), (T.pt, 0), (T.pe, 0), (T.ps, 0))
    home = {d: banks[i] + (i,) for i, d in enumerate(away + [mate, rank])}

    def add_up(d, name=None, more=(), cut=16):
        i = korder.index(d)
        b, c, _ = home[d]
        for u in range(2):
            need("t", "p%d" % i, *(more if cut < 8 * u + 8 else ()))
            ins = E.matmul(b[:, c + u:c + u + 31:2], T.fg[:, 256 * i + 128 * u:256 * i + 128 * u + 128], T.qs[:, 16:32], True, True)
        if name:
            fin(ins, name)

    places(0)
    places(1)
    a, b, c, d, e, f = away
    near, wide = sorted((a, b), key=reach)
    pick("v", near)
    pick("s", wide)
    pick("v", c)
    pick("s", d)
    add_up(near)
    add_up(wide, "t_f0")
    pick("v", e, 0, F1)
    need("v", "t_f0")
    fin(V.tensor_copy(T.sendf[:, 0:64], T.pf0[:, 0:64]), "v_e0")
    pick("s", e, F1, 16, "p8")
    pick("v", f, 0, F2)
    pick("s", f, F2, 16, "p11")
    add_up(c)
    add_up(d, "t_f4")
    need("s", "t_f4")
    table(T.sendf[:, 64:128], T.po[:, 0:64], 1.0, 0.0, "v_e2")
    need("t", "v_u", "v_l0", "v_off")
    add_up(e, "t_f1", ("p8",), F1)
    add_up(f, "t_f5", ("p11",), F2)
    pick("v", mate, 0, F3)
    need("v", "t_f1")
    fin(V.tensor_copy(T.sendf[:, 128:160], T.pf1[:, 0:32]), "v_e1")
    pick("s", mate, F3, 16, "p9")
    pick("v", rank, 0, F4)
    need("v", "t_f5")
    fin(V.tensor_copy(T.sendf[:, 160:192], T.pt[:, 0:32]), "v_e3")
    pick("s", rank, F4, 16, "p10")
    need("v", "t_w", "i_kw")
    fin(V.tensor_tensor(T.wout[:], T.pm[0:1, 300:308], T.kw[:], A.add), "v_w")

    def samples(d):
        return T.fg[:, 256 * korder.index(d):256 * korder.index(d) + 256]

    for h in TURNS:
        dests = calls(rank)[h]
        em = masks(rank, dests)
        need("g", *(["v_e0"], ["v_e2"], ["v_e1"], ["v_e3"], ["p9", "p%d" % korder.index(mate)])[h])
        tr = []
        for d in dests:
            k = home[d][2]
            src, to = (samples(d), T.landm[:]) if d == mate else (T.sendf[:, 32 * k:32 * k + 32], T.landf[:, mine])
            tr.append(RemoteDMATransfer(dst_ids=[dst(d)], dma_engine_mask=bits(em[d]), remote_sem=T.sem["r_f%d" % rank],
                                        srcs=[src], dsts=[to]))
            cnt["l_f"] = cnt.get("l_f", 0) + len(em[d])
        g.remote_dma_fused(tr, local_sem=T.sem["l_f"])
    coming = []
    for h in TURNS:
        rs = [r for r in others(rank) if rank in calls(r)[h]]
        coming += rs
        for r in rs:
            cnt["r_f%d" % r] = len(masks(r, calls(r)[h])[rank])

    need("y", "v_w")
    fin(Y.dma_start(T.w[:], T.wout[:]), "s_y", 16)

    need("t", "v_l1", "v_e3")
    for i, r in enumerate([rank] + coming):
        need("t", *(["r_f%d" % r] if r != rank else ["p10", "p%d" % korder.index(rank)]))
        for x, b in enumerate((T.pc, T.pt)):
            if r in off:
                terms = [(T.landf[:, 32 * r:32 * r + 32], T.idh[:, 64 * x:64 * x + 64])]
            else:
                c = 256 * korder.index(rank) if r == rank else 0
                terms = [(T.qu[:, 1 - u:33 - u], (T.fg if r == rank else T.landm)[:, c + 128 * u + 64 * x:c + 128 * u + 64 * x + 64])
                         for u in range(2)]
            for j, (lhs, rhs) in enumerate(terms):
                last = i == n - 1 and j == len(terms) - 1
                mm(b[0:32, 0:64], lhs, rhs, i == 0 and j == 0, last, ("t_y1", "t_y")[x] if last else None)
    need("s", "t_y1")
    table(T.yout[:, 0:64], T.pc[0:32, 0:64], 1.0, 0.0, "a_y")
    need("v", "t_y")
    fin(V.tensor_copy(T.yout[:, 64:128], T.pt[0:32, 0:64]), "v_y")
    need("y", "v_y", "a_y")
    fin(Y.dma_start(T.y[:], T.yout[:]), "s_y", 16)
    need("y", "s_y")
    done = {}
    for (q, nm), k in seen.items():
        done[nm] = max(done.get(nm, 0), k)
    for nm in list(cnt):
        if done.get(nm, 0) < cnt[nm]:
            need("g", nm)
